import numpy as np, ml_dtypes
CORES = [83,85,87,115,117,119]
N = 6
BF = ml_dtypes.bfloat16
def f(rng, *shape):
    return (rng.standard_normal(shape, dtype=np.float32) * np.exp2(rng.integers(-2, 3, shape[:-1] + (1,)))).astype(BF)
def wide(rng, *shape):
    v = f(rng, *shape).astype(np.float32); k = shape[:-2] + (1, shape[-1])
    return (v * np.exp2(rng.integers(-6, 7, k)) * (rng.random(k) > 0.0625)).astype(BF)
def gentries(a):
    return np.ascontiguousarray(a.reshape(8, 16, -1).transpose(0, 2, 1)).reshape(8, -1)
def gtable(e):
    e = np.asarray(e); return np.ascontiguousarray(e.reshape(8, -1, 16).transpose(0, 2, 1)).reshape(128, -1).astype(np.int32)
L, M, S0, R = 3072, 6144, 28, 3
S = 32
def tame(v):
    u = np.minimum(np.maximum(v.astype(np.float32), np.float32(-960)), np.float32(960))
    return np.where(np.abs(u) < np.float32(2.0 ** -16), np.float32(0), u).astype(BF)
def speech(rng):
    q = 2.0 ** (-0.4 * rng.permutation(24)); ks = rng.integers(2, 7, 24); ks[np.argmax(q)] = 5
    W = [rng.permutation(S0)[:k] for k in ks]; w = np.zeros((N, 8, L), np.int64)
    for r in range(N):
        acc = np.add.accumulate(q * 2.0 ** rng.integers(-1, 2, 24))
        for g in range(8):
            i = np.minimum(np.searchsorted(acc, rng.random(L // 2) * acc[-1], side="right"), 23)
            v = np.concatenate([W[j] for j in i])[:L]; w[r, g] = np.where(rng.random(L) < 0.1, rng.integers(0, S0, L), v)
    return w
def lengths(rng):
    le = rng.integers(L // 2, L + 1, (N, 8)); le[rng.integers(0, N), rng.integers(0, 8)] = L
    return le
def plant(rng, w, le):
    r = rng.integers(0, len(w)); w[r, np.argmax(le[r]), :S0] = rng.permutation(S0)
def make(rng, w, le):
    st = np.zeros((N, 8, M), np.int32); ps = np.zeros((N, 8, L), np.int64)
    for r in range(N):
        for g in range(8):
            v = rng.permutation(np.concatenate((np.arange(S0), rng.integers(0, S0, M - S0)))); o = np.argsort(v, kind="stable")
            c = np.bincount(v, minlength=S0); first = np.add.accumulate(c) - c
            st[r, g] = v; ps[r, g] = o[first[w[r, g]] + rng.integers(0, c[w[r, g]])]
    return {"ve": tame(f(rng, N, 128, M)), "st": st, "pos": np.stack([gtable(p) for p in ps]), "le": le.reshape(N, 8, 1).astype(np.int32)}
def setup_inputs(rng):
    w, le = speech(rng), lengths(rng); plant(rng, w, le); return make(rng, w, le)
def setup_inputs_ends(rng):
    w, le = speech(rng), lengths(rng)
    for r in range(N): le[r, rng.permutation(8)[:4]] = np.array([0, 1, 2, L])
    ab = rng.permutation(S0)[:2]; v = w.reshape(N, 8, L // 2, 2); v[rng.random((N, 8, L // 2)) < 0.4] = ab; w = v.reshape(N, 8, L); w[:, :, :2] = ab
    for r in range(N):
        for g in range(8):
            if le[r, g] >= 2: w[r, g, le[r, g] - 2:le[r, g]] = ab
    plant(rng, w, le); d = make(rng, w, le)
    d["pos"][:, 8::16, 2] = 0; d["pos"][:, 9::16, 2] = M - 1; return d
def setup_inputs_ties(rng):
    w, le = speech(rng)[:N // 2], lengths(rng)[:N // 2]; plant(rng, w, le)
    return make(rng, np.concatenate((w, w ^ 1)), np.concatenate((le, le)))
def setup_inputs_few(rng):
    w = speech(rng); le = rng.integers(0, 2, (N, 8)); r, q = rng.permutation(N)[:2]; g = rng.integers(0, 8); le[q] = 0; le[q, (g + 3) % 8] = 1; le[r, g] = S0 + 2
    p = 1 + rng.permutation(S0 - 1); w[r, g, :S0 + 2] = np.concatenate((p[:1], [0], p[1:], [0], p[:1])); return make(rng, w, le)
def setup_inputs_loop(rng):
    W = [rng.permutation(S0)[:k] for k in range(2, 8)]; le = lengths(rng); w = np.zeros((N, 8, L), np.int64)
    for r in range(N):
        for g, i in enumerate(rng.permutation(np.array([0, 1, 2, 2, 3, 4, 5, 5]))): w[r, g] = W[i][(np.arange(L) + rng.integers(0, 8)) % len(W[i])]
    plant(rng, w, le); return make(rng, w, le)
def setup_inputs_spread(rng):
    w = np.stack([np.stack([np.repeat(rng.integers(0, S0, L), rng.integers(1, 40, L))[:L] for g in range(8)]) for r in range(N)])
    le = np.maximum(np.floor(L * rng.random((N, 8)) ** 4).astype(np.int64), 1); le[np.arange(N), rng.integers(0, 8, N)] = L
    plant(rng, w, le); d = make(rng, w, le); d["ve"] = tame(wide(rng, N, 128, M)); return d
def rounds(st, pos, le):
    s, pl = [], []
    for r in range(N):
        P = gentries(pos[r]).astype(np.int64)
        for g in range(8):
            p = P[g, :int(le[r, g, 0])]; pl.append(p); s.append(st[r, g][p].astype(np.int64))
    mg = np.zeros((R, 3), np.float32)
    for t in range(R):
        h = np.zeros(S * S, np.int64)
        for v in s: h += np.bincount((v[:-1] * S + v[1:])[v[:-1] != v[1:]], minlength=S * S)
        k = int(np.argmax(h)); a = k // S; b = k - S * a; mg[t] = a, b, h[k]
        for i in range(len(s)):
            v = s[i]; hit = np.zeros(v.size, bool); hit[:-1] = (v[:-1] == a) & (v[1:] == b)
            keep = np.ones(v.size, bool); keep[1:] = ~hit[:-1]
            s[i] = np.where(hit, S0 + t, v)[keep]; pl[i] = pl[i][keep]
    return s, pl, mg
def check_inputs(d):
    try:
        bad = []
        if not np.isfinite(d["ve"].astype(np.float32)).all(): bad.append("ve is finite")
        if d["st"].min() < 0 or d["st"].max() >= S0: bad.append("st is 0 to S0 - 1")
        if d["pos"].min() < 0 or d["pos"].max() >= M: bad.append("pos is 0 to M - 1")
        if d["le"].min() < 0 or d["le"].max() > L: bad.append("le is 0 to L")
        if not bad and rounds(d["st"], d["pos"], d["le"])[2][:, 2].min() < 1: bad.append("a pair is left in every round")
        return bad
    except Exception:
        return ["shapes"]
def reference(ve, st, pos, le):
    s, pl, mg = rounds(st, pos, le)
    y = np.zeros((N, 128, L), BF); fs = np.full((N, 8, L), -1, np.float32); fl = np.zeros((N, 8, 1), np.float32)
    for r in range(N):
        for g in range(8):
            v, p = s[8 * r + g], pl[8 * r + g]; fl[r, g, 0] = v.size; fs[r, g, :v.size] = v
            y[r, 16 * g:16 * g + 16, :v.size] = ve[r, 16 * g:16 * g + 16][:, p]
    return {"y": y, "fs": fs, "fl": fl, "mg": np.tile(mg, (N, 1, 1))}

@@ -1,0 +1,507 @@
+from concourse.bass import DstId, RemoteDMATransfer
+from concourse.mybir import AluOpType as A, AxisListType, ActivationFunctionType as F
+
+N, L, M, S0 = 6, 3072, 6144, 28
+HL, B = 4, 34
+BIG = 8388608.0
+GV = 74
+NPV = 22
+YV, YA = (18, 18, 34), 22
+KB = (3, 6, 7)
+XB = (0, 1, 2, 7)
+bf, f32, i32, u16 = "bfloat16", "float32", "int32", "uint16"
+
+_SBUF = [
+    (i32, [192], "posi rint"), (i32, [512], "sti"), (i32, [4], "lei pint pnt2 cnt"), (i32, [272], "wi wj"),
+    (u16, [192], "r16 p16 j16"), (u16, [32], "o16"),
+    (bf, [M], "vew"), (bf, [512], "stb xs"), (bf, [2048], "win"), (bf, [3088], "G W Y0"), (bf, [L], "Y"), (bf, [400], "fz"),
+    (bf, [192], "fa fb fv fab i32c rst d12 b3 hsv d3 sy"), (bf, [8, B], "S bn0 bn1 C1 C2 dd"), (bf, [8, 24], "inv g1 h1"),
+    (bf, [8, 25, 32], "OH"), (bf, [8, 25, 28 - NPV], "tab"), (bf, [272], "onb"), (bf, [4, 8, 16], "selh"), (bf, [8, 80], "mst"),
+    (bf, [4, 8], "pk"), (bf, [9, 128], "dg"), (bf, [128], "tris trii ngb"), (bf, [4, 32, 16], "X"), (bf, [8, 36], "zs"),
+    (bf, [3, 8, 6], "zt"), (bf, [21, 128], "zsel"),
+    (f32, [4], "lef kcol flb"), (f32, [272], "fT"), (f32, [128], "onf rep idf yrev sumt mrb mr mrt rvt ent eqb"),
+    (f32, [192], "jl jt"), (f32, [4, 32], "rmm"), (f32, [8, 16], "sixu"), (f32, [512], "urow ucon"),
+    (f32, [32], "xrow col c32 zer nega k0 k0t mlb ml mlt mlu cv enx ksb msg r1 r2 bc row ne"),
+    (f32, [16], "colk mL mR"), (f32, [2, 16], "tLR"), (f32, [N, 32], "land"), (f32, [24], "ld1 ld2"), (f32, [3, 32], "run"),
+    (f32, [64], "sc"), (f32, [12], "mgs"), (f32, [144], "zf"), (f32, [384], "fsb"),
+]
+SCRATCH = {n: ("sbuf", [128] + s, d) for d, s, names in _SBUF for n in names.split()}
+for _k in range(8):
+    SCRATCH["P%d" % _k] = ("psum", [128, 32, 16] if _k in (4, 5) else [128, 512], f32)
+
+SEMAPHORES = (["cV", "cS", "cP", "cG", "dpos", "dst", "dle", "dve", "dout", "sent", "ar1", "ar2"]
+              + ["a%d" % r for r in range(N)])
+
+
+def rank_program(g, core, T, topo):
+    rank = T.rank_of(core)
+    if rank is None:
+        return
+    eng = {"V": g.vector, "S": g.scalar, "P": g.tensor, "G": g, "Y": g.sync}
+    count = {"V": 0, "S": 0, "P": 0, "G": 0}
+    waited = {e: {} for e in eng}
+    lastw, readers = {}, {}
+
+    def wait(e, sem, val):
+        if waited[e].get(sem, 0) < val:
+            eng[e].wait_ge(T.sem[sem], val)
+            waited[e][sem] = val
+
+    def order(e, r, w):
+        for k in r:
+            if k in lastw and not (e == "P" and lastw[k][2] == "P"):
+                wait(e, lastw[k][0], lastw[k][1])
+            if k[0] == "P":
+                for x in readers.get(k, []):
+                    if x[2] != e:
+                        wait(e, x[0], x[1])
+        for k in w:
+            for x in readers.get(k, []) + ([lastw[k]] if k in lastw else []):
+                if not (e == "P" and x[2] == "P"):
+                    wait(e, x[0], x[1])
+
+    def note(tok, r, w):
+        for k in r:
+            readers.setdefault(k, []).append(tok)
+        for k in w:
+            lastw[k] = tok
+            readers[k] = []
+
+    def op(e, fn, r, w):
+        r, w = r.split(), w.split()
+        order(e, r, w)
+        count[e] += 1
+        fn().then_inc(T.sem["c" + e], 1)
+        note(("c" + e, count[e], e), r, w)
+
+    def ts(out, in0, s1, s2, o0, o1, r, w):
+        if o1 is None:
+            op("V", lambda: g.vector.tensor_scalar(out, in0, s1, None, o0), r, w)
+        else:
+            op("V", lambda: g.vector.tensor_scalar(out, in0, s1, s2, o0, o1), r, w)
+
+    def tt(out, a, b, o, r, w):
+        op("V", lambda: g.vector.tensor_tensor(out, a, b, o), r, w)
+
+    def cp(out, a, r, w):
+        op("V", lambda: g.vector.tensor_copy(out, a), r, w)
+
+    def ms(out, c, w):
+        op("V", lambda: g.vector.memset(out, c), "", w)
+
+    def red(out, a, o, r, w):
+        op("V", lambda: g.vector.tensor_reduce(out, a, AxisListType.X, o), r, w)
+
+    def scan(out, d0, d1, o0, o1, r, w):
+        op("V", lambda: g.vector.tensor_tensor_scan(out, d0, d1, 0.0, o0, o1), r, w)
+
+    def act(out, a, fn, r, w, bias=None, scale=1.0):
+        if bias is None:
+            op("S", lambda: g.scalar.activation(out, a, fn), r, w)
+        else:
+            op("S", lambda: g.scalar.activation(out, a, fn, bias=bias, scale=scale), r, w)
+
+    def mm(out, lhsT, rhs, start, stop, r, w):
+        op("P", lambda: g.tensor.matmul(out, lhsT, rhs, start, stop), r, w)
+
+    def mms(out, terms, r, w, start=True, stop=True):
+        for n, (lhsT, rhs) in enumerate(terms):
+            mm(out, lhsT, rhs, start and n == 0, stop and n == len(terms) - 1, r, w)
+
+    def iota(out, pat, base, cm, w, fl=True):
+        if fl:
+            op("G", lambda: g.iota(out, pat, base, cm, allow_small_or_imprecise_dtypes=True), "", w)
+        else:
+            op("G", lambda: g.iota(out, pat, base, cm), "", w)
+
+    def sel(out, a, pat, cmp, base, cm, r, w):
+        op("G", lambda: g.affine_select(out, a, pat, cmp, 0.0, base, cm), r, w)
+
+    ndma = {}
+
+    def dma(e, out, a, sem, r, w):
+        r, w = r.split(), w.split()
+        order(e, r, w)
+        ndma[sem] = ndma.get(sem, 0) + 16
+        eng[e].dma_start(out, a).then_inc(T.sem[sem], 16)
+        note((sem, ndma[sem], "D"), r, w)
+
+    others = [r for r in range(N) if r != rank]
+    near = [r for r in others if topo.chip(T.cores[r]) == topo.chip(core)]
+    far = [r for r in others if r not in near]
+    far_eng = topo.engines(core, T.cores[far[0]])
+    near_eng = [e for e in topo.engines(core, T.cores[near[0]]) if e not in far_eng]
+    nsent = [0]
+
+    def send(src, dst, sem, r):
+        order("G", r.split(), [])
+        trs = []
+        for peers, engs in ((far, far_eng), (near, near_eng)):
+            ids = [DstId(rid=topo.addr(T.cores[p])[0], pnc=topo.addr(T.cores[p])[1]) for p in peers]
+            trs.append(RemoteDMATransfer(dst_ids=ids, dma_engine_mask=sum(1 << e for e in engs), remote_sem=T.sem[sem],
+                                         srcs=[src], dsts=[dst] * len(peers)))
+            nsent[0] += len(engs)
+        g.remote_dma_fused(trs, local_sem=T.sem.sent)
+
+    arrive = len(far) * len(far_eng) + len(near) * len(near_eng)
+    P = [T["P%d" % k] for k in range(8)]
+    EQ, ADD, SUB, MUL, MAX = A.is_equal, A.add, A.subtract, A.mult, A.max
+    idb, idn, idm, i29, i30, i8, iL, iR, cst = (T.dg[:, k, :] for k in range(9))
+    own = slice(HL, HL + 24)
+
+    dma("S", T.sti[0:96, :], T.st[:], "dst", "", "sti")
+    dma("Y", T.posi[:], T.pos[:], "dpos", "", "posi")
+    dma("Y", T.lei[0:8, 0:1], T.le[:], "dle", "", "lei")
+    dma("Y", T.vew[:], T.ve[:], "dve", "posi sti", "vew")
+
+    ms(T.onb[:], 1.0, "onb")
+    ms(T.selh[:], 0.0, "selh")
+    ms(T.onf[:], 1.0, "onf")
+    ms(T.mst[:], 0.0, "mst")
+    ms(T.fz[:], 0.0, "fz")
+    ms(T.G[:, 0:16], 0.0, "Gl")
+    ms(T.G[:, 3072:3088], 0.0, "G")
+    ms(T.OH[:, :, :, 28:32], 0.0, "OH28 OH29 OH30")
+    ms(T.msg[:], 0.0, "msg")
+    ms(T.ngb[:], -1.0, "ngb")
+    ms(T.sixu[:], 0.0, "sixu")
+    sel(T.selh[:, :, :, 0:3], T.onb[:, 0:96], [[-1, 4], [-12, 8], [-4, 3]], EQ, 0, 1, "onb", "selh")
+    iota(T.kcol[:, 0:1], [[0, 1]], 0, 16, "kcol")
+    sel(T.mst[:, :, 32:48], T.onb[:, 0:128], [[-16, 8], [-1, 16]], EQ, 0, 1, "onb", "mst")
+    sel(T.rep[:], T.onf[:], [[-1, 8], [0, 16]], EQ, 0, 1, "onf", "rep")
+    iota(T.jl[:], [[16, 192]], 0, 1, "jl")
+    iota(T.pint[:, 0:1], [[0, 1]], 0, 1, "pint", False)
+    iota(T.yrev[:], [[0, 4], [-1, 32]], 31, 0, "yrev")
+    iota(T.xrow[:], [[1, 32]], 0, 0, "xrow")
+    sel(T.idf[:], T.onf[:], [[-1, 128]], EQ, 0, 1, "onf", "idf")
+    sel(idb, T.onb[:, 0:128], [[-1, 128]], EQ, 0, 1, "onb", "idb")
+    sel(T.tris[:], T.ngb[:], [[1, 128]], A.is_gt, 0, -1, "ngb", "tris")
+    sel(T.trii[:], T.ngb[:], [[1, 128]], A.is_ge, 0, -1, "ngb", "trii")
+    sel(T.rmm[:], T.onf[:], [[-1, 4], [-4, 32]], EQ, 0, 1, "onf", "rmm")
+    iota(T.sixu[:, :, 12:16], [[0, 8], [6, 4]], 0, 24, "sixu")
+    iota(T.i32c[:], [[0, 32], [32, 6]], 0, 0, "i32c")
+    iota(T.urow[:, 0:256], [[1, 256]], -256, 0, "urow0")
+    iota(T.urow[:, 256:512], [[1, 256]], 1, 0, "urow1")
+    ts(T.pk[:, 1, :], T.mst[:, :, 33], 64.0, None, MUL, None, "mst", "pk1")
+    ts(T.pk[:, 2, :], T.mst[:, :, 34], 4096.0, None, MUL, None, "mst", "pk2")
+    tt(T.pk[:, 3, :], T.pk[:, 1, :], T.mst[:, :, 32], ADD, "pk1 mst", "pk3")
+    tt(T.pk[:, 0, :], T.pk[:, 3, :], T.pk[:, 2, :], ADD, "pk3 pk2", "pk")
+
+    ts(T.rint[:], T.posi[:], 2047, None, A.bitwise_and, None, "posi", "rint")
+    cp(T.r16[:], T.rint[:], "rint", "r16")
+    for k in range(2):
+        cs = slice(256 * k, 256 * k + 256)
+        ts(T.stb[0:96, cs], T.sti[0:96, cs], 1.0, None, ADD, None, "sti", "stb%d" % k)
+        for h in range(4):
+            mm(P[2 * k + h // 2][:, 256 * (h % 2):256 * (h % 2) + 256], T.selh[0:96, h, :, :], T.stb[0:96, cs], True, True,
+               "selh stb%d" % k, "P%d" % (2 * k + h // 2))
+    tt(T.lef[0:8, 0:1], T.lei[0:8, 0:1], T.kcol[0:8, 0:1], ADD, "lei kcol", "lef")
+    mm(P[7][:, 0:1], T.rep[0:8, :], T.lef[0:8, 0:1], True, True, "rep lef", "P7")
+    ts(T.fa[:], T.posi[:], 2048.0, 1.0 / 64, A.is_lt, MAX, "posi", "fa")
+    ts(T.fb[:], T.posi[:], 4096.0, 1.0 / 64, A.is_lt, MAX, "posi", "fb")
+    for k in range(2):
+        for h in range(4):
+            bank, c0 = 2 * k + h // 2, 512 * h + 256 * k
+            src = P[bank][:, 256 * (h % 2):256 * (h % 2) + 256]
+            if h >= 2:
+                cp(T.win[:, c0:c0 + 256], src, "P%d" % bank, "win%d%d" % (k, h))
+            else:
+                act(T.win[:, c0:c0 + 256], src, F.Copy, "P%d" % bank, "win%d%d" % (k, h))
+    WIN = "win01 win03 win11 win13 r16"
+    act(T.G[:, HL + 16 * GV:HL + L], T.win[:].indirect(T.r16[:, GV:192]), F.Copy, WIN + " G", "GS")
+    ts(T.fv[:], T.jl[:], P[7][:, 0:1], None, A.is_lt, None, "jl P7", "fv")
+    tt(T.fab[:], T.fa[:], T.fb[:], MUL, "fa fb", "fab")
+    for x in range(3):
+        tt(T.fz[:, 6 + x:6 + x + 384:6], T.fab[:, x::3], T.fv[:, x::3], MUL, "fab fv fz", "fz%d" % x)
+    cp(T.G[:, HL:HL + 16 * GV], T.win[:].indirect(T.r16[:, 0:GV]), WIN + " Gl", "GV")
+
+    def f_terms(pairs, b0, n):
+        return [(T.fz[:, 6 + 6 * (x // 3) + x % 3 - 3 * rho:388 + 6 * (x // 3) + x % 3 - 3 * rho:3],
+                 T.mst[:, :, 32 - HL + 24 * rho - 16 * x + b0:32 - HL + 24 * rho - 16 * x + b0 + n]) for rho, x in pairs]
+
+    FZ = "fz0 fz1 fz2 mst"
+    mms(P[7][:, 0:200], f_terms(((0, 0), (0, 1), (1, 1), (1, 2), (1, 3)), 4, 25), FZ, "P7")
+    mms(P[7][:, 200:232], f_terms(((0, -1), (1, 1)), 0, 4), FZ, "P7")
+    mms(P[7][:, 232:272], f_terms(((0, 1), (1, 3)), 29, 5), FZ, "P7")
+    act(T.fT[:], P[7][:, 0:272], F.Copy, "P7", "fT")
+    for b in list(range(4, 29)) + list(range(4)) + list(range(29, B)):
+        out = P[6][:, b - 4:200:25] if 4 <= b < 29 else P[3][:, b:32:4] if b < 4 else P[3][:, b + 3:72:5]
+        mm(out, T.G[:, b:b + 3049:24], T.pk[:, 0, :], True, True, "GV GS pk", "P6" if 4 <= b < 29 else "P3")
+    zc, kc, z28, le28, isE, isV, yc, e1, e2, e3 = (T.col[:, k:k + 1] for k in range(10))
+    ts(T.pnt2[:, 0:1], T.pint[:, 0:1], 31, None, A.bitwise_and, None, "pint", "pa")
+    ts(T.pnt2[:, 1:2], T.pint[:, 0:1], 5, None, A.arith_shift_right, None, "pint", "pb")
+    ts(T.pnt2[:, 2:3], T.pint[:, 0:1], 15, None, A.bitwise_and, None, "pint", "pc")
+    cp(T.p16[:], T.posi[:], "posi", "p16")
+    cp(T.col[:, 0:2], T.pnt2[:, 0:2], "pa pb", "zc")
+    ms(T.Y0[:, 1536:1542], 0.0, "Y0h")
+    ms(T.Y0[:, 3078:3088], 0.0, "Y0e")
+    ts(T.sumt[:], T.yrev[:], zc, 32.0, EQ, MUL, "yrev zc", "sumt")
+    ts(yc, zc, -1.0, 31.0, MUL, ADD, "zc", "yc")
+    ts(idn, idb, -1.0, None, MUL, None, "idb", "idn")
+    ts(T.k0t[:], T.xrow[:], yc, -BIG, EQ, MUL, "xrow yc", "k0t")
+    ts(idm, idb, -1.0 / 32, None, MUL, None, "idb", "idm")
+    tt(T.k0[:], T.k0t[:], T.yrev[:, 0:32], ADD, "k0t yrev", "k0")
+    tt(T.wi[:, 0:200], P[6][:, 0:200], T.fT[:, 0:200], MUL, "P6 fT", "wi")
+    ts(T.wj[:, 0:200], T.wi[:, 0:200], 63, None, A.bitwise_and, None, "wi", "wj")
+    cp(T.S[:, :, 4:29], T.wj[:, 0:200], "wj", "S")
+
+    for h in range(2):
+        gs = slice(4 * h, 4 * h + 4)
+        for x in range(NPV, 28):
+            act(T.tab[:, gs, :, x - NPV], T.S[:, gs, HL:HL + 25], F.Abs, "S", "tab%d_%d" % (h, x), bias=-float(x + 1))
+        act(T.OH[:, gs, :, NPV:28], T.tab[:, gs, :, :], F.Relu, " ".join("tab%d_%d" % (h, x) for x in range(NPV, 28)),
+            "OHs%d" % h, bias=1.0, scale=-1.0)
+        for x in range(NPV):
+            ts(T.OH[:, gs, :, x], T.S[:, gs, HL:HL + 25], float(x + 1), None, EQ, None, "S", "OHv%d_%d" % (h, x))
+        for q in range(24):
+            gg, b0 = 4 * h + q // 6, 4 * (q % 6)
+            mm(P[2][:, 0:112], T.OH[:, gg, b0 + 1:b0 + 5, :], T.OH[:, gg, b0:b0 + 4, 0:28], h == 0 and q == 0,
+               h == 1 and q == 23, "OHs%d OHv%d_%d OH28" % (h, h, NPV - 1), "P2")
+    act(T.Y0[:, 0:1536], T.vew[:].indirect(T.p16[:, 0:96]), F.Copy, "vew p16", "Y0a")
+    act(T.Y0[:, 1542:3078], T.vew[:].indirect(T.p16[:, 96:192]), F.Copy, "vew p16", "Y0b")
+    act(T.W[:], T.G[:], F.Identity, "GV GS", "W", bias=0.0, scale=0.0)
+    act(T.X[:], T.G[:, 0:2048], F.Identity, "GV GS", "X", bias=0.0, scale=0.0)
+
+    def code_of(out, prev, cur, n, r, w):
+        mms(out, [(cst, T.onb[:, 0:n]), (idn, prev)] + [(idm, c) for c in cur], r + " cst idn idm onb", w)
+
+    tt(T.wi[:, 200:272], P[3][:, 0:72], T.fT[:, 200:272], MUL, "P3 fT", "wih")
+    ms(T.dg[0:32, 8, :], 1.0, "cs0")
+    ts(T.wj[:, 200:272], T.wi[:, 200:272], 63, None, A.bitwise_and, None, "wih", "wjh")
+    ms(T.dg[32:64, 8, :], 1.0 / 1024, "cs1")
+    ms(T.dg[64:128, 8, :], 0.0, "cst")
+    cp(T.S[:, :, 0:4], T.wj[:, 200:232], "wjh", "Sl")
+    cp(T.S[:, :, 29:B], T.wj[:, 232:272], "wjh", "Sr")
+    ms(T.c32[:], 1.0 / 32, "c32")
+    ms(T.zer[:], 0.0, "zer")
+    ts(T.colk[:], T.xrow[:, 0:16], kc, None, SUB, None, "xrow zc", "colk")
+    ts(z28, zc, 28.0, None, EQ, None, "zc", "z28")
+    ts(le28, zc, 28.5, None, A.is_lt, None, "zc", "le28")
+    ts(T.mL[:], T.colk[:], 4.0, None, EQ, None, "colk", "mL")
+    ts(T.mR[:], T.colk[:], 1.0, None, EQ, None, "colk", "mR")
+    ts(T.mlb[:], T.xrow[:], zc, le28, EQ, MUL, "xrow zc le28", "mlb")
+    ts(T.mrb[:], T.sumt[:], le28, None, MUL, None, "sumt le28", "mrb")
+    for k in range(4):
+        cp(T.msg[32 * k:32 * k + 32, 0:28], P[2][32 * k:32 * k + 32, 28 * k:28 * k + 28], "P2 msg", "msg%d" % k)
+    MSG = "msg0 msg1 msg2 msg3"
+    send(T.msg[:], T.land[:, rank, :], "a%d" % rank, MSG)
+    code_of(P[1][:, 0:264], T.S[:, :, 0:33], [T.S[:, :, 1:34]], 264, "S Sl Sr cs0 cs1", "P1")
+    K = [P[k][:, 0:32] for k in KB]
+    mms(K[0], [(T.idf[:], T.k0[:]), (T.sumt[:], T.msg[:])], "idf k0 sumt " + MSG, "P3", stop=False)
+    for n, r in enumerate(near + far):
+        wait("P", "a%d" % r, len(near_eng) if r in near else len(far_eng))
+        mm(K[0], T.sumt[:], T.land[:, r, :], False, n == N - 2, "sumt", "P3")
+
+    ts(i29, idb, 29.0, None, MUL, None, "idb", "i29")
+    ts(i30, idb, 30.0, None, MUL, None, "idb", "i30")
+    ts(i8, idb, 8.0, None, MUL, None, "idb", "i8")
+    ts(T.inv[:], T.S[:, :, own], 0.0, 8.0, EQ, MUL, "S", "inv")
+    ms(T.rst[:], 1.0, "rst")
+    ms(T.zf[:], 0.0, "zf")
+    ms(T.zs[:], 0.0, "zs")
+    ms(T.rst[:, 0::6], 0.0, "rst")
+    ts(T.zt[:, 0, :, :], T.mst[:, :, 38:44], 192.0, None, MUL, None, "mst", "zt0")
+    ts(T.zt[:, 1, :, 0:2], T.mst[:, :, 46:48], 192.0, None, MUL, None, "mst", "zt1")
+    tt(T.zs[:, :, 15:21], T.zt[:, 0, :, :], T.mst[:, :, 32:38], ADD, "zt0 mst", "zs")
+    tt(T.zt[:, 2, :, 0:2], T.zt[:, 1, :, 0:2], T.mst[:, :, 44:46], ADD, "zt1 mst", "zt2")
+    ts(e1, T.pnt2[:, 2:3], 5.5, None, A.is_gt, None, "pc", "e1")
+    ts(e2, T.pnt2[:, 2:3], 12.5, None, SUB, None, "pc", "e2")
+    tt(T.zs[:, :, 15:17], T.zs[:, :, 15:17], T.zt[:, 2, :, 0:2], ADD, "zs zt2", "zs")
+    ts(e3, e2, e2, 0.5, MUL, A.is_gt, "e2", "e3")
+    tt(isE, e1, e3, MUL, "e1 e3", "isE")
+    ts(isV, isE, -1.0, 1.0, MUL, ADD, "isE", "isV")
+    act(T.ucon[:], T.urow[:], F.Identity, "urow0 urow1 isE isV", "ucon", bias=isV, scale=isE)
+
+    def sc(t, k):
+        return T.sc[:, 16 * t + k:16 * t + k + 1]
+
+    def winner(t):
+        red(sc(t, 0), K[t], MAX, "P%d" % KB[t], "ck")
+        ts(T.bc[:], T.zer[:], sc(t, 0), None, ADD, None, "zer ck", "bc")
+        op("V", lambda: g.vector.transpose(T.row[:], T.bc[:]), "bc", "row")
+        red(sc(t, 1), T.row[:], MAX, "row", "gm")
+        ts(T.cnt[:, t:t + 1], sc(t, 1), -15.5, 1.0 / 32, ADD, MUL, "gm", "cnt")
+        ts(T.ne[:], T.row[:], sc(t, 1), None, A.not_equal, None, "row gm", "ne")
+        ts(sc(t, 2), T.cnt[:, t:t + 1], -32.0, sc(t, 1), MUL, ADD, "cnt gm", "ap%d" % t)
+        scan(T.run[:, t, :], T.c32[:], T.ne[:], ADD, MUL, "c32 ne", "b32%d" % t)
+
+    def record(t):
+        ts(T.mgs[:, 3 * t:3 * t + 1], sc(t, 2), -1.0, 31.0, MUL, ADD, "ap%d" % t, "a%d" % t)
+        ts(T.mgs[:, 3 * t + 1:3 * t + 2], T.run[:, t, 31:32], 32.0, None, MUL, None, "b32%d" % t, "b%d" % t)
+        cp(T.mgs[:, 3 * t + 2:3 * t + 3], T.cnt[:, t:t + 1], "cnt", "c%d" % t)
+
+    def bun(src, c0, s):
+        return src[:, :, c0 + 6 * s:c0 + 6 * s + 6]
+
+    def ends(src, s):
+        return src[:, 48 * s + 5:48 * s + 48:6]
+
+    def firsts(src, key, stop):
+        for s in range(4):
+            mms(P[3][:, 12 + s:128:16], [(T.trii[:] if s2 < s else T.tris[:], ends(src, s2)) for s2 in range(4)],
+                "trii tris " + key, "P3", False, stop and s == 3)
+
+    def bundles(bank, terms, r):
+        for lhsT, src, c0 in terms:
+            for s in range(4):
+                mm(P[bank][:, 8 * s:8 * s + 8, 0:6], lhsT, bun(src, c0, s), False, False, r, "P%d" % bank)
+
+    for t in range(2):
+        winner(t)
+        ap, b32 = sc(t, 2), T.run[:, t, 31:32]
+        av, bv = T.mgs[:, 3 * t:3 * t + 1], T.mgs[:, 3 * t + 1:3 * t + 2]
+        bn, lo, hi = (T.bn0, 1, B) if t == 0 else (T.bn1, 2, B - 1)
+        bk, kb, nb = "bn%d" % t, "P%d" % KB[t], "P%d" % KB[t + 1]
+        ts(bn[:, :, lo:hi], P[1][:, 0:8 * (hi - lo)], b32, ap, ADD, EQ, "P1 ap%d b32%d" % (t, t), bk)
+        cp(T.OH[:, :, 0:24, 29], bn[:, :, own], bk, "OH29")
+        if t == 1:
+            cp(T.OH[:, :, 0:24, 30], bn[:, :, HL - 1:HL + 23], bk, "OH30")
+        mms(P[4][:, 0, 0:9], [(T.OH[:, q // 6, 4 * (q % 6):4 * (q % 6) + 4, :], bn[:, q // 6, 4 * (q % 6) + 2:4 * (q % 6) + 11])
+                              for q in range(48)], "OH28 OH29 OH30 " + bk, "P4")
+        record(t)
+        n = float(S0 + t)
+        cp(T.ksb[:], K[t], kb, "ksb")
+        if t == 0:
+            ts(sc(t, 5), zc, 29.0, None, EQ, None, "zc", "selz")
+            mms(P[0][:, 0:256], [(i29, bn[:, :, 1:33]), (i29, bn[:, :, 2:34])], "i29 " + bk, "P0")
+        else:
+            ts(sc(t, 3), av, 28.0, None, EQ, None, "a1", "sL")
+            ts(sc(t, 4), bv, 28.0, None, EQ, None, "b1", "sR")
+            ts(iL, i30, sc(t, 3), None, MUL, None, "i30 sL", "iL")
+            ts(iR, i30, sc(t, 4), None, MUL, None, "i30 sR", "iR")
+            ts(T.mL[:], T.colk[:], sc(t, 3), 4.0, SUB, EQ, "colk sL", "mL")
+            ts(T.mR[:], T.colk[:], sc(t, 4), 1.0, ADD, EQ, "colk sR", "mR")
+            ts(sc(t, 5), zc, sc(t, 4), 29.0, SUB, EQ, "zc sR", "selz")
+            tt(T.dd[:, :, 4:30], T.bn0[:, :, 4:30], bn[:, :, 4:30], ADD, "bn0 bn1", "dd")
+            mms(P[0][:, 0:224], [(i30, bn[:, :, 3:31]), (i30, bn[:, :, 4:32]), (iL, bn[:, :, 5:33]), (iR, bn[:, :, 2:30])],
+                "i30 iL iR " + bk, "P0")
+            for s in range(4):
+                mm(P[2][:, 192 + 48 * s:240 + 48 * s], idb, bun(T.dd, HL, s), True, True, "dd", "P2")
+        ts(T.enx[:], T.xrow[:], n, None, EQ, None, "xrow", "enx")
+        ts(T.mlt[:], T.xrow[:], bv, None, EQ, None, "xrow b%d" % t, "mlt")
+        ts(T.nega[:], T.xrow[:], av, -BIG / 128, EQ, MUL, "xrow a%d" % t, "nega")
+        tt(T.cv[:], T.enx[:], T.mlt[:], SUB, "enx mlt", "cv")
+        ts(T.eqb[:], T.yrev[:], bv, None, EQ, None, "yrev b%d" % t, "eqb")
+        ld = T.ld1 if t == 0 else T.ld2
+        tt(T.tLR[:, 0, 0:9], P[4][:, 0, 0:9], T.mL[:, 0:9], MUL, "P4 mL", "tL")
+        tt(T.tLR[:, 1, 0:9], P[4][:, 0, 0:9], T.mR[:, 0:9], MUL, "P4 mR", "tR")
+        red(ld[:, 4 * rank:4 * rank + 2], T.tLR[:, :, 0:9], ADD, "tL tR", "o%d" % t)
+        send(ld[:, 4 * rank:4 * rank + 2], ld[:, 4 * rank:4 * rank + 2], "ar%d" % (t + 1), "o%d" % t)
+        if t == 0:
+            tt(T.C1[:, :, 1:33], P[0][:, 0:256], T.S[:, :, 1:33], MAX, "P0 S Sl Sr", "C1")
+            code_of(P[1][:, 0:248], T.C1[:, :, 1:32], [T.C1[:, :, 2:33]], 248, "C1", "P1")
+            ts(T.OH[:, :, 0:24, 28], T.C1[:, :, own], 29.0, None, EQ, None, "C1", "OH28")
+        else:
+            C = T.C2
+            tt(C[:, :, 3:31], P[0][:, 0:224], T.C1[:, :, 3:31], MAX, "P0 C1", "C2")
+            mms(P[1][:, 0:192], [(idb, C[:, :, 7:31]), (idn, C[:, :, 6:30])], "C2", "P1")
+            scan(T.d12[:], T.rst[:], P[2][:, 192:384], MUL, ADD, "rst P2", "d12")
+        mms(K[t + 1], [(T.idf[:], T.ksb[:]), (T.eqb[:], T.nega[:])], "idf ksb eqb nega", nb, stop=False)
+        ts(T.mlu[:], T.cv[:], sc(t, 5), None, MUL, None, "cv selz", "mlu")
+        ts(T.ent[:], T.yrev[:], n, 32.0, EQ, MUL, "yrev", "ent")
+        if t == 1:
+            tt(T.g1[:], P[1][:, 0:192], T.dd[:, :, 6:30], MUL, "P1 dd", "g1")
+            mms(P[2][:, 0:192], [(idb, T.g1[:]), (idb, C[:, :, 6:30]), (idn, C[:, :, 5:29])], "C2 g1", "P2")
+            for s in range(4):
+                code_of(P[6][:, 48 * s:48 * s + 48], bun(C, 3, s), [bun(C, HL, s)], 48, "C2", "P6")
+        ts(T.mrt[:], T.yrev[:], av, 32.0, EQ, MUL, "yrev a%d" % t, "mrt")
+        tt(T.ml[:], T.mlu[:], T.mlb[:], ADD, "mlu mlb", "ml")
+        if t == 1:
+            tt(T.h1[:], P[2][:, 0:192], T.dd[:, :, 5:29], MUL, "P2 dd", "h1")
+            for s in range(4):
+                code_of(P[6][:, 192 + 48 * s:240 + 48 * s], bun(C, HL, s), [bun(T.h1, 0, s), bun(C, 5, s)], 48, "C2 h1", "P6")
+            mm(P[3][:, 0:128], T.idf[:], T.sixu[:], True, False, "sixu", "P3")
+            firsts(T.d12, "d12", False)
+            mm(P[4][:, :, 0:6], idb, T.d12[:], True, False, "d12", "P4")
+            mm(P[5][:, :, 0:6], idb, T.i32c[:], True, False, "i32c", "P5")
+            bundles(4, [(i8, T.dd, HL), (idb, T.inv, 0)], "dd inv i8")
+            bundles(5, [(idb, C, HL)], "C2")
+        tt(T.rvt[:], T.ent[:], T.mrt[:], SUB, "ent mrt", "rvt")
+        if t == 0:
+            ts(T.mlu[:], T.mlt[:], z28, None, MUL, None, "mlt z28", "mlu")
+            ts(T.ent[:], T.mrt[:], z28, None, MUL, None, "mrt z28", "ent")
+            tt(T.mlb[:], T.mlb[:], T.mlu[:], SUB, "mlb mlu", "mlb")
+            tt(T.mr[:], T.mrb[:], T.ent[:], SUB, "mrb ent", "mr")
+            for e in range(-5, 16):
+                cp(T.zsel[:, e + 5, :], T.zs[:, :, 15 - e:31 - e], "zs", "zsel" if e == 15 else "zsel%d" % e)
+        wait("V", "ar%d" % (t + 1), arrive)
+        red(sc(t, 6), ld[:, 0::4], ADD, "o%d" % t, "Ls")
+        red(sc(t, 7), ld[:, 1::4], ADD, "o%d" % t, "Rs")
+        ts(T.r1[:], T.ml[:], sc(t, 6), None, MUL, None, "ml Ls", "r1")
+        ts(T.r2[:], T.cv[:], sc(t, 7), None, MUL, None, "cv Rs", "r2")
+        mm(K[t + 1], T.rvt[:], T.r1[:], False, False, "rvt r1", nb)
+        mm(K[t + 1], T.mrb[:] if t == 0 else T.mr[:], T.r2[:], False, True, "mrb mr r2", nb)
+
+    winner(2)
+    wv, dv = sc(2, 8), sc(2, 9)
+    ap, b32 = sc(2, 2), T.run[:, 2, 31:32]
+    ts(T.b3[:], P[6][:, 0:192], b32, ap, ADD, EQ, "P6 ap2 b322", "b3")
+    mm(P[4][:, :, 0:6], i8, T.b3[:], False, False, "b3", "P4")
+    tt(wv, ap, b32, SUB, "ap2 b322", "wv")
+    ts(dv, ap, -1.0, None, ADD, None, "ap2", "dv")
+    scan(T.d3[:], T.rst[:], T.b3[:], MUL, ADD, "rst b3", "d3")
+    mm(P[4][:, :, 0:6], idb, T.d3[:], False, True, "d3", "P4")
+    ts(T.hsv[:], P[6][:, 192:384], wv, dv, EQ, MUL, "P6 wv dv", "hsv")
+    mm(P[5][:, :, 0:6], idb, T.hsv[:], False, True, "hsv", "P5")
+    firsts(T.d3, "d3", True)
+
+    def mask(d):
+        out = T.X[:, d, :, 6:12 - d] if d < 4 else T.X[:, 0, :, 14:16]
+        ts(out, P[4][:, :, d:6], float(d), None, EQ, None, "P4 X", "Xm%d" % d)
+
+    def value(d):
+        out, m = (T.X[:, d, :, 0:6 - d], T.X[:, d, :, 6:12 - d]) if d < 4 else (T.X[:, 0, :, 12:14], T.X[:, 0, :, 14:16])
+        tt(out, P[5][:, :, d:6], m, MUL, "P5 Xm%d" % d, "Xv%d" % d)
+        if d < 4:
+            for s in range(4):
+                mm(P[XB[s]][:, 0:128], T.X[:, d, 8 * s:8 * s + 8, :], idb, d == 0, d == 3, "Xv%d Xv4" % d, "P%d" % XB[s])
+
+    mask(4)
+    mask(0)
+    value(4)
+    value(0)
+    mask(1)
+    mask(2)
+    value(1)
+    cp(T.zf[:, 0:128], P[3][:, 0:128], "P3", "zf")
+    mask(3)
+    value(2)
+    value(3)
+    mms(P[6][:, 0:32], [(T.zf[:, 12 - 4 * m4:140 - 4 * m4], T.rmm[:, m4, :]) for m4 in range(4)], "zf rmm", "P6")
+    record(2)
+    for s in range(4):
+        tt(T.xs[:, s::4], P[XB[s]][:, 0:128], T.ucon[:, s::4], MUL, "P%d ucon" % XB[s], "xs%d" % s)
+    cp(T.o16[:], P[6][:, 0:32], "P6", "o16")
+    cp(T.W[:, 16:3088].indirect(T.o16[:]), T.xs[:], "o16 xs0 xs1 xs2 xs3", "W")
+    dma("Y", T.mg[:], T.mgs[0:1, 0:9], "dout", "a0 b0 c0 a1 b1 c1 a2 b2 c2", "")
+    mms(P[7][0:8, 0:1], [(ends(d, s), T.onb[:, 0:1]) for d in (T.d12, T.d3) for s in range(4)], "d12 d3 onb", "P7")
+    for c in range(3):
+        mms(P[c][:, 0:64], [(T.zsel[:, e + 5, :], T.W[:, 16 + e + 1024 * c:16 + e + 1024 * c + 1009:16])
+                            for e in range(-5, 16)], "zsel W", "P%d" % c)
+    tt(T.flb[0:8, 0:1], T.lei[0:8, 0:1], P[7][0:8, 0:1], SUB, "lei P7", "flb")
+    dma("Y", T.fl[:], T.flb[0:8, 0:1], "dout", "flb", "")
+    YW = "Y0a Y0b Y0h Y0e"
+    for c in range(3):
+        cs = slice(64 * c, 64 * c + 64)
+        ts(T.j16[:, cs], P[c][:, 0:64], 49152.0 - 15.5, 1.0 / 32, ADD, MUL, "P%d" % c, "j%d" % c)
+        a0, a1, a2 = 64 * c, 64 * c + YV[c], 64 * c + 64
+        act(T.Y[:, 16 * a1:16 * a2], T.Y0[:].indirect(T.j16[:, a1:a2]), F.Copy, YW + " j%d" % c, "YS%d" % c)
+        ts(T.jt[:, cs], T.j16[:, cs], -32.0, 49151.0, MUL, ADD, "j%d" % c, "jt%d" % c)
+        tt(T.sy[:, cs], P[c][:, 0:64], T.jt[:, cs], ADD, "P%d jt%d" % (c, c), "sy%d" % c)
+        if c == 2:
+            mms(P[3][0:64, 0:384], [(T.sy[:, x::3], T.mst[:, :, 32 - 16 * x:80 - 16 * x]) for x in range(3)],
+                "sy0 sy1 sy2 mst", "P3")
+        for b0, b1 in ((a0, a1),) if c < 2 else ((a0, a0 + YA), (a0 + YA, a1)):
+            cp(T.Y[:, 16 * b0:16 * b1], T.Y0[:].indirect(T.j16[:, b0:b1]), YW + " j%d" % c, "YV%d" % b0)
+            if b0 == 128:
+                cp(T.fsb[0:64, :], P[3][0:64, 0:384], "P3", "fsb")
+                for gg in range(8):
+                    dma("Y", T.fs[gg, :], T.fsb[0:64, 48 * gg:48 * gg + 48], "dout", "fsb", "")
+        dma("Y", T.y[:, 16 * a0:16 * a1], T.Y[:, 16 * a0:16 * a1], "dout", "YV%d YV%d" % (a0, b0), "")
+        dma("Y" if c < 2 else "S", T.y[:, 16 * a1:16 * a2], T.Y[:, 16 * a1:16 * a2], "dout", "YS%d" % c, "")
+
+    for e in count:
+        wait("G", "c" + e, count[e])
+    for s in ndma:
+        wait("G", s, ndma[s])
+    wait("G", "sent", nsent[0])

@@ -6,24 +6,26 @@ HL, B = 4, 34
 BIG = 8388608.0
 GV = 74
 NPV = 22
-YV, YA = (18, 18, 34), 22
+CUT = (32, 22, 12, 0)
+YS = ((132, 192), (72, 132), (52, 72))
+YV = ((0, 30), (30, 52))
 KB = (3, 6, 7)
-XB = (0, 1, 2, 7)
-bf, f32, i32, u16 = "bfloat16", "float32", "int32", "uint16"
+bf, f16, f32, i32, u16 = "bfloat16", "float16", "float32", "int32", "uint16"
 
 _SBUF = [
     (i32, [192], "posi rint"), (i32, [512], "sti"), (i32, [4], "lei pint pnt2 cnt"), (i32, [272], "wi wj"),
     (u16, [192], "r16 p16 j16"), (u16, [32], "o16"),
-    (bf, [M], "vew"), (bf, [512], "stb xs"), (bf, [2048], "win"), (bf, [3088], "G W Y0"), (bf, [L], "Y"), (bf, [400], "fz"),
+    (bf, [M], "vew"), (bf, [512], "stb xr ucon"), (bf, [2048], "win"), (bf, [3088], "G W Y0"), (bf, [L], "Y"), (bf, [400], "fz"),
     (bf, [192], "fa fb fv fab i32c rst d12 b3 hsv d3 sy"), (bf, [8, B], "S bn0 bn1 C1 C2 dd"), (bf, [8, 24], "inv g1 h1"),
     (bf, [8, 25, 32], "OH"), (bf, [8, 25, 28 - NPV], "tab"), (bf, [272], "onb"), (bf, [4, 8, 16], "selh"), (bf, [8, 80], "mst"),
-    (bf, [4, 8], "pk"), (bf, [9, 128], "dg"), (bf, [128], "tris trii ngb"), (bf, [4, 32, 16], "X"), (bf, [8, 36], "zs"),
+    (bf, [4, 8], "pk"), (bf, [8, 128], "dg"), (bf, [128], "tris trii ngb"), (bf, [4, 32, 16], "X"), (bf, [8, 36], "zs"),
     (bf, [3, 8, 6], "zt"), (bf, [21, 128], "zsel"),
+    (f16, [144], "zf"), (f16, [4, 32], "rmh"),
     (f32, [4], "lef kcol flb"), (f32, [272], "fT"), (f32, [128], "onf rep idf yrev sumt mrb mr mrt rvt ent eqb"),
-    (f32, [192], "jl jt"), (f32, [4, 32], "rmm"), (f32, [8, 16], "sixu"), (f32, [512], "urow ucon"),
-    (f32, [32], "xrow col c32 zer nega k0 k0t mlb ml mlt mlu cv enx ksb msg r1 r2 bc row ne"),
-    (f32, [16], "colk mL mR"), (f32, [2, 16], "tLR"), (f32, [N, 32], "land"), (f32, [24], "ld1 ld2"), (f32, [3, 32], "run"),
-    (f32, [64], "sc"), (f32, [12], "mgs"), (f32, [144], "zf"), (f32, [384], "fsb"),
+    (f32, [192], "jl jt"), (f32, [4, 32], "rmm"), (f32, [8, 16], "sixu"), (f32, [512], "urow"),
+    (f32, [32], "xrow col nega k0t mlb ml mlt mlu cv enx msg r1 r2 row"), (f32, [64], "zer k0 ksb bc"),
+    (f32, [33], "c32 ne"), (f32, [16], "colk mL mR"), (f32, [N, 32], "land"), (f32, [12 * N], "ld1 ld2"),
+    (f32, [3, 33], "run"), (f32, [64], "sc"), (f32, [12], "mgs"), (f32, [384], "fsb"),
 ]
 SCRATCH = {n: ("sbuf", [128] + s, d) for d, s, names in _SBUF for n in names.split()}
 for _k in range(8):
@@ -146,7 +148,7 @@ def rank_program(g, core, T, topo):
     arrive = len(far) * len(far_eng) + len(near) * len(near_eng)
     P = [T["P%d" % k] for k in range(8)]
     EQ, ADD, SUB, MUL, MAX = A.is_equal, A.add, A.subtract, A.mult, A.max
-    idb, idn, idm, i29, i30, i8, iL, iR, cst = (T.dg[:, k, :] for k in range(9))
+    idb, idn, idm, i29, i30, i8, iL, iR = (T.dg[:, k, :] for k in range(8))
     own = slice(HL, HL + 24)
 
     dma("S", T.sti[0:96, :], T.st[:], "dst", "", "sti")
@@ -161,10 +163,20 @@ def rank_program(g, core, T, topo):
     ms(T.fz[:], 0.0, "fz")
     ms(T.G[:, 0:16], 0.0, "Gl")
     ms(T.G[:, 3072:3088], 0.0, "G")
-    ms(T.OH[:, :, :, 28:32], 0.0, "OH28 OH29 OH30")
+    ms(T.OH[:, :, :, 28:32], 0.0, "OH28 OH290 OH291 OH300 OH301")
     ms(T.msg[:], 0.0, "msg")
     ms(T.ngb[:], -1.0, "ngb")
     ms(T.sixu[:], 0.0, "sixu")
+    ms(T.k0[:], 0.0, "k0")
+    ms(T.c32[:], 1.0 / 32, "c32")
+    ms(T.zer[:], 0.0, "zer")
+    ms(T.ne[:], 1.0, "ne")
+    ms(T.Y0[:, 1536:1542], 0.0, "Y0h")
+    ms(T.Y0[:, 3078:3088], 0.0, "Y0e")
+    ms(T.rst[:], 1.0, "rst")
+    ms(T.zf[:], 0.0, "zf")
+    ms(T.zs[:], 0.0, "zs")
+    ms(T.rst[:, 0::6], 0.0, "rst")
     sel(T.selh[:, :, :, 0:3], T.onb[:, 0:96], [[-1, 4], [-12, 8], [-4, 3]], EQ, 0, 1, "onb", "selh")
     iota(T.kcol[:, 0:1], [[0, 1]], 0, 16, "kcol")
     sel(T.mst[:, :, 32:48], T.onb[:, 0:128], [[-16, 8], [-1, 16]], EQ, 0, 1, "onb", "mst")
@@ -178,7 +190,7 @@ def rank_program(g, core, T, topo):
     sel(T.tris[:], T.ngb[:], [[1, 128]], A.is_gt, 0, -1, "ngb", "tris")
     sel(T.trii[:], T.ngb[:], [[1, 128]], A.is_ge, 0, -1, "ngb", "trii")
     sel(T.rmm[:], T.onf[:], [[-1, 4], [-4, 32]], EQ, 0, 1, "onf", "rmm")
-    iota(T.sixu[:, :, 12:16], [[0, 8], [6, 4]], 0, 24, "sixu")
+    iota(T.sixu[:, :, 12:16], [[0, 8], [6, 4]], -L // 2, 24, "sixu")
     iota(T.i32c[:], [[0, 32], [32, 6]], 0, 0, "i32c")
     iota(T.urow[:, 0:256], [[1, 256]], -256, 0, "urow0")
     iota(T.urow[:, 256:512], [[1, 256]], 1, 0, "urow1")
@@ -233,14 +245,13 @@ def rank_program(g, core, T, topo):
     ts(T.pnt2[:, 2:3], T.pint[:, 0:1], 15, None, A.bitwise_and, None, "pint", "pc")
     cp(T.p16[:], T.posi[:], "posi", "p16")
     cp(T.col[:, 0:2], T.pnt2[:, 0:2], "pa pb", "zc")
-    ms(T.Y0[:, 1536:1542], 0.0, "Y0h")
-    ms(T.Y0[:, 3078:3088], 0.0, "Y0e")
+    ts(idn, idb, -1.0, None, MUL, None, "idb", "idn")
     ts(T.sumt[:], T.yrev[:], zc, 32.0, EQ, MUL, "yrev zc", "sumt")
     ts(yc, zc, -1.0, 31.0, MUL, ADD, "zc", "yc")
-    ts(idn, idb, -1.0, None, MUL, None, "idb", "idn")
-    ts(T.k0t[:], T.xrow[:], yc, -BIG, EQ, MUL, "xrow yc", "k0t")
     ts(idm, idb, -1.0 / 32, None, MUL, None, "idb", "idm")
-    tt(T.k0[:], T.k0t[:], T.yrev[:, 0:32], ADD, "k0t yrev", "k0")
+    ts(T.k0t[:], T.xrow[:], yc, -BIG, EQ, MUL, "xrow yc", "k0t")
+    ts(z28, zc, 28.0, None, EQ, None, "zc", "z28")
+    tt(T.k0[:, 0:32], T.k0t[:], T.yrev[:, 0:32], ADD, "k0t yrev", "k0")
     tt(T.wi[:, 0:200], P[6][:, 0:200], T.fT[:, 0:200], MUL, "P6 fT", "wi")
     ts(T.wj[:, 0:200], T.wi[:, 0:200], 63, None, A.bitwise_and, None, "wi", "wj")
     cp(T.S[:, :, 4:29], T.wj[:, 0:200], "wj", "S")
@@ -262,73 +273,71 @@ def rank_program(g, core, T, topo):
     act(T.W[:], T.G[:], F.Identity, "GV GS", "W", bias=0.0, scale=0.0)
     act(T.X[:], T.G[:, 0:2048], F.Identity, "GV GS", "X", bias=0.0, scale=0.0)
 
-    def code_of(out, prev, cur, n, r, w):
-        mms(out, [(cst, T.onb[:, 0:n]), (idn, prev)] + [(idm, c) for c in cur], r + " cst idn idm onb", w)
+    def code_of(out, prev, cur, r, w):
+        mms(out, [(idn, prev)] + [(idm, c) for c in cur], r + " idn idm", w)
 
     tt(T.wi[:, 200:272], P[3][:, 0:72], T.fT[:, 200:272], MUL, "P3 fT", "wih")
-    ms(T.dg[0:32, 8, :], 1.0, "cs0")
+    ts(T.colk[:], T.xrow[:, 0:16], kc, None, SUB, None, "xrow zc", "colk")
     ts(T.wj[:, 200:272], T.wi[:, 200:272], 63, None, A.bitwise_and, None, "wih", "wjh")
-    ms(T.dg[32:64, 8, :], 1.0 / 1024, "cs1")
-    ms(T.dg[64:128, 8, :], 0.0, "cst")
+    ts(le28, zc, 28.5, None, A.is_lt, None, "zc", "le28")
     cp(T.S[:, :, 0:4], T.wj[:, 200:232], "wjh", "Sl")
     cp(T.S[:, :, 29:B], T.wj[:, 232:272], "wjh", "Sr")
-    ms(T.c32[:], 1.0 / 32, "c32")
-    ms(T.zer[:], 0.0, "zer")
-    ts(T.colk[:], T.xrow[:, 0:16], kc, None, SUB, None, "xrow zc", "colk")
-    ts(z28, zc, 28.0, None, EQ, None, "zc", "z28")
-    ts(le28, zc, 28.5, None, A.is_lt, None, "zc", "le28")
     ts(T.mL[:], T.colk[:], 4.0, None, EQ, None, "colk", "mL")
     ts(T.mR[:], T.colk[:], 1.0, None, EQ, None, "colk", "mR")
     ts(T.mlb[:], T.xrow[:], zc, le28, EQ, MUL, "xrow zc le28", "mlb")
     ts(T.mrb[:], T.sumt[:], le28, None, MUL, None, "sumt le28", "mrb")
+    ts(T.zt[:, 0, :, :], T.mst[:, :, 38:44], 192.0, None, MUL, None, "mst", "zt0")
+    ts(T.zt[:, 1, :, 0:2], T.mst[:, :, 46:48], 192.0, None, MUL, None, "mst", "zt1")
     for k in range(4):
         cp(T.msg[32 * k:32 * k + 32, 0:28], P[2][32 * k:32 * k + 32, 28 * k:28 * k + 28], "P2 msg", "msg%d" % k)
     MSG = "msg0 msg1 msg2 msg3"
     send(T.msg[:], T.land[:, rank, :], "a%d" % rank, MSG)
-    code_of(P[1][:, 0:264], T.S[:, :, 0:33], [T.S[:, :, 1:34]], 264, "S Sl Sr cs0 cs1", "P1")
     K = [P[k][:, 0:32] for k in KB]
-    mms(K[0], [(T.idf[:], T.k0[:]), (T.sumt[:], T.msg[:])], "idf k0 sumt " + MSG, "P3", stop=False)
+    KW = [P[k][:, 0:64] for k in KB]
+    mm(KW[0], T.idf[:], T.k0[:], True, False, "idf k0", "P3")
+    mm(K[0], T.sumt[:], T.msg[:], False, False, "sumt " + MSG, "P3")
+    code_of(P[1][:, 0:264], T.S[:, :, 0:33], [T.S[:, :, 1:34]], "S Sl Sr", "P1")
     for n, r in enumerate(near + far):
         wait("P", "a%d" % r, len(near_eng) if r in near else len(far_eng))
         mm(K[0], T.sumt[:], T.land[:, r, :], False, n == N - 2, "sumt", "P3")
 
-    ts(i29, idb, 29.0, None, MUL, None, "idb", "i29")
-    ts(i30, idb, 30.0, None, MUL, None, "idb", "i30")
-    ts(i8, idb, 8.0, None, MUL, None, "idb", "i8")
-    ts(T.inv[:], T.S[:, :, own], 0.0, 8.0, EQ, MUL, "S", "inv")
-    ms(T.rst[:], 1.0, "rst")
-    ms(T.zf[:], 0.0, "zf")
-    ms(T.zs[:], 0.0, "zs")
-    ms(T.rst[:, 0::6], 0.0, "rst")
-    ts(T.zt[:, 0, :, :], T.mst[:, :, 38:44], 192.0, None, MUL, None, "mst", "zt0")
-    ts(T.zt[:, 1, :, 0:2], T.mst[:, :, 46:48], 192.0, None, MUL, None, "mst", "zt1")
     tt(T.zs[:, :, 15:21], T.zt[:, 0, :, :], T.mst[:, :, 32:38], ADD, "zt0 mst", "zs")
     tt(T.zt[:, 2, :, 0:2], T.zt[:, 1, :, 0:2], T.mst[:, :, 44:46], ADD, "zt1 mst", "zt2")
+    ts(i29, idb, 29.0, None, MUL, None, "idb", "i29")
+    ts(i30, idb, 30.0, None, MUL, None, "idb", "i30")
+    tt(T.zs[:, :, 15:17], T.zs[:, :, 15:17], T.zt[:, 2, :, 0:2], ADD, "zs zt2", "zs")
+    ts(i8, idb, 8.0, None, MUL, None, "idb", "i8")
+    ts(T.inv[:], T.S[:, :, own], 0.0, 8.0, EQ, MUL, "S", "inv")
     ts(e1, T.pnt2[:, 2:3], 5.5, None, A.is_gt, None, "pc", "e1")
     ts(e2, T.pnt2[:, 2:3], 12.5, None, SUB, None, "pc", "e2")
-    tt(T.zs[:, :, 15:17], T.zs[:, :, 15:17], T.zt[:, 2, :, 0:2], ADD, "zs zt2", "zs")
+    cp(T.rmh[:], T.rmm[:], "rmm", "rmh")
     ts(e3, e2, e2, 0.5, MUL, A.is_gt, "e2", "e3")
+    ts(T.sc[:, 5:6], zc, 29.0, None, EQ, None, "zc", "selz")
     tt(isE, e1, e3, MUL, "e1 e3", "isE")
+    ts(T.enx[:], T.xrow[:], float(S0), None, EQ, None, "xrow", "enx")
     ts(isV, isE, -1.0, 1.0, MUL, ADD, "isE", "isV")
+    ts(T.ent[:], T.yrev[:], float(S0), 32.0, EQ, MUL, "yrev", "ent")
+    for e in range(-5, 16):
+        act(T.zsel[:, e + 5, :], T.zs[:, :, 15 - e:31 - e], F.Copy, "zs", "zsel" if e == 15 else "zsel%d" % e)
     act(T.ucon[:], T.urow[:], F.Identity, "urow0 urow1 isE isV", "ucon", bias=isV, scale=isE)
 
     def sc(t, k):
         return T.sc[:, 16 * t + k:16 * t + k + 1]
 
     def winner(t):
-        red(sc(t, 0), K[t], MAX, "P%d" % KB[t], "ck")
-        ts(T.bc[:], T.zer[:], sc(t, 0), None, ADD, None, "zer ck", "bc")
-        op("V", lambda: g.vector.transpose(T.row[:], T.bc[:]), "bc", "row")
+        scan(T.bc[:], KW[t], T.zer[:], MAX, ADD, "P%d zer" % KB[t], "bc")
+        op("V", lambda: g.vector.transpose(T.row[:], T.bc[:, 32:64]), "bc", "row")
         red(sc(t, 1), T.row[:], MAX, "row", "gm")
-        ts(T.cnt[:, t:t + 1], sc(t, 1), -15.5, 1.0 / 32, ADD, MUL, "gm", "cnt")
-        ts(T.ne[:], T.row[:], sc(t, 1), None, A.not_equal, None, "row gm", "ne")
+        ts(T.cnt[:, t:t + 1], sc(t, 1), 16.5, 1.0 / 32, ADD, MUL, "gm", "cnt")
+        ts(T.ne[:, 0:32], T.row[:], sc(t, 1), None, A.not_equal, None, "row gm", "ne")
         ts(sc(t, 2), T.cnt[:, t:t + 1], -32.0, sc(t, 1), MUL, ADD, "cnt gm", "ap%d" % t)
         scan(T.run[:, t, :], T.c32[:], T.ne[:], ADD, MUL, "c32 ne", "b32%d" % t)
+        return sc(t, 2), T.run[:, t, 32:33]
 
     def record(t):
-        ts(T.mgs[:, 3 * t:3 * t + 1], sc(t, 2), -1.0, 31.0, MUL, ADD, "ap%d" % t, "a%d" % t)
-        ts(T.mgs[:, 3 * t + 1:3 * t + 2], T.run[:, t, 31:32], 32.0, None, MUL, None, "b32%d" % t, "b%d" % t)
-        cp(T.mgs[:, 3 * t + 2:3 * t + 3], T.cnt[:, t:t + 1], "cnt", "c%d" % t)
+        ts(T.mgs[:, 3 * t:3 * t + 1], sc(t, 2), -1.0, -1.0, MUL, ADD, "ap%d" % t, "a%d" % t)
+        ts(T.mgs[:, 3 * t + 1:3 * t + 2], T.run[:, t, 32:33], 32.0, -1.0, MUL, ADD, "b32%d" % t, "b%d" % t)
+        ts(T.mgs[:, 3 * t + 2:3 * t + 3], T.cnt[:, t:t + 1], -1.0, None, ADD, None, "cnt", "c%d" % t)
 
     def bun(src, c0, s):
         return src[:, :, c0 + 6 * s:c0 + 6 * s + 6]
@@ -346,102 +355,103 @@ def rank_program(g, core, T, topo):
             for s in range(4):
                 mm(P[bank][:, 8 * s:8 * s + 8, 0:6], lhsT, bun(src, c0, s), False, False, r, "P%d" % bank)
 
+    C = T.C2
     for t in range(2):
-        winner(t)
-        ap, b32 = sc(t, 2), T.run[:, t, 31:32]
+        ap, b32 = winner(t)
         av, bv = T.mgs[:, 3 * t:3 * t + 1], T.mgs[:, 3 * t + 1:3 * t + 2]
         bn, lo, hi = (T.bn0, 1, B) if t == 0 else (T.bn1, 2, B - 1)
-        bk, kb, nb = "bn%d" % t, "P%d" % KB[t], "P%d" % KB[t + 1]
-        ts(bn[:, :, lo:hi], P[1][:, 0:8 * (hi - lo)], b32, ap, ADD, EQ, "P1 ap%d b32%d" % (t, t), bk)
-        cp(T.OH[:, :, 0:24, 29], bn[:, :, own], bk, "OH29")
-        if t == 1:
-            cp(T.OH[:, :, 0:24, 30], bn[:, :, HL - 1:HL + 23], bk, "OH30")
-        mms(P[4][:, 0, 0:9], [(T.OH[:, q // 6, 4 * (q % 6):4 * (q % 6) + 4, :], bn[:, q // 6, 4 * (q % 6) + 2:4 * (q % 6) + 11])
-                              for q in range(48)], "OH28 OH29 OH30 " + bk, "P4")
+        bk, kb, nb = "bn%d0 bn%d1" % (t, t), "P%d" % KB[t], "P%d" % KB[t + 1]
+        for h in range(2):
+            ts(bn[:, 4 * h:4 * h + 4, lo:hi], P[1][:, 4 * h * (hi - lo):(4 * h + 4) * (hi - lo)], b32, ap, ADD, EQ,
+               "P1 ap%d b32%d" % (t, t), "bn%d%d" % (t, h))
+        for h in range(2):
+            gs, bh = slice(4 * h, 4 * h + 4), "bn%d%d" % (t, h)
+            cp(T.OH[:, gs, 0:24, 29], bn[:, gs, own], bh, "OH29%d" % h)
+            if t == 1:
+                cp(T.OH[:, gs, 0:24, 30], bn[:, gs, HL - 1:HL + 23], bh, "OH30%d" % h)
+            mms(P[4][:, 0, 0:9], [(T.OH[:, q // 6, 4 * (q % 6):4 * (q % 6) + 4, :], bn[:, q // 6, 4 * (q % 6) + 2:4 * (q % 6) + 11])
+                                  for q in range(24 * h, 24 * h + 24)], "OH28 OH29%d OH30%d %s" % (h, h, bh), "P4", h == 0, h == 1)
         record(t)
-        n = float(S0 + t)
-        cp(T.ksb[:], K[t], kb, "ksb")
+        cp(T.ksb[:], KW[t], kb, "ksb")
         if t == 0:
-            ts(sc(t, 5), zc, 29.0, None, EQ, None, "zc", "selz")
             mms(P[0][:, 0:256], [(i29, bn[:, :, 1:33]), (i29, bn[:, :, 2:34])], "i29 " + bk, "P0")
         else:
             ts(sc(t, 3), av, 28.0, None, EQ, None, "a1", "sL")
             ts(sc(t, 4), bv, 28.0, None, EQ, None, "b1", "sR")
-            ts(iL, i30, sc(t, 3), None, MUL, None, "i30 sL", "iL")
-            ts(iR, i30, sc(t, 4), None, MUL, None, "i30 sR", "iR")
-            ts(T.mL[:], T.colk[:], sc(t, 3), 4.0, SUB, EQ, "colk sL", "mL")
-            ts(T.mR[:], T.colk[:], sc(t, 4), 1.0, ADD, EQ, "colk sR", "mR")
-            ts(sc(t, 5), zc, sc(t, 4), 29.0, SUB, EQ, "zc sR", "selz")
-            tt(T.dd[:, :, 4:30], T.bn0[:, :, 4:30], bn[:, :, 4:30], ADD, "bn0 bn1", "dd")
-            mms(P[0][:, 0:224], [(i30, bn[:, :, 3:31]), (i30, bn[:, :, 4:32]), (iL, bn[:, :, 5:33]), (iR, bn[:, :, 2:30])],
-                "i30 iL iR " + bk, "P0")
-            for s in range(4):
-                mm(P[2][:, 192 + 48 * s:240 + 48 * s], idb, bun(T.dd, HL, s), True, True, "dd", "P2")
-        ts(T.enx[:], T.xrow[:], n, None, EQ, None, "xrow", "enx")
         ts(T.mlt[:], T.xrow[:], bv, None, EQ, None, "xrow b%d" % t, "mlt")
         ts(T.nega[:], T.xrow[:], av, -BIG / 128, EQ, MUL, "xrow a%d" % t, "nega")
+        if t == 1:
+            ts(T.mL[:], T.colk[:], sc(t, 3), 4.0, SUB, EQ, "colk sL", "mL")
+            ts(T.mR[:], T.colk[:], sc(t, 4), 1.0, ADD, EQ, "colk sR", "mR")
+            ts(iL, i30, sc(t, 3), None, MUL, None, "i30 sL", "iL")
+            ts(iR, i30, sc(t, 4), None, MUL, None, "i30 sR", "iR")
+            ts(sc(t, 5), zc, sc(t, 4), 29.0, SUB, EQ, "zc sR", "selz")
+            mms(P[0][:, 0:224], [(i30, bn[:, :, 3:31]), (i30, bn[:, :, 4:32]), (iL, bn[:, :, 5:33]), (iR, bn[:, :, 2:30])],
+                "i30 iL iR " + bk, "P0")
         tt(T.cv[:], T.enx[:], T.mlt[:], SUB, "enx mlt", "cv")
         ts(T.eqb[:], T.yrev[:], bv, None, EQ, None, "yrev b%d" % t, "eqb")
-        ld = T.ld1 if t == 0 else T.ld2
-        tt(T.tLR[:, 0, 0:9], P[4][:, 0, 0:9], T.mL[:, 0:9], MUL, "P4 mL", "tL")
-        tt(T.tLR[:, 1, 0:9], P[4][:, 0, 0:9], T.mR[:, 0:9], MUL, "P4 mR", "tR")
-        red(ld[:, 4 * rank:4 * rank + 2], T.tLR[:, :, 0:9], ADD, "tL tR", "o%d" % t)
-        send(ld[:, 4 * rank:4 * rank + 2], ld[:, 4 * rank:4 * rank + 2], "ar%d" % (t + 1), "o%d" % t)
+        ts(T.mrt[:], T.yrev[:], av, 32.0, EQ, MUL, "yrev a%d" % t, "mrt")
+        ts(T.mlu[:], T.cv[:], sc(t, 5), None, MUL, None, "cv selz", "mlu")
+        mm(KW[t + 1], T.idf[:], T.ksb[:], True, False, "idf ksb", nb)
+        mm(K[t + 1], T.eqb[:], T.nega[:], False, False, "eqb nega", nb)
+        if t == 0:
+            tt(T.rvt[:], T.ent[:], T.mrt[:], SUB, "ent mrt", "rvt")
+            tt(T.ml[:], T.mlu[:], T.mlb[:], ADD, "mlu mlb", "ml")
+        ld, c0 = T.ld1 if t == 0 else T.ld2, 12 * rank
+        tt(ld[:, c0:c0 + 12:2], P[4][:, 0, 3:9], T.mL[:, 3:9], MUL, "P4 mL", "tL%d" % t)
+        tt(ld[:, c0 + 1:c0 + 12:2], P[4][:, 0, 0:6], T.mR[:, 0:6], MUL, "P4 mR", "tR%d" % t)
+        send(ld[:, c0:c0 + 12], ld[:, c0:c0 + 12], "ar%d" % (t + 1), "tL%d tR%d" % (t, t))
         if t == 0:
             tt(T.C1[:, :, 1:33], P[0][:, 0:256], T.S[:, :, 1:33], MAX, "P0 S Sl Sr", "C1")
-            code_of(P[1][:, 0:248], T.C1[:, :, 1:32], [T.C1[:, :, 2:33]], 248, "C1", "P1")
-            ts(T.OH[:, :, 0:24, 28], T.C1[:, :, own], 29.0, None, EQ, None, "C1", "OH28")
-        else:
-            C = T.C2
-            tt(C[:, :, 3:31], P[0][:, 0:224], T.C1[:, :, 3:31], MAX, "P0 C1", "C2")
-            mms(P[1][:, 0:192], [(idb, C[:, :, 7:31]), (idn, C[:, :, 6:30])], "C2", "P1")
-            scan(T.d12[:], T.rst[:], P[2][:, 192:384], MUL, ADD, "rst P2", "d12")
-        mms(K[t + 1], [(T.idf[:], T.ksb[:]), (T.eqb[:], T.nega[:])], "idf ksb eqb nega", nb, stop=False)
-        ts(T.mlu[:], T.cv[:], sc(t, 5), None, MUL, None, "cv selz", "mlu")
-        ts(T.ent[:], T.yrev[:], n, 32.0, EQ, MUL, "yrev", "ent")
-        if t == 1:
-            tt(T.g1[:], P[1][:, 0:192], T.dd[:, :, 6:30], MUL, "P1 dd", "g1")
-            mms(P[2][:, 0:192], [(idb, T.g1[:]), (idb, C[:, :, 6:30]), (idn, C[:, :, 5:29])], "C2 g1", "P2")
-            for s in range(4):
-                code_of(P[6][:, 48 * s:48 * s + 48], bun(C, 3, s), [bun(C, HL, s)], 48, "C2", "P6")
-        ts(T.mrt[:], T.yrev[:], av, 32.0, EQ, MUL, "yrev a%d" % t, "mrt")
-        tt(T.ml[:], T.mlu[:], T.mlb[:], ADD, "mlu mlb", "ml")
-        if t == 1:
-            tt(T.h1[:], P[2][:, 0:192], T.dd[:, :, 5:29], MUL, "P2 dd", "h1")
-            for s in range(4):
-                code_of(P[6][:, 192 + 48 * s:240 + 48 * s], bun(C, HL, s), [bun(T.h1, 0, s), bun(C, 5, s)], 48, "C2 h1", "P6")
-            mm(P[3][:, 0:128], T.idf[:], T.sixu[:], True, False, "sixu", "P3")
-            firsts(T.d12, "d12", False)
-            mm(P[4][:, :, 0:6], idb, T.d12[:], True, False, "d12", "P4")
-            mm(P[5][:, :, 0:6], idb, T.i32c[:], True, False, "i32c", "P5")
-            bundles(4, [(i8, T.dd, HL), (idb, T.inv, 0)], "dd inv i8")
-            bundles(5, [(idb, C, HL)], "C2")
-        tt(T.rvt[:], T.ent[:], T.mrt[:], SUB, "ent mrt", "rvt")
-        if t == 0:
             ts(T.mlu[:], T.mlt[:], z28, None, MUL, None, "mlt z28", "mlu")
             ts(T.ent[:], T.mrt[:], z28, None, MUL, None, "mrt z28", "ent")
+            code_of(P[1][:, 0:248], T.C1[:, :, 1:32], [T.C1[:, :, 2:33]], "C1", "P1")
+            ts(T.OH[:, :, 0:24, 28], T.C1[:, :, own], 29.0, None, EQ, None, "C1", "OH28")
             tt(T.mlb[:], T.mlb[:], T.mlu[:], SUB, "mlb mlu", "mlb")
             tt(T.mr[:], T.mrb[:], T.ent[:], SUB, "mrb ent", "mr")
-            for e in range(-5, 16):
-                cp(T.zsel[:, e + 5, :], T.zs[:, :, 15 - e:31 - e], "zs", "zsel" if e == 15 else "zsel%d" % e)
+        else:
+            tt(C[:, :, 3:31], P[0][:, 0:224], T.C1[:, :, 3:31], MAX, "P0 C1", "C2")
+            tt(T.dd[:, :, 4:30], T.bn0[:, :, 4:30], bn[:, :, 4:30], ADD, "bn00 bn01 " + bk, "dd")
+            mms(P[1][:, 0:192], [(idb, C[:, :, 7:31]), (idn, C[:, :, 6:30])], "C2", "P1")
+            for s in range(4):
+                code_of(P[6][:, 48 * s:48 * s + 48], bun(C, 3, s), [bun(C, HL, s)], "C2", "P6")
+            for s in range(4):
+                mm(P[0][:, 48 * s:48 + 48 * s], idb, bun(T.dd, HL, s), True, True, "dd", "P0")
+            tt(T.ml[:], T.mlu[:], T.mlb[:], ADD, "mlu mlb", "ml")
+            tt(T.g1[:], P[1][:, 0:192], T.dd[:, :, 6:30], MUL, "P1 dd", "g1")
+            tt(T.rvt[:], T.ent[:], T.mrt[:], SUB, "ent mrt", "rvt")
+            mms(P[2][:, 0:192], [(idb, C[:, :, 6:30]), (idn, C[:, :, 5:29]), (idb, T.g1[:])], "C2 g1", "P2")
+            scan(T.d12[:], T.rst[:], P[0][:, 0:192], MUL, ADD, "rst P0", "d12")
+            mm(P[3][:, 0:128], T.idf[:], T.sixu[:], True, False, "sixu", "P3")
         wait("V", "ar%d" % (t + 1), arrive)
-        red(sc(t, 6), ld[:, 0::4], ADD, "o%d" % t, "Ls")
-        red(sc(t, 7), ld[:, 1::4], ADD, "o%d" % t, "Rs")
+        red(sc(t, 6), ld[:, 0::2], ADD, "tL%d" % t, "Ls")
+        red(sc(t, 7), ld[:, 1::2], ADD, "tR%d" % t, "Rs")
         ts(T.r1[:], T.ml[:], sc(t, 6), None, MUL, None, "ml Ls", "r1")
         ts(T.r2[:], T.cv[:], sc(t, 7), None, MUL, None, "cv Rs", "r2")
         mm(K[t + 1], T.rvt[:], T.r1[:], False, False, "rvt r1", nb)
         mm(K[t + 1], T.mrb[:] if t == 0 else T.mr[:], T.r2[:], False, True, "mrb mr r2", nb)
+        if t == 0:
+            ts(T.enx[:], T.xrow[:], float(S0 + 1), None, EQ, None, "xrow", "enx")
+            ts(T.ent[:], T.yrev[:], float(S0 + 1), 32.0, EQ, MUL, "yrev", "ent")
+        else:
+            tt(T.h1[:], P[2][:, 0:192], T.dd[:, :, 5:29], MUL, "P2 dd", "h1")
+            mm(P[4][:, :, 0:6], idb, T.d12[:], True, False, "d12", "P4")
+            bundles(4, [(i8, T.dd, HL), (idb, T.inv, 0)], "dd inv i8")
+            mm(P[5][:, :, 0:6], idb, T.i32c[:], True, False, "i32c", "P5")
+            bundles(5, [(idb, C, HL)], "C2")
+            for s in range(4):
+                code_of(P[1][:, 48 * s:48 + 48 * s], bun(C, HL, s), [bun(C, 5, s), bun(T.h1, 0, s)], "C2 h1", "P1")
+            firsts(T.d12, "d12", False)
 
-    winner(2)
+    ap, b32 = winner(2)
     wv, dv = sc(2, 8), sc(2, 9)
-    ap, b32 = sc(2, 2), T.run[:, 2, 31:32]
     ts(T.b3[:], P[6][:, 0:192], b32, ap, ADD, EQ, "P6 ap2 b322", "b3")
     mm(P[4][:, :, 0:6], i8, T.b3[:], False, False, "b3", "P4")
     tt(wv, ap, b32, SUB, "ap2 b322", "wv")
-    ts(dv, ap, -1.0, None, ADD, None, "ap2", "dv")
+    ts(dv, ap, 31.0, None, ADD, None, "ap2", "dv")
     scan(T.d3[:], T.rst[:], T.b3[:], MUL, ADD, "rst b3", "d3")
     mm(P[4][:, :, 0:6], idb, T.d3[:], False, True, "d3", "P4")
-    ts(T.hsv[:], P[6][:, 192:384], wv, dv, EQ, MUL, "P6 wv dv", "hsv")
+    ts(T.hsv[:], P[1][:, 0:192], wv, dv, EQ, MUL, "P1 wv dv", "hsv")
     mm(P[5][:, :, 0:6], idb, T.hsv[:], False, True, "hsv", "P5")
     firsts(T.d3, "d3", True)
 
@@ -454,7 +464,8 @@ def rank_program(g, core, T, topo):
         tt(out, P[5][:, :, d:6], m, MUL, "P5 Xm%d" % d, "Xv%d" % d)
         if d < 4:
             for s in range(4):
-                mm(P[XB[s]][:, 0:128], T.X[:, d, 8 * s:8 * s + 8, :], idb, d == 0, d == 3, "Xv%d Xv4" % d, "P%d" % XB[s])
+                mm(P[0][:, s::4], T.X[:, d, 8 * s:8 * s + 8, :], idb, d == 0 and s == 0, d == 3 and s == 3,
+                   "Xv%d Xv4" % d, "P0")
 
     mask(4)
     mask(0)
@@ -462,43 +473,70 @@ def rank_program(g, core, T, topo):
     value(0)
     mask(1)
     mask(2)
-    value(1)
     cp(T.zf[:, 0:128], P[3][:, 0:128], "P3", "zf")
+    value(1)
+    mms(P[6][:, 0:32], [(T.zf[:, 12 - 4 * m4:140 - 4 * m4], T.rmh[:, m4, :]) for m4 in range(4)], "zf rmh", "P6")
     mask(3)
     value(2)
     value(3)
-    mms(P[6][:, 0:32], [(T.zf[:, 12 - 4 * m4:140 - 4 * m4], T.rmm[:, m4, :]) for m4 in range(4)], "zf rmm", "P6")
+    ts(T.o16[:], P[6][:, 0:32], float(L // 2), None, ADD, None, "P6", "o16")
     record(2)
-    for s in range(4):
-        tt(T.xs[:, s::4], P[XB[s]][:, 0:128], T.ucon[:, s::4], MUL, "P%d ucon" % XB[s], "xs%d" % s)
-    cp(T.o16[:], P[6][:, 0:32], "P6", "o16")
-    cp(T.W[:, 16:3088].indirect(T.o16[:]), T.xs[:], "o16 xs0 xs1 xs2 xs3", "W")
     dma("Y", T.mg[:], T.mgs[0:1, 0:9], "dout", "a0 b0 c0 a1 b1 c1 a2 b2 c2", "")
+    for k in range(3):
+        us = slice(16 * CUT[k + 1], 16 * CUT[k])
+        act(T.xr[:, us], P[0][:, us], F.Copy, "P0", "xr%d" % k)
     mms(P[7][0:8, 0:1], [(ends(d, s), T.onb[:, 0:1]) for d in (T.d12, T.d3) for s in range(4)], "d12 d3 onb", "P7")
-    for c in range(3):
-        mms(P[c][:, 0:64], [(T.zsel[:, e + 5, :], T.W[:, 16 + e + 1024 * c:16 + e + 1024 * c + 1009:16])
-                            for e in range(-5, 16)], "zsel W", "P%d" % c)
     tt(T.flb[0:8, 0:1], T.lei[0:8, 0:1], P[7][0:8, 0:1], SUB, "lei P7", "flb")
     dma("Y", T.fl[:], T.flb[0:8, 0:1], "dout", "flb", "")
+
+    def scatter(k):
+        us = slice(16 * CUT[k + 1], 16 * CUT[k])
+        tt(T.W[:, 16:16 + 96 * CUT[k] - 5].indirect(T.o16[:, CUT[k + 1]:CUT[k]]), T.xr[:, us], T.ucon[:, us], MUL,
+           "o16 xr%d ucon W" % k, "Ws W%d" % k)
+        c0, n = 6 * CUT[k + 1], 6 * (CUT[k] - CUT[k + 1])
+        mms(P[1 + k][:, 0:n], [(T.zsel[:, e + 5, :], T.W[:, 16 + e + 16 * c0:16 + e + 16 * (c0 + n) - 15:16])
+                               for e in range(-5, 16)], "zsel W%d" % k, "P%d" % (1 + k))
+
+    def places(k):
+        c0, c1 = 6 * CUT[k + 1], 6 * CUT[k]
+        ts(T.j16[:, c0:c1], P[1 + k][:, 0:c1 - c0], 49152.0 - 15.5, 1.0 / 32, ADD, MUL, "P%d" % (1 + k), "j%d" % k)
+
+    def symbols(k):
+        c0, c1 = 6 * CUT[k + 1], 6 * CUT[k]
+        ts(T.jt[:, c0:c1], T.j16[:, c0:c1], -32.0, 49151.0, MUL, ADD, "j%d" % k, "jt%d" % k)
+        tt(T.sy[:, c0:c1], P[1 + k][:, 0:c1 - c0], T.jt[:, c0:c1], ADD, "P%d jt%d" % (1 + k, k), "sy%d" % k)
+
     YW = "Y0a Y0b Y0h Y0e"
-    for c in range(3):
-        cs = slice(64 * c, 64 * c + 64)
-        ts(T.j16[:, cs], P[c][:, 0:64], 49152.0 - 15.5, 1.0 / 32, ADD, MUL, "P%d" % c, "j%d" % c)
-        a0, a1, a2 = 64 * c, 64 * c + YV[c], 64 * c + 64
-        act(T.Y[:, 16 * a1:16 * a2], T.Y0[:].indirect(T.j16[:, a1:a2]), F.Copy, YW + " j%d" % c, "YS%d" % c)
-        ts(T.jt[:, cs], T.j16[:, cs], -32.0, 49151.0, MUL, ADD, "j%d" % c, "jt%d" % c)
-        tt(T.sy[:, cs], P[c][:, 0:64], T.jt[:, cs], ADD, "P%d jt%d" % (c, c), "sy%d" % c)
-        if c == 2:
-            mms(P[3][0:64, 0:384], [(T.sy[:, x::3], T.mst[:, :, 32 - 16 * x:80 - 16 * x]) for x in range(3)],
-                "sy0 sy1 sy2 mst", "P3")
-        for b0, b1 in ((a0, a1),) if c < 2 else ((a0, a0 + YA), (a0 + YA, a1)):
-            cp(T.Y[:, 16 * b0:16 * b1], T.Y0[:].indirect(T.j16[:, b0:b1]), YW + " j%d" % c, "YV%d" % b0)
-            if b0 == 128:
-                cp(T.fsb[0:64, :], P[3][0:64, 0:384], "P3", "fsb")
-                for gg in range(8):
-                    dma("Y", T.fs[gg, :], T.fsb[0:64, 48 * gg:48 * gg + 48], "dout", "fsb", "")
-        dma("Y", T.y[:, 16 * a0:16 * a1], T.Y[:, 16 * a0:16 * a1], "dout", "YV%d YV%d" % (a0, b0), "")
-        dma("Y" if c < 2 else "S", T.y[:, 16 * a1:16 * a2], T.Y[:, 16 * a1:16 * a2], "dout", "YS%d" % c, "")
+
+    def vectors(e, k, c0, c1, queue="Y"):
+        src, key = T.Y0[:].indirect(T.j16[:, c0:c1]), "Y_%d" % c0
+        if e == "S":
+            act(T.Y[:, 16 * c0:16 * c1], src, F.Copy, YW + " j%d" % k, key)
+        else:
+            cp(T.Y[:, 16 * c0:16 * c1], src, YW + " j%d" % k, key)
+        return lambda: dma(queue, T.y[:, 16 * c0:16 * c1], T.Y[:, 16 * c0:16 * c1], "dout", key, "")
+
+    scatter(0)
+    scatter(1)
+    places(0)
+    vectors("S", 0, *YS[0])()
+    scatter(2)
+    places(1)
+    store1 = vectors("S", 1, *YS[1])
+    symbols(0)
+    symbols(1)
+    places(2)
+    symbols(2)
+    mms(P[0][0:64, 0:384], [(T.sy[:, x::3], T.mst[:, :, 32 - 16 * x:80 - 16 * x]) for x in range(3)],
+        "sy0 sy1 sy2 mst", "P0")
+    store2 = vectors("V", 2, *YV[0])
+    store1()
+    cp(T.fsb[0:64, :], P[0][0:64, 0:384], "P0", "fsb")
+    store2()
+    for gg in range(8):
+        dma("Y", T.fs[gg, :], T.fsb[0:64, 48 * gg:48 * gg + 48], "dout", "fsb", "")
+    vectors("S", 2, *YS[2], queue="S")()
+    vectors("V", 2, *YV[1])()
 
     for e in count:
         wait("G", "c" + e, count[e])

@@ -4,34 +4,34 @@ from concourse.mybir import AluOpType as A, AxisListType, ActivationFunctionType
 N, L, M, S0 = 6, 3072, 6144, 28
 HL, B = 4, 34
 BIG = 8388608.0
-GV = 74
+WV = (3, 5, 7)
+GV = 88
 NPV = 22
 CUT = (32, 22, 12, 0)
-YS = ((132, 192), (72, 132), (52, 72))
-YV = ((0, 30), (30, 52))
+HB = (2, 0)
 KB = (3, 6, 7)
 bf, f16, f32, i32, u16 = "bfloat16", "float16", "float32", "int32", "uint16"
 
 _SBUF = [
-    (i32, [192], "posi rint"), (i32, [512], "sti"), (i32, [4], "lei pint pnt2 cnt"), (i32, [272], "wi wj"),
+    (i32, [192], "posi rint pce"), (i32, [512], "sti"), (i32, [4], "lei pint pnt2 cnt"), (i32, [272], "wi wj"),
     (u16, [192], "r16 p16 j16"), (u16, [32], "o16"),
-    (bf, [M], "vew"), (bf, [512], "stb xr ucon"), (bf, [2048], "win"), (bf, [3088], "G W Y0"), (bf, [L], "Y"), (bf, [400], "fz"),
-    (bf, [192], "fa fb fv fab i32c rst d12 b3 hsv d3 sy"), (bf, [8, B], "S bn0 bn1 C1 C2 dd"), (bf, [8, 24], "inv g1 h1"),
-    (bf, [8, 25, 32], "OH"), (bf, [8, 25, 28 - NPV], "tab"), (bf, [272], "onb"), (bf, [4, 8, 16], "selh"), (bf, [8, 80], "mst"),
+    (bf, [M], "vew"), (bf, [512], "stb xr ucon"), (bf, [2048], "win"), (bf, [3088], "G W Y0"), (bf, [L], "Y"), (bf, [2, 400], "fz"),
+    (bf, [192], "i32c rst d12 b3 hsv d3"), (bf, [8, B], "S bn0 bn1 C1 C2 dd"), (bf, [8, 24], "inv g1 h1"),
+    (bf, [8, 25, 32], "OH"), (bf, [8, 25, 28 - NPV], "tab"), (bf, [400], "onb"), (bf, [4, 8, 16], "selh"), (bf, [8, 80], "mst"),
     (bf, [4, 8], "pk"), (bf, [8, 128], "dg"), (bf, [128], "tris trii ngb"), (bf, [4, 32, 16], "X"), (bf, [8, 36], "zs"),
     (bf, [3, 8, 6], "zt"), (bf, [21, 128], "zsel"),
-    (f16, [144], "zf"), (f16, [4, 32], "rmh"),
+    (f16, [144], "zf"), (f16, [4, 32], "rmh"), (f16, [128], "sumh"), (f16, [2, 32], "msg"), (f16, [2, N, 32], "land"),
     (f32, [4], "lef kcol flb"), (f32, [272], "fT"), (f32, [128], "onf rep idf yrev sumt mrb mr mrt rvt ent eqb"),
-    (f32, [192], "jl jt"), (f32, [4, 32], "rmm"), (f32, [8, 16], "sixu"), (f32, [512], "urow"),
-    (f32, [32], "xrow col nega k0t mlb ml mlt mlu cv enx msg r1 r2 row"), (f32, [64], "zer k0 ksb bc"),
-    (f32, [33], "c32 ne"), (f32, [16], "colk mL mR"), (f32, [N, 32], "land"), (f32, [12 * N], "ld1 ld2"),
-    (f32, [3, 33], "run"), (f32, [64], "sc"), (f32, [12], "mgs"), (f32, [384], "fsb"),
+    (f32, [192], "jl jt sy"), (f32, [4, 32], "rmm"), (f32, [8, 16], "sixu"), (f32, [512], "urow"),
+    (f32, [32], "xrow col nega k0t mlb ml mlt mlu cv enx r1 r2 row"), (f32, [64], "zer k0 ksb bc"),
+    (f32, [33], "c32 ne"), (f32, [16], "colk mL mR"), (f32, [12 * N], "ld1 ld2"),
+    (f32, [3, 33], "run"), (f32, [64], "sc"), (f32, [12], "mgs"), (f32, [2, 6, 16], "fsb"),
 ]
 SCRATCH = {n: ("sbuf", [128] + s, d) for d, s, names in _SBUF for n in names.split()}
 for _k in range(8):
     SCRATCH["P%d" % _k] = ("psum", [128, 32, 16] if _k in (4, 5) else [128, 512], f32)
 
-SEMAPHORES = (["cV", "cS", "cP", "cG", "dpos", "dst", "dle", "dve", "dout", "sent", "ar1", "ar2"]
+SEMAPHORES = (["cV", "cS", "cP", "cG", "dpos", "dst", "dle", "dve", "dout", "sent", "ar0", "ar1", "ar2"]
               + ["a%d" % r for r in range(N)])
 
 
@@ -151,38 +151,40 @@ def rank_program(g, core, T, topo):
     idb, idn, idm, i29, i30, i8, iL, iR = (T.dg[:, k, :] for k in range(8))
     own = slice(HL, HL + 24)
 
-    dma("S", T.sti[0:96, :], T.st[:], "dst", "", "sti")
+    dma("Y", T.sti[0:96, :], T.st[:], "dst", "", "sti")
     dma("Y", T.posi[:], T.pos[:], "dpos", "", "posi")
-    dma("Y", T.lei[0:8, 0:1], T.le[:], "dle", "", "lei")
+    dma("S", T.lei[0:8, 0:1], T.le[:], "dle", "", "lei")
     dma("Y", T.vew[:], T.ve[:], "dve", "posi sti", "vew")
 
     ms(T.onb[:], 1.0, "onb")
     ms(T.selh[:], 0.0, "selh")
     ms(T.onf[:], 1.0, "onf")
     ms(T.mst[:], 0.0, "mst")
-    ms(T.fz[:], 0.0, "fz")
-    ms(T.G[:, 0:16], 0.0, "Gl")
-    ms(T.G[:, 3072:3088], 0.0, "G")
-    ms(T.OH[:, :, :, 28:32], 0.0, "OH28 OH290 OH291 OH300 OH301")
     ms(T.msg[:], 0.0, "msg")
     ms(T.ngb[:], -1.0, "ngb")
-    ms(T.sixu[:], 0.0, "sixu")
-    ms(T.k0[:], 0.0, "k0")
-    ms(T.c32[:], 1.0 / 32, "c32")
-    ms(T.zer[:], 0.0, "zer")
-    ms(T.ne[:], 1.0, "ne")
-    ms(T.Y0[:, 1536:1542], 0.0, "Y0h")
-    ms(T.Y0[:, 3078:3088], 0.0, "Y0e")
-    ms(T.rst[:], 1.0, "rst")
     ms(T.zf[:], 0.0, "zf")
-    ms(T.zs[:], 0.0, "zs")
-    ms(T.rst[:, 0::6], 0.0, "rst")
-    sel(T.selh[:, :, :, 0:3], T.onb[:, 0:96], [[-1, 4], [-12, 8], [-4, 3]], EQ, 0, 1, "onb", "selh")
+
+    def fill(out, n, c, w):
+        act(out, T.onb[:, 0:n], F.Identity, "onb", w, bias=c, scale=0.0)
+
+    fill(T.G[:, 0:16], 16, 0.0, "Gl")
+    fill(T.G[:, 3072:3088], 16, 0.0, "G")
+    for k in range(2):
+        fill(T.fz[:, k, :], 400, 0.0, "fz_ fz" if k else "fz_")
+        fill(T.OH[:, 4 * k:4 * k + 4, :, 28:32], 400, 0.0, "OH_ OH28 OH290 OH291 OH300 OH301" if k else "OH_")
+    fill(T.sixu[:], 128, 0.0, "sixu")
+    fill(T.k0[:], 64, 0.0, "k0")
+    fill(T.zer[:], 64, 0.0, "zer")
+    fill(T.c32[:], 33, 1.0 / 32, "c32")
+    fill(T.ne[:], 33, 1.0, "ne")
+    fill(T.Y0[:, 1536:1542], 6, 0.0, "Y0h")
+    fill(T.Y0[:, 3078:3088], 10, 0.0, "Y0e")
+    iota(T.pint[:, 0:1], [[0, 1]], 0, 1, "pint", False)
     iota(T.kcol[:, 0:1], [[0, 1]], 0, 16, "kcol")
+    sel(T.selh[:, :, :, 0:3], T.onb[:, 0:96], [[-1, 4], [-12, 8], [-4, 3]], EQ, 0, 1, "onb", "selh")
     sel(T.mst[:, :, 32:48], T.onb[:, 0:128], [[-16, 8], [-1, 16]], EQ, 0, 1, "onb", "mst")
     sel(T.rep[:], T.onf[:], [[-1, 8], [0, 16]], EQ, 0, 1, "onf", "rep")
     iota(T.jl[:], [[16, 192]], 0, 1, "jl")
-    iota(T.pint[:, 0:1], [[0, 1]], 0, 1, "pint", False)
     iota(T.yrev[:], [[0, 4], [-1, 32]], 31, 0, "yrev")
     iota(T.xrow[:], [[1, 32]], 0, 0, "xrow")
     sel(T.idf[:], T.onf[:], [[-1, 128]], EQ, 0, 1, "onf", "idf")
@@ -194,80 +196,85 @@ def rank_program(g, core, T, topo):
     iota(T.i32c[:], [[0, 32], [32, 6]], 0, 0, "i32c")
     iota(T.urow[:, 0:256], [[1, 256]], -256, 0, "urow0")
     iota(T.urow[:, 256:512], [[1, 256]], 1, 0, "urow1")
-    ts(T.pk[:, 1, :], T.mst[:, :, 33], 64.0, None, MUL, None, "mst", "pk1")
-    ts(T.pk[:, 2, :], T.mst[:, :, 34], 4096.0, None, MUL, None, "mst", "pk2")
-    tt(T.pk[:, 3, :], T.pk[:, 1, :], T.mst[:, :, 32], ADD, "pk1 mst", "pk3")
-    tt(T.pk[:, 0, :], T.pk[:, 3, :], T.pk[:, 2, :], ADD, "pk3 pk2", "pk")
-
-    ts(T.rint[:], T.posi[:], 2047, None, A.bitwise_and, None, "posi", "rint")
-    cp(T.r16[:], T.rint[:], "rint", "r16")
-    for k in range(2):
-        cs = slice(256 * k, 256 * k + 256)
-        ts(T.stb[0:96, cs], T.sti[0:96, cs], 1.0, None, ADD, None, "sti", "stb%d" % k)
-        for h in range(4):
-            mm(P[2 * k + h // 2][:, 256 * (h % 2):256 * (h % 2) + 256], T.selh[0:96, h, :, :], T.stb[0:96, cs], True, True,
-               "selh stb%d" % k, "P%d" % (2 * k + h // 2))
-    tt(T.lef[0:8, 0:1], T.lei[0:8, 0:1], T.kcol[0:8, 0:1], ADD, "lei kcol", "lef")
-    mm(P[7][:, 0:1], T.rep[0:8, :], T.lef[0:8, 0:1], True, True, "rep lef", "P7")
-    ts(T.fa[:], T.posi[:], 2048.0, 1.0 / 64, A.is_lt, MAX, "posi", "fa")
-    ts(T.fb[:], T.posi[:], 4096.0, 1.0 / 64, A.is_lt, MAX, "posi", "fb")
-    for k in range(2):
-        for h in range(4):
-            bank, c0 = 2 * k + h // 2, 512 * h + 256 * k
-            src = P[bank][:, 256 * (h % 2):256 * (h % 2) + 256]
-            if h >= 2:
-                cp(T.win[:, c0:c0 + 256], src, "P%d" % bank, "win%d%d" % (k, h))
-            else:
-                act(T.win[:, c0:c0 + 256], src, F.Copy, "P%d" % bank, "win%d%d" % (k, h))
-    WIN = "win01 win03 win11 win13 r16"
-    act(T.G[:, HL + 16 * GV:HL + L], T.win[:].indirect(T.r16[:, GV:192]), F.Copy, WIN + " G", "GS")
-    ts(T.fv[:], T.jl[:], P[7][:, 0:1], None, A.is_lt, None, "jl P7", "fv")
-    tt(T.fab[:], T.fa[:], T.fb[:], MUL, "fa fb", "fab")
-    for x in range(3):
-        tt(T.fz[:, 6 + x:6 + x + 384:6], T.fab[:, x::3], T.fv[:, x::3], MUL, "fab fv fz", "fz%d" % x)
-    cp(T.G[:, HL:HL + 16 * GV], T.win[:].indirect(T.r16[:, 0:GV]), WIN + " Gl", "GV")
-
-    def f_terms(pairs, b0, n):
-        return [(T.fz[:, 6 + 6 * (x // 3) + x % 3 - 3 * rho:388 + 6 * (x // 3) + x % 3 - 3 * rho:3],
-                 T.mst[:, :, 32 - HL + 24 * rho - 16 * x + b0:32 - HL + 24 * rho - 16 * x + b0 + n]) for rho, x in pairs]
-
-    FZ = "fz0 fz1 fz2 mst"
-    mms(P[7][:, 0:200], f_terms(((0, 0), (0, 1), (1, 1), (1, 2), (1, 3)), 4, 25), FZ, "P7")
-    mms(P[7][:, 200:232], f_terms(((0, -1), (1, 1)), 0, 4), FZ, "P7")
-    mms(P[7][:, 232:272], f_terms(((0, 1), (1, 3)), 29, 5), FZ, "P7")
-    act(T.fT[:], P[7][:, 0:272], F.Copy, "P7", "fT")
-    for b in list(range(4, 29)) + list(range(4)) + list(range(29, B)):
-        out = P[6][:, b - 4:200:25] if 4 <= b < 29 else P[3][:, b:32:4] if b < 4 else P[3][:, b + 3:72:5]
-        mm(out, T.G[:, b:b + 3049:24], T.pk[:, 0, :], True, True, "GV GS pk", "P6" if 4 <= b < 29 else "P3")
     zc, kc, z28, le28, isE, isV, yc, e1, e2, e3 = (T.col[:, k:k + 1] for k in range(10))
     ts(T.pnt2[:, 0:1], T.pint[:, 0:1], 31, None, A.bitwise_and, None, "pint", "pa")
     ts(T.pnt2[:, 1:2], T.pint[:, 0:1], 5, None, A.arith_shift_right, None, "pint", "pb")
     ts(T.pnt2[:, 2:3], T.pint[:, 0:1], 15, None, A.bitwise_and, None, "pint", "pc")
-    cp(T.p16[:], T.posi[:], "posi", "p16")
     cp(T.col[:, 0:2], T.pnt2[:, 0:2], "pa pb", "zc")
-    ts(idn, idb, -1.0, None, MUL, None, "idb", "idn")
-    ts(T.sumt[:], T.yrev[:], zc, 32.0, EQ, MUL, "yrev zc", "sumt")
+    ts(e1, T.pnt2[:, 2:3], 5.5, None, A.is_gt, None, "pc", "e1")
+    ts(e2, T.pnt2[:, 2:3], 12.5, None, SUB, None, "pc", "e2")
     ts(yc, zc, -1.0, 31.0, MUL, ADD, "zc", "yc")
-    ts(idm, idb, -1.0 / 32, None, MUL, None, "idb", "idm")
-    ts(T.k0t[:], T.xrow[:], yc, -BIG, EQ, MUL, "xrow yc", "k0t")
+    ts(T.pk[:, 1, :], T.mst[:, :, 33], 64.0, None, MUL, None, "mst", "pk1")
+    ts(T.pk[:, 2, :], T.mst[:, :, 34], 4096.0, None, MUL, None, "mst", "pk2")
     ts(z28, zc, 28.0, None, EQ, None, "zc", "z28")
+    tt(T.pk[:, 3, :], T.pk[:, 1, :], T.mst[:, :, 32], ADD, "pk1 mst", "pk3")
+    ts(le28, zc, 28.5, None, A.is_lt, None, "zc", "le28")
+    tt(T.pk[:, 0, :], T.pk[:, 3, :], T.pk[:, 2, :], ADD, "pk3 pk2", "pk")
+
+    tt(T.lef[0:8, 0:1], T.lei[0:8, 0:1], T.kcol[0:8, 0:1], ADD, "lei kcol", "lef")
+    mm(P[7][:, 256:257], T.rep[0:8, :], T.lef[0:8, 0:1], True, True, "rep lef", "P7")
+    for k in range(2):
+        cs = slice(256 * k, 256 * k + 256)
+        ts(T.stb[0:96, cs], T.sti[0:96, cs], 1.0, None, ADD, None, "sti", "stb%d" % k)
+        for h in range(4):
+            mm(P[4 * k + h][:, 0:16, :] if 4 * k + h in (4, 5) else P[4 * k + h][:, 0:256], T.selh[0:96, h, :, :],
+               T.stb[0:96, cs], True, True, "selh stb%d" % k, "P%d" % (4 * k + h))
+    ts(T.rint[:], T.posi[:], 2047, None, A.bitwise_and, None, "posi", "rint")
+    ts(T.pce[:], T.posi[:], -3071.5, 1.0 / 2048, ADD, MUL, "posi", "pce")
+    cp(T.r16[:], T.rint[:], "rint", "r16")
+    for bank in range(8):
+        c0 = 512 * (bank % 4) + 256 * (bank // 4)
+        src = P[bank][:, 0:16, :] if bank in (4, 5) else P[bank][:, 0:256]
+        if bank in WV:
+            cp(T.win[:, c0:c0 + 256], src, "P%d" % bank, "win%d" % bank)
+        else:
+            act(T.win[:, c0:c0 + 256], src, F.Copy, "P%d" % bank, "win%d" % bank)
+    WIN = " ".join("win%d" % k for k in range(8)) + " r16"
+    act(T.G[:, HL + 16 * GV:HL + L], T.win[:].indirect(T.r16[:, GV:192]), F.Copy, WIN + " G", "GS")
+    for x in range(3):
+        ts(T.fz[:, 0, 6 + x:6 + x + 384:6], T.pce[:, x::3], -63.0 / 64, -63.0 / 4096, MUL, MAX, "pce fz", "fz%d" % x)
+        ts(T.fz[:, 1, 6 + x:6 + x + 384:6], T.jl[:, x::3], P[7][:, 256:257], -2.0, A.is_ge, MUL, "jl P7 fz", "fv%d" % x)
+    cp(T.G[:, HL:HL + 16 * GV], T.win[:].indirect(T.r16[:, 0:GV]), WIN + " Gl", "GV")
+
+    def f_terms(pairs, b0, n):
+        return [(T.fz[:, k, 6 + 6 * (x // 3) + x % 3 - 3 * rho:388 + 6 * (x // 3) + x % 3 - 3 * rho:3],
+                 T.mst[:, :, 32 - HL + 24 * rho - 16 * x + b0:32 - HL + 24 * rho - 16 * x + b0 + n])
+                for rho, x in pairs for k in range(2)]
+
+    FZ = "fz0 fz1 fz2 fv0 fv1 fv2 mst"
+    mms(P[7][:, 0:200], f_terms(((0, 0), (0, 1), (1, 1), (1, 2), (1, 3)), 4, 25), FZ, "P7")
+    mms(P[7][:, 200:232], f_terms(((0, -1), (1, 1)), 0, 4), FZ, "P7")
+    mms(P[7][:, 232:272], f_terms(((0, 1), (1, 3)), 29, 5), FZ, "P7")
+    act(T.fT[:], P[7][:, 0:272], F.Relu, "P7", "fT", bias=1.0 / 64)
+    for b in list(range(4, 29)) + list(range(4)) + list(range(29, B)):
+        out = P[6][:, b - 4:200:25] if 4 <= b < 29 else P[3][:, b:32:4] if b < 4 else P[3][:, b + 3:72:5]
+        mm(out, T.G[:, b:b + 3049:24], T.pk[:, 0, :], True, True, "GV GS pk", "P6" if 4 <= b < 29 else "P3")
+    cp(T.p16[:], T.posi[:], "posi", "p16")
+    ts(T.k0t[:], T.xrow[:], yc, -BIG, EQ, MUL, "xrow yc", "k0t")
+    ts(idn, idb, -1.0, None, MUL, None, "idb", "idn")
+    ts(idm, idb, -1.0 / 32, None, MUL, None, "idb", "idm")
     tt(T.k0[:, 0:32], T.k0t[:], T.yrev[:, 0:32], ADD, "k0t yrev", "k0")
-    tt(T.wi[:, 0:200], P[6][:, 0:200], T.fT[:, 0:200], MUL, "P6 fT", "wi")
-    ts(T.wj[:, 0:200], T.wi[:, 0:200], 63, None, A.bitwise_and, None, "wi", "wj")
-    cp(T.S[:, :, 4:29], T.wj[:, 0:200], "wj", "S")
+    ts(T.sumh[:], T.yrev[:], zc, 32.0, EQ, MUL, "yrev zc", "sumh")
+    ts(T.k0[:, 0:28], T.k0[:, 0:28], 32.0 * 4 * 2 * N * (L // 2), None, ADD, None, "k0", "k0")
+    for h in range(2):
+        tt(T.wi[:, 100 * h:100 * h + 100], P[6][:, 100 * h:100 * h + 100], T.fT[:, 100 * h:100 * h + 100], MUL, "P6 fT", "wi%d" % h)
+    for h in range(2):
+        ts(T.wj[:, 100 * h:100 * h + 100], T.wi[:, 100 * h:100 * h + 100], 63, None, A.bitwise_and, None, "wi%d" % h, "wj%d" % h)
+    for h in range(2):
+        cp(T.S[:, 4 * h:4 * h + 4, 4:29], T.wj[:, 100 * h:100 * h + 100], "wj%d" % h, "S%d" % h)
 
     for h in range(2):
         gs = slice(4 * h, 4 * h + 4)
         for x in range(NPV, 28):
-            act(T.tab[:, gs, :, x - NPV], T.S[:, gs, HL:HL + 25], F.Abs, "S", "tab%d_%d" % (h, x), bias=-float(x + 1))
+            act(T.tab[:, gs, :, x - NPV], T.S[:, gs, HL:HL + 25], F.Abs, "S%d" % h, "tab%d_%d" % (h, x), bias=-float(x + 1))
         act(T.OH[:, gs, :, NPV:28], T.tab[:, gs, :, :], F.Relu, " ".join("tab%d_%d" % (h, x) for x in range(NPV, 28)),
             "OHs%d" % h, bias=1.0, scale=-1.0)
         for x in range(NPV):
-            ts(T.OH[:, gs, :, x], T.S[:, gs, HL:HL + 25], float(x + 1), None, EQ, None, "S", "OHv%d_%d" % (h, x))
+            ts(T.OH[:, gs, :, x], T.S[:, gs, HL:HL + 25], float(x + 1), None, EQ, None, "S%d" % h, "OHv%d_%d" % (h, x))
         for q in range(24):
             gg, b0 = 4 * h + q // 6, 4 * (q % 6)
-            mm(P[2][:, 0:112], T.OH[:, gg, b0 + 1:b0 + 5, :], T.OH[:, gg, b0:b0 + 4, 0:28], h == 0 and q == 0,
-               h == 1 and q == 23, "OHs%d OHv%d_%d OH28" % (h, h, NPV - 1), "P2")
+            mm(P[HB[h]][:, 0:112], T.OH[:, gg, b0 + 1:b0 + 5, :], T.OH[:, gg, b0:b0 + 4, 0:28], q == 0, q == 23,
+               "OHs%d OHv%d_%d OH28" % (h, h, NPV - 1), "P%d" % HB[h])
     act(T.Y0[:, 0:1536], T.vew[:].indirect(T.p16[:, 0:96]), F.Copy, "vew p16", "Y0a")
     act(T.Y0[:, 1542:3078], T.vew[:].indirect(T.p16[:, 96:192]), F.Copy, "vew p16", "Y0b")
     act(T.W[:], T.G[:], F.Identity, "GV GS", "W", bias=0.0, scale=0.0)
@@ -276,40 +283,48 @@ def rank_program(g, core, T, topo):
     def code_of(out, prev, cur, r, w):
         mms(out, [(idn, prev)] + [(idm, c) for c in cur], r + " idn idm", w)
 
+    def counts(h):
+        for k in range(4):
+            ts(T.msg[32 * k:32 * k + 32, h, 0:28], P[HB[h]][32 * k:32 * k + 32, 28 * k:28 * k + 28], -float(L // 2), None,
+               ADD, None, "P%d msg" % HB[h], "msg%d%d" % (h, k))
+        keys = " ".join("msg%d%d" % (h, k) for k in range(4))
+        send(T.msg[:, h, :], T.land[:, h, rank, :], "ar0" if h == 0 else "a%d" % rank, keys)
+        return keys
+
+    MSG0 = counts(0)
     tt(T.wi[:, 200:272], P[3][:, 0:72], T.fT[:, 200:272], MUL, "P3 fT", "wih")
     ts(T.colk[:], T.xrow[:, 0:16], kc, None, SUB, None, "xrow zc", "colk")
     ts(T.wj[:, 200:272], T.wi[:, 200:272], 63, None, A.bitwise_and, None, "wih", "wjh")
-    ts(le28, zc, 28.5, None, A.is_lt, None, "zc", "le28")
+    ts(T.mL[:], T.colk[:], 4.0, None, EQ, None, "colk", "mL")
     cp(T.S[:, :, 0:4], T.wj[:, 200:232], "wjh", "Sl")
     cp(T.S[:, :, 29:B], T.wj[:, 232:272], "wjh", "Sr")
-    ts(T.mL[:], T.colk[:], 4.0, None, EQ, None, "colk", "mL")
     ts(T.mR[:], T.colk[:], 1.0, None, EQ, None, "colk", "mR")
     ts(T.mlb[:], T.xrow[:], zc, le28, EQ, MUL, "xrow zc le28", "mlb")
-    ts(T.mrb[:], T.sumt[:], le28, None, MUL, None, "sumt le28", "mrb")
     ts(T.zt[:, 0, :, :], T.mst[:, :, 38:44], 192.0, None, MUL, None, "mst", "zt0")
     ts(T.zt[:, 1, :, 0:2], T.mst[:, :, 46:48], 192.0, None, MUL, None, "mst", "zt1")
-    for k in range(4):
-        cp(T.msg[32 * k:32 * k + 32, 0:28], P[2][32 * k:32 * k + 32, 28 * k:28 * k + 28], "P2 msg", "msg%d" % k)
-    MSG = "msg0 msg1 msg2 msg3"
-    send(T.msg[:], T.land[:, rank, :], "a%d" % rank, MSG)
+    MSG1 = counts(1)
     K = [P[k][:, 0:32] for k in KB]
     KW = [P[k][:, 0:64] for k in KB]
     mm(KW[0], T.idf[:], T.k0[:], True, False, "idf k0", "P3")
-    mm(K[0], T.sumt[:], T.msg[:], False, False, "sumt " + MSG, "P3")
-    code_of(P[1][:, 0:264], T.S[:, :, 0:33], [T.S[:, :, 1:34]], "S Sl Sr", "P1")
+    code_of(P[1][:, 0:264], T.S[:, :, 0:33], [T.S[:, :, 1:34]], "S0 S1 Sl Sr", "P1")
+    mms(K[0], [(T.sumh[:], T.msg[:, h, :]) for h in range(2)], "sumh %s %s" % (MSG0, MSG1), "P3", False, False)
+    wait("P", "ar0", arrive)
+    mms(K[0], [(T.sumh[:], T.land[:, 0, r, :]) for r in others], "sumh", "P3", False, False)
     for n, r in enumerate(near + far):
         wait("P", "a%d" % r, len(near_eng) if r in near else len(far_eng))
-        mm(K[0], T.sumt[:], T.land[:, r, :], False, n == N - 2, "sumt", "P3")
+        mm(K[0], T.sumh[:], T.land[:, 1, r, :], False, n == N - 2, "sumh", "P3")
 
+    ms(T.zs[:], 0.0, "zs")
+    ms(T.rst[:], 1.0, "rst")
+    ts(T.mrb[:], T.sumh[:], le28, None, MUL, None, "sumh le28", "mrb")
+    ms(T.rst[:, 0::6], 0.0, "rst")
     tt(T.zs[:, :, 15:21], T.zt[:, 0, :, :], T.mst[:, :, 32:38], ADD, "zt0 mst", "zs")
     tt(T.zt[:, 2, :, 0:2], T.zt[:, 1, :, 0:2], T.mst[:, :, 44:46], ADD, "zt1 mst", "zt2")
     ts(i29, idb, 29.0, None, MUL, None, "idb", "i29")
     ts(i30, idb, 30.0, None, MUL, None, "idb", "i30")
     tt(T.zs[:, :, 15:17], T.zs[:, :, 15:17], T.zt[:, 2, :, 0:2], ADD, "zs zt2", "zs")
     ts(i8, idb, 8.0, None, MUL, None, "idb", "i8")
-    ts(T.inv[:], T.S[:, :, own], 0.0, 8.0, EQ, MUL, "S", "inv")
-    ts(e1, T.pnt2[:, 2:3], 5.5, None, A.is_gt, None, "pc", "e1")
-    ts(e2, T.pnt2[:, 2:3], 12.5, None, SUB, None, "pc", "e2")
+    ts(T.inv[:], T.S[:, :, own], 0.0, 8.0, EQ, MUL, "S0 S1", "inv")
     cp(T.rmh[:], T.rmm[:], "rmm", "rmh")
     ts(e3, e2, e2, 0.5, MUL, A.is_gt, "e2", "e3")
     ts(T.sc[:, 5:6], zc, 29.0, None, EQ, None, "zc", "selz")
@@ -402,7 +417,7 @@ def rank_program(g, core, T, topo):
         tt(ld[:, c0 + 1:c0 + 12:2], P[4][:, 0, 0:6], T.mR[:, 0:6], MUL, "P4 mR", "tR%d" % t)
         send(ld[:, c0:c0 + 12], ld[:, c0:c0 + 12], "ar%d" % (t + 1), "tL%d tR%d" % (t, t))
         if t == 0:
-            tt(T.C1[:, :, 1:33], P[0][:, 0:256], T.S[:, :, 1:33], MAX, "P0 S Sl Sr", "C1")
+            tt(T.C1[:, :, 1:33], P[0][:, 0:256], T.S[:, :, 1:33], MAX, "P0 S0 S1 Sl Sr", "C1")
             ts(T.mlu[:], T.mlt[:], z28, None, MUL, None, "mlt z28", "mlu")
             ts(T.ent[:], T.mrt[:], z28, None, MUL, None, "mrt z28", "ent")
             code_of(P[1][:, 0:248], T.C1[:, :, 1:32], [T.C1[:, :, 2:33]], "C1", "P1")
@@ -473,11 +488,11 @@ def rank_program(g, core, T, topo):
     value(0)
     mask(1)
     mask(2)
-    cp(T.zf[:, 0:128], P[3][:, 0:128], "P3", "zf")
     value(1)
-    mms(P[6][:, 0:32], [(T.zf[:, 12 - 4 * m4:140 - 4 * m4], T.rmh[:, m4, :]) for m4 in range(4)], "zf rmh", "P6")
     mask(3)
     value(2)
+    cp(T.zf[:, 0:128], P[3][:, 0:128], "P3", "zf")
+    mms(P[6][:, 0:32], [(T.zf[:, 12 - 4 * m4:140 - 4 * m4], T.rmh[:, m4, :]) for m4 in range(4)], "zf rmh", "P6")
     value(3)
     ts(T.o16[:], P[6][:, 0:32], float(L // 2), None, ADD, None, "P6", "o16")
     record(2)
@@ -519,24 +534,27 @@ def rank_program(g, core, T, topo):
     scatter(0)
     scatter(1)
     places(0)
-    vectors("S", 0, *YS[0])()
+    vectors("S", 0, 162, 192)()
+    vectors("S", 0, 132, 162)()
     scatter(2)
     places(1)
-    store1 = vectors("S", 1, *YS[1])
+    store = [vectors("S", 1, 110, 132), vectors("S", 1, 88, 110)]
     symbols(0)
     symbols(1)
+    vectors("V", 1, 72, 88)()
     places(2)
+    store[0]()
     symbols(2)
-    mms(P[0][0:64, 0:384], [(T.sy[:, x::3], T.mst[:, :, 32 - 16 * x:80 - 16 * x]) for x in range(3)],
-        "sy0 sy1 sy2 mst", "P0")
-    store2 = vectors("V", 2, *YV[0])
-    store1()
-    cp(T.fsb[0:64, :], P[0][0:64, 0:384], "P0", "fsb")
-    store2()
-    for gg in range(8):
-        dma("Y", T.fs[gg, :], T.fsb[0:64, 48 * gg:48 * gg + 48], "dout", "fsb", "")
-    vectors("S", 2, *YS[2], queue="S")()
-    vectors("V", 2, *YV[1])()
+    store[1]()
+    store = [vectors("S", 2, 54, 72), vectors("S", 2, 40, 54, queue="S")]
+    for b in range(6):
+        op("V", lambda: g.vector.transpose(T.fsb[:, :, b, :], T.sy[:, b::6]), "sy0 sy1 sy2", "fsb%d" % b)
+    for k in range(2):
+        dma("Y", T.fs[k::2, :], T.fsb[:, k, :, :], "dout", " ".join("fsb%d" % b for b in range(6)), "")
+    store[0]()
+    vectors("V", 2, 20, 40)()
+    store[1]()
+    vectors("V", 2, 0, 20)()
 
     for e in count:
         wait("G", "c" + e, count[e])

@@ -4,26 +4,28 @@ from concourse.mybir import AluOpType as A, AxisListType, ActivationFunctionType
 N, L, M, S0 = 6, 3072, 6144, 28
 HL, B = 4, 34
 BIG = 8388608.0
-WV = (3, 5, 7)
-GV = 88
-NPV = 22
-CUT = (32, 22, 12, 0)
+WV = (860, 1312, 1680)
+GV = 96
+NPV = 21
+CUT = (32, 26, 18, 8, 0)
+TS = (124, 66, 16)
+SB = (1, 2, 3, 6)
 HB = (2, 0)
 KB = (3, 6, 7)
 bf, f16, f32, i32, u16 = "bfloat16", "float16", "float32", "int32", "uint16"
 
 _SBUF = [
-    (i32, [192], "posi rint pce"), (i32, [512], "sti"), (i32, [4], "lei pint pnt2 cnt"), (i32, [272], "wi wj"),
+    (i32, [192], "posi rint pce"), (i32, [2048], "win"), (i32, [4], "lei pint pnt2 cnt"), (i32, [8, 25], "wi wj"), (i32, [2, 72], "wm"),
     (u16, [192], "r16 p16 j16"), (u16, [32], "o16"),
-    (bf, [M], "vew"), (bf, [512], "stb xr ucon"), (bf, [2048], "win"), (bf, [3088], "G W Y0"), (bf, [L], "Y"), (bf, [2, 400], "fz"),
+    (bf, [M], "vew"), (bf, [512], "xr ucon"), (bf, [3088], "G W Y0"), (bf, [L], "Y"), (bf, [2, 400], "fz"),
     (bf, [192], "i32c rst d12 b3 hsv d3"), (bf, [8, B], "S bn0 bn1 C1 C2 dd"), (bf, [8, 24], "inv g1 h1"),
-    (bf, [8, 25, 32], "OH"), (bf, [8, 25, 28 - NPV], "tab"), (bf, [400], "onb"), (bf, [4, 8, 16], "selh"), (bf, [8, 80], "mst"),
-    (bf, [4, 8], "pk"), (bf, [8, 128], "dg"), (bf, [128], "tris trii ngb"), (bf, [4, 32, 16], "X"), (bf, [8, 36], "zs"),
-    (bf, [3, 8, 6], "zt"), (bf, [21, 128], "zsel"),
+    (bf, [8, 25, 32], "OH"), (bf, [8, 25, 28 - NPV], "tab"), (bf, [400], "onb"), (bf, [8, 80], "mst"), (f16, [8, B], "cd"), (f16, [192], "cb"),
+    (bf, [8], "pk"), (bf, [8, 128], "dg"), (bf, [128], "tris trii ngb zeb"), (bf, [4, 32, 16], "X"), (bf, [8, 36], "zs"),
+    (bf, [21, 128], "zsel"),
     (f16, [144], "zf"), (f16, [4, 32], "rmh"), (f16, [128], "sumh"), (f16, [2, 32], "msg"), (f16, [2, N, 32], "land"),
-    (f32, [4], "lef kcol flb"), (f32, [272], "fT"), (f32, [128], "onf rep idf yrev sumt mrb mr mrt rvt ent eqb"),
+    (f32, [4], "lef kcol flb"), (f32, [8, 25], "fT"), (f32, [72], "fm"), (f32, [128], "onf rep idf yrev mrb mr mrt rvt ent en1 eqb zer"),
     (f32, [192], "jl jt sy"), (f32, [4, 32], "rmm"), (f32, [8, 16], "sixu"), (f32, [512], "urow"),
-    (f32, [32], "xrow col nega k0t mlb ml mlt mlu cv enx r1 r2 row"), (f32, [64], "zer k0 ksb bc"),
+    (f32, [32], "xrow col nega k0t mlb ml mlt mlu cv enx r1 r2 row"), (f32, [64], "k0 ksb bc"),
     (f32, [33], "c32 ne"), (f32, [16], "colk mL mR"), (f32, [12 * N], "ld1 ld2"),
     (f32, [3, 33], "run"), (f32, [64], "sc"), (f32, [12], "mgs"), (f32, [2, 6, 16], "fsb"),
 ]
@@ -151,40 +153,40 @@ def rank_program(g, core, T, topo):
     idb, idn, idm, i29, i30, i8, iL, iR = (T.dg[:, k, :] for k in range(8))
     own = slice(HL, HL + 24)
 
-    dma("Y", T.sti[0:96, :], T.st[:], "dst", "", "sti")
     dma("Y", T.posi[:], T.pos[:], "dpos", "", "posi")
     dma("S", T.lei[0:8, 0:1], T.le[:], "dle", "", "lei")
-    dma("Y", T.vew[:], T.ve[:], "dve", "posi sti", "vew")
-
-    ms(T.onb[:], 1.0, "onb")
-    ms(T.selh[:], 0.0, "selh")
-    ms(T.onf[:], 1.0, "onf")
-    ms(T.mst[:], 0.0, "mst")
-    ms(T.msg[:], 0.0, "msg")
-    ms(T.ngb[:], -1.0, "ngb")
-    ms(T.zf[:], 0.0, "zf")
-
     def fill(out, n, c, w):
         act(out, T.onb[:, 0:n], F.Identity, "onb", w, bias=c, scale=0.0)
 
-    fill(T.G[:, 0:16], 16, 0.0, "Gl")
-    fill(T.G[:, 3072:3088], 16, 0.0, "G")
+    ms(T.onb[:], 1.0, "onb")
+    ms(T.win[:, 0:WV[0]], 0, "win0")
+    iota(T.win[:, WV[0]:WV[1]], [[0, WV[1] - WV[0]]], 0, 0, "win1", False)
+    fill(T.win[:, WV[1]:WV[2]], WV[2] - WV[1], 0.0, "win2")
+    fill(T.win[:, WV[2]:2048], 2048 - WV[2], 0.0, "win3")
+    order("Y", [], ["win0", "win1", "win2", "win3"])
+    order("S", [], ["win0", "win1", "win2", "win3"])
+    for k in range(3):
+        dma("YSY"[k], T.win[k::16, :], T.st[:, 2048 * k:2048 * k + 2048], "dst", "", "win" if k == 2 else "")
+    dma("Y", T.vew[:], T.ve[:], "dve", "posi win", "vew")
+
+    ms(T.onf[:], 1.0, "onf")
+    ms(T.mst[:], 0.0, "mst")
+    ms(T.msg[:], 0.0, "msg")
+    ms(T.zf[:], 0.0, "zf")
+    ms(T.pk[:], 0.0, "pk")
     for k in range(2):
         fill(T.fz[:, k, :], 400, 0.0, "fz_ fz" if k else "fz_")
-        fill(T.OH[:, 4 * k:4 * k + 4, :, 28:32], 400, 0.0, "OH_ OH28 OH290 OH291 OH300 OH301" if k else "OH_")
+    fill(T.G[:, 0:16], 16, 0.0, "Gl")
+    fill(T.G[:, 3072:3088], 16, 0.0, "G")
+    fill(T.ngb[:], 128, -1.0, "ngb")
     fill(T.sixu[:], 128, 0.0, "sixu")
-    fill(T.k0[:], 64, 0.0, "k0")
-    fill(T.zer[:], 64, 0.0, "zer")
-    fill(T.c32[:], 33, 1.0 / 32, "c32")
-    fill(T.ne[:], 33, 1.0, "ne")
-    fill(T.Y0[:, 1536:1542], 6, 0.0, "Y0h")
-    fill(T.Y0[:, 3078:3088], 10, 0.0, "Y0e")
     iota(T.pint[:, 0:1], [[0, 1]], 0, 1, "pint", False)
     iota(T.kcol[:, 0:1], [[0, 1]], 0, 16, "kcol")
-    sel(T.selh[:, :, :, 0:3], T.onb[:, 0:96], [[-1, 4], [-12, 8], [-4, 3]], EQ, 0, 1, "onb", "selh")
-    sel(T.mst[:, :, 32:48], T.onb[:, 0:128], [[-16, 8], [-1, 16]], EQ, 0, 1, "onb", "mst")
     sel(T.rep[:], T.onf[:], [[-1, 8], [0, 16]], EQ, 0, 1, "onf", "rep")
     iota(T.jl[:], [[16, 192]], 0, 1, "jl")
+    sel(T.mst[:, :, 32:48], T.onb[:, 0:128], [[-16, 8], [-1, 16]], EQ, 0, 1, "onb", "mst")
+    for k in range(3):
+        op("G", lambda: g.affine_select(T.pk[:], T.pk[:], [[-16, 8]], A.not_equal, 64.0 ** k, -k, 1), "pk", "pk")
     iota(T.yrev[:], [[0, 4], [-1, 32]], 31, 0, "yrev")
     iota(T.xrow[:], [[1, 32]], 0, 0, "xrow")
     sel(T.idf[:], T.onf[:], [[-1, 128]], EQ, 0, 1, "onf", "idf")
@@ -197,44 +199,18 @@ def rank_program(g, core, T, topo):
     iota(T.urow[:, 0:256], [[1, 256]], -256, 0, "urow0")
     iota(T.urow[:, 256:512], [[1, 256]], 1, 0, "urow1")
     zc, kc, z28, le28, isE, isV, yc, e1, e2, e3 = (T.col[:, k:k + 1] for k in range(10))
-    ts(T.pnt2[:, 0:1], T.pint[:, 0:1], 31, None, A.bitwise_and, None, "pint", "pa")
-    ts(T.pnt2[:, 1:2], T.pint[:, 0:1], 5, None, A.arith_shift_right, None, "pint", "pb")
-    ts(T.pnt2[:, 2:3], T.pint[:, 0:1], 15, None, A.bitwise_and, None, "pint", "pc")
-    cp(T.col[:, 0:2], T.pnt2[:, 0:2], "pa pb", "zc")
-    ts(e1, T.pnt2[:, 2:3], 5.5, None, A.is_gt, None, "pc", "e1")
-    ts(e2, T.pnt2[:, 2:3], 12.5, None, SUB, None, "pc", "e2")
-    ts(yc, zc, -1.0, 31.0, MUL, ADD, "zc", "yc")
-    ts(T.pk[:, 1, :], T.mst[:, :, 33], 64.0, None, MUL, None, "mst", "pk1")
-    ts(T.pk[:, 2, :], T.mst[:, :, 34], 4096.0, None, MUL, None, "mst", "pk2")
-    ts(z28, zc, 28.0, None, EQ, None, "zc", "z28")
-    tt(T.pk[:, 3, :], T.pk[:, 1, :], T.mst[:, :, 32], ADD, "pk1 mst", "pk3")
-    ts(le28, zc, 28.5, None, A.is_lt, None, "zc", "le28")
-    tt(T.pk[:, 0, :], T.pk[:, 3, :], T.pk[:, 2, :], ADD, "pk3 pk2", "pk")
 
     tt(T.lef[0:8, 0:1], T.lei[0:8, 0:1], T.kcol[0:8, 0:1], ADD, "lei kcol", "lef")
     mm(P[7][:, 256:257], T.rep[0:8, :], T.lef[0:8, 0:1], True, True, "rep lef", "P7")
-    for k in range(2):
-        cs = slice(256 * k, 256 * k + 256)
-        ts(T.stb[0:96, cs], T.sti[0:96, cs], 1.0, None, ADD, None, "sti", "stb%d" % k)
-        for h in range(4):
-            mm(P[4 * k + h][:, 0:16, :] if 4 * k + h in (4, 5) else P[4 * k + h][:, 0:256], T.selh[0:96, h, :, :],
-               T.stb[0:96, cs], True, True, "selh stb%d" % k, "P%d" % (4 * k + h))
     ts(T.rint[:], T.posi[:], 2047, None, A.bitwise_and, None, "posi", "rint")
     ts(T.pce[:], T.posi[:], -3071.5, 1.0 / 2048, ADD, MUL, "posi", "pce")
     cp(T.r16[:], T.rint[:], "rint", "r16")
-    for bank in range(8):
-        c0 = 512 * (bank % 4) + 256 * (bank // 4)
-        src = P[bank][:, 0:16, :] if bank in (4, 5) else P[bank][:, 0:256]
-        if bank in WV:
-            cp(T.win[:, c0:c0 + 256], src, "P%d" % bank, "win%d" % bank)
-        else:
-            act(T.win[:, c0:c0 + 256], src, F.Copy, "P%d" % bank, "win%d" % bank)
-    WIN = " ".join("win%d" % k for k in range(8)) + " r16"
-    act(T.G[:, HL + 16 * GV:HL + L], T.win[:].indirect(T.r16[:, GV:192]), F.Copy, WIN + " G", "GS")
+    act(T.G[:, HL + 16 * GV:HL + L], T.win[:].indirect(T.r16[:, GV:192]), F.Identity, "win r16 G", "GS", bias=1.0)
     for x in range(3):
         ts(T.fz[:, 0, 6 + x:6 + x + 384:6], T.pce[:, x::3], -63.0 / 64, -63.0 / 4096, MUL, MAX, "pce fz", "fz%d" % x)
+    for x in range(3):
         ts(T.fz[:, 1, 6 + x:6 + x + 384:6], T.jl[:, x::3], P[7][:, 256:257], -2.0, A.is_ge, MUL, "jl P7 fz", "fv%d" % x)
-    cp(T.G[:, HL:HL + 16 * GV], T.win[:].indirect(T.r16[:, 0:GV]), WIN + " Gl", "GV")
+    ts(T.G[:, HL:HL + 16 * GV], T.win[:].indirect(T.r16[:, 0:GV]), 1.0, None, ADD, None, "win r16 Gl", "GV")
 
     def f_terms(pairs, b0, n):
         return [(T.fz[:, k, 6 + 6 * (x // 3) + x % 3 - 3 * rho:388 + 6 * (x // 3) + x % 3 - 3 * rho:3],
@@ -245,40 +221,45 @@ def rank_program(g, core, T, topo):
     mms(P[7][:, 0:200], f_terms(((0, 0), (0, 1), (1, 1), (1, 2), (1, 3)), 4, 25), FZ, "P7")
     mms(P[7][:, 200:232], f_terms(((0, -1), (1, 1)), 0, 4), FZ, "P7")
     mms(P[7][:, 232:272], f_terms(((0, 1), (1, 3)), 29, 5), FZ, "P7")
-    act(T.fT[:], P[7][:, 0:272], F.Relu, "P7", "fT", bias=1.0 / 64)
+    act(T.fT[:], P[7][:, 0:200], F.Relu, "P7", "fT", bias=1.0 / 64)
+    act(T.fm[:], P[7][:, 200:272], F.Relu, "P7", "fm", bias=1.0 / 64)
+    for k in range(2):
+        fill(T.OH[:, 4 * k:4 * k + 4, :, 28:32], 400, 0.0, "OH_ OH28 OH290 OH291 OH300 OH301" if k else "OH_")
+    HALF = (slice(0, 13), slice(13, 25))
     for b in list(range(4, 29)) + list(range(4)) + list(range(29, B)):
-        out = P[6][:, b - 4:200:25] if 4 <= b < 29 else P[3][:, b:32:4] if b < 4 else P[3][:, b + 3:72:5]
-        mm(out, T.G[:, b:b + 3049:24], T.pk[:, 0, :], True, True, "GV GS pk", "P6" if 4 <= b < 29 else "P3")
-    cp(T.p16[:], T.posi[:], "posi", "p16")
-    ts(T.k0t[:], T.xrow[:], yc, -BIG, EQ, MUL, "xrow yc", "k0t")
+        bank = 3 if b < 4 or b >= 29 else 4 if b < 17 else 5
+        out = P[bank][:, 0:8, (b - 4) % 13] if bank > 3 else P[3][:, b:32:4] if b < 4 else P[3][:, b + 3:72:5]
+        mm(out, T.G[:, b:b + 3049:24], T.pk[:], True, True, "GV GS pk", "P%d" % bank)
+    ts(T.pnt2[:, 0:1], T.pint[:, 0:1], 31, None, A.bitwise_and, None, "pint", "pa")
+    ts(T.pnt2[:, 1:2], T.pint[:, 0:1], 5, None, A.arith_shift_right, None, "pint", "pb")
+    ts(T.pnt2[:, 2:3], T.pint[:, 0:1], 15, None, A.bitwise_and, None, "pint", "pc")
+    ms(T.k0[:], 0.0, "k0")
+    cp(T.col[:, 0:2], T.pnt2[:, 0:2], "pa pb", "zc")
     ts(idn, idb, -1.0, None, MUL, None, "idb", "idn")
     ts(idm, idb, -1.0 / 32, None, MUL, None, "idb", "idm")
-    tt(T.k0[:, 0:32], T.k0t[:], T.yrev[:, 0:32], ADD, "k0t yrev", "k0")
+    ts(yc, zc, -1.0, 31.0, MUL, ADD, "zc", "yc")
     ts(T.sumh[:], T.yrev[:], zc, 32.0, EQ, MUL, "yrev zc", "sumh")
-    ts(T.k0[:, 0:28], T.k0[:, 0:28], 32.0 * 4 * 2 * N * (L // 2), None, ADD, None, "k0", "k0")
-    for h in range(2):
-        tt(T.wi[:, 100 * h:100 * h + 100], P[6][:, 100 * h:100 * h + 100], T.fT[:, 100 * h:100 * h + 100], MUL, "P6 fT", "wi%d" % h)
-    for h in range(2):
-        ts(T.wj[:, 100 * h:100 * h + 100], T.wi[:, 100 * h:100 * h + 100], 63, None, A.bitwise_and, None, "wi%d" % h, "wj%d" % h)
-    for h in range(2):
-        cp(T.S[:, 4 * h:4 * h + 4, 4:29], T.wj[:, 100 * h:100 * h + 100], "wj%d" % h, "S%d" % h)
+    ts(T.k0t[:], T.xrow[:], yc, -BIG, EQ, MUL, "xrow yc", "k0t")
+    SH = (T.S[:, :, HL:HL + 13], T.S[:, :, HL + 13:HL + 25])
+    digit = [[lambda h=h: tt(T.wi[:, :, HALF[h]], P[4 + h][:, 0:8, 0:13 - h], T.fT[:, :, HALF[h]], MUL, "P%d fT" % (4 + h), "wi%d" % h),
+              lambda h=h: ts(T.wj[:, :, HALF[h]], T.wi[:, :, HALF[h]], 63, None, A.bitwise_and, None, "wi%d" % h, "wj%d" % h),
+              lambda h=h: cp(SH[h], T.wj[:, :, HALF[h]], "wj%d" % h, "S%d" % h)] for h in range(2)]
+    for step in digit[0] + digit[1][:1]:
+        step()
 
     for h in range(2):
-        gs = slice(4 * h, 4 * h + 4)
         for x in range(NPV, 28):
-            act(T.tab[:, gs, :, x - NPV], T.S[:, gs, HL:HL + 25], F.Abs, "S%d" % h, "tab%d_%d" % (h, x), bias=-float(x + 1))
-        act(T.OH[:, gs, :, NPV:28], T.tab[:, gs, :, :], F.Relu, " ".join("tab%d_%d" % (h, x) for x in range(NPV, 28)),
-            "OHs%d" % h, bias=1.0, scale=-1.0)
+            act(T.tab[:, :, HALF[h], x - NPV], T.wj[:, :, HALF[h]], F.Abs, "wj%d" % h, "tab%d_%d" % (h, x), bias=-float(x + 1))
+        act(T.OH[:, :, HALF[h], NPV:28], T.tab[:, :, HALF[h], :], F.Relu,
+            " ".join("tab%d_%d" % (h, x) for x in range(NPV, 28)), "OHs%d" % h, bias=1.0, scale=-1.0)
         for x in range(NPV):
-            ts(T.OH[:, gs, :, x], T.S[:, gs, HL:HL + 25], float(x + 1), None, EQ, None, "S%d" % h, "OHv%d_%d" % (h, x))
+            ts(T.OH[:, :, HALF[h], x], SH[h], float(x + 1), None, EQ, None, "S%d" % h, "OHv%d_%d" % (h, x))
+            if h == 0 and x in (1, 4):
+                digit[1][1 + x // 4]()
         for q in range(24):
-            gg, b0 = 4 * h + q // 6, 4 * (q % 6)
+            gg, b0 = q // 3, 12 * h + 4 * (q % 3)
             mm(P[HB[h]][:, 0:112], T.OH[:, gg, b0 + 1:b0 + 5, :], T.OH[:, gg, b0:b0 + 4, 0:28], q == 0, q == 23,
                "OHs%d OHv%d_%d OH28" % (h, h, NPV - 1), "P%d" % HB[h])
-    act(T.Y0[:, 0:1536], T.vew[:].indirect(T.p16[:, 0:96]), F.Copy, "vew p16", "Y0a")
-    act(T.Y0[:, 1542:3078], T.vew[:].indirect(T.p16[:, 96:192]), F.Copy, "vew p16", "Y0b")
-    act(T.W[:], T.G[:], F.Identity, "GV GS", "W", bias=0.0, scale=0.0)
-    act(T.X[:], T.G[:, 0:2048], F.Identity, "GV GS", "X", bias=0.0, scale=0.0)
 
     def code_of(out, prev, cur, r, w):
         mms(out, [(idn, prev)] + [(idm, c) for c in cur], r + " idn idm", w)
@@ -292,17 +273,23 @@ def rank_program(g, core, T, topo):
         return keys
 
     MSG0 = counts(0)
-    tt(T.wi[:, 200:272], P[3][:, 0:72], T.fT[:, 200:272], MUL, "P3 fT", "wih")
+    tt(T.wm[:, 0, :], P[3][:, 0:72], T.fm[:], MUL, "P3 fm", "wih")
     ts(T.colk[:], T.xrow[:, 0:16], kc, None, SUB, None, "xrow zc", "colk")
-    ts(T.wj[:, 200:272], T.wi[:, 200:272], 63, None, A.bitwise_and, None, "wih", "wjh")
+    ts(T.wm[:, 1, :], T.wm[:, 0, :], 63, None, A.bitwise_and, None, "wih", "wjh")
     ts(T.mL[:], T.colk[:], 4.0, None, EQ, None, "colk", "mL")
-    cp(T.S[:, :, 0:4], T.wj[:, 200:232], "wjh", "Sl")
-    cp(T.S[:, :, 29:B], T.wj[:, 232:272], "wjh", "Sr")
+    cp(T.S[:, :, 0:4], T.wm[:, 1, 0:32], "wjh", "Sl")
+    cp(T.S[:, :, 29:B], T.wm[:, 1, 32:72], "wjh", "Sr")
+    tt(T.k0[:, 0:32], T.k0t[:], T.yrev[:, 0:32], ADD, "k0t yrev", "k0")
+    cp(T.p16[:], T.posi[:], "posi", "p16")
+    ts(T.k0[:, 0:28], T.k0[:, 0:28], 32.0 * 4 * 2 * N * (L // 2), None, ADD, None, "k0", "k0")
     ts(T.mR[:], T.colk[:], 1.0, None, EQ, None, "colk", "mR")
-    ts(T.mlb[:], T.xrow[:], zc, le28, EQ, MUL, "xrow zc le28", "mlb")
-    ts(T.zt[:, 0, :, :], T.mst[:, :, 38:44], 192.0, None, MUL, None, "mst", "zt0")
-    ts(T.zt[:, 1, :, 0:2], T.mst[:, :, 46:48], 192.0, None, MUL, None, "mst", "zt1")
+    ms(T.zeb[:], 0.0, "zeb")
+    ms(T.zer[:], 0.0, "zer")
     MSG1 = counts(1)
+    act(T.W[:], T.G[:], F.Identity, "GV GS", "W", bias=0.0, scale=0.0)
+    act(T.Y0[:, 0:1536], T.vew[:].indirect(T.p16[:, 0:96]), F.Copy, "vew p16", "Y0a")
+    act(T.Y0[:, 1542:3078], T.vew[:].indirect(T.p16[:, 96:192]), F.Copy, "vew p16", "Y0b")
+    act(T.X[:], T.G[:, 0:2048], F.Identity, "GV GS", "X", bias=0.0, scale=0.0)
     K = [P[k][:, 0:32] for k in KB]
     KW = [P[k][:, 0:64] for k in KB]
     mm(KW[0], T.idf[:], T.k0[:], True, False, "idf k0", "P3")
@@ -314,24 +301,36 @@ def rank_program(g, core, T, topo):
         wait("P", "a%d" % r, len(near_eng) if r in near else len(far_eng))
         mm(K[0], T.sumh[:], T.land[:, 1, r, :], False, n == N - 2, "sumh", "P3")
 
+    def put(out, a, pat, base, cm, val, r, w):
+        op("G", lambda: g.affine_select(out, a, pat, A.not_equal, val, base, cm), r, w)
+
+    ms(T.c32[:], 1.0 / 32, "c32")
+    ms(T.ne[:], 1.0, "ne")
     ms(T.zs[:], 0.0, "zs")
-    ms(T.rst[:], 1.0, "rst")
-    ts(T.mrb[:], T.sumh[:], le28, None, MUL, None, "sumh le28", "mrb")
-    ms(T.rst[:, 0::6], 0.0, "rst")
-    tt(T.zs[:, :, 15:21], T.zt[:, 0, :, :], T.mst[:, :, 32:38], ADD, "zt0 mst", "zs")
-    tt(T.zt[:, 2, :, 0:2], T.zt[:, 1, :, 0:2], T.mst[:, :, 44:46], ADD, "zt1 mst", "zt2")
-    ts(i29, idb, 29.0, None, MUL, None, "idb", "i29")
-    ts(i30, idb, 30.0, None, MUL, None, "idb", "i30")
-    tt(T.zs[:, :, 15:17], T.zs[:, :, 15:17], T.zt[:, 2, :, 0:2], ADD, "zs zt2", "zs")
-    ts(i8, idb, 8.0, None, MUL, None, "idb", "i8")
-    ts(T.inv[:], T.S[:, :, own], 0.0, 8.0, EQ, MUL, "S0 S1", "inv")
-    cp(T.rmh[:], T.rmm[:], "rmm", "rmh")
-    ts(e3, e2, e2, 0.5, MUL, A.is_gt, "e2", "e3")
+    cp(T.cd[:, :, 1:B], P[1][:, 0:264], "P1", "cd")
+    ts(le28, zc, 28.5, None, A.is_lt, None, "zc", "le28")
+    ts(z28, zc, 28.0, None, EQ, None, "zc", "z28")
+    ts(e1, T.pnt2[:, 2:3], 5.5, None, A.is_gt, None, "pc", "e1")
+    ts(e2, T.pnt2[:, 2:3], 12.5, None, SUB, None, "pc", "e2")
     ts(T.sc[:, 5:6], zc, 29.0, None, EQ, None, "zc", "selz")
-    tt(isE, e1, e3, MUL, "e1 e3", "isE")
+    ts(T.mlb[:], T.xrow[:], zc, le28, EQ, MUL, "xrow zc le28", "mlb")
+    ts(T.mrb[:], T.sumh[:], le28, None, MUL, None, "sumh le28", "mrb")
+    ts(e3, e2, e2, 0.5, MUL, A.is_gt, "e2", "e3")
     ts(T.enx[:], T.xrow[:], float(S0), None, EQ, None, "xrow", "enx")
+    ts(T.inv[:], T.S[:, :, own], 0.0, 8.0, EQ, MUL, "S0 S1", "inv")
+    tt(isE, e1, e3, MUL, "e1 e3", "isE")
+    cp(T.rmh[:], T.rmm[:], "rmm", "rmh")
     ts(isV, isE, -1.0, 1.0, MUL, ADD, "isE", "isV")
-    ts(T.ent[:], T.yrev[:], float(S0), 32.0, EQ, MUL, "yrev", "ent")
+    put(T.ent[:], T.zer[:], [[0, 4], [-1, 32]], 31 - S0, 0, 32.0, "zer", "ent")
+    put(i29, T.zeb[:], [[-1, 128]], 0, 1, 29.0, "zeb", "i29")
+    put(T.en1[:], T.zer[:], [[0, 4], [-1, 32]], 30 - S0, 0, 32.0, "zer", "en1")
+    put(i30, T.zeb[:], [[-1, 128]], 0, 1, 30.0, "zeb", "i30")
+    put(i8, T.zeb[:], [[-1, 128]], 0, 1, 8.0, "zeb", "i8")
+    iota(T.Y0[:, 1536:1542], [[0, 6]], 0, 0, "Y0h")
+    iota(T.Y0[:, 3078:3088], [[0, 10]], 0, 0, "Y0e")
+    for lane, n, val in ((0, 6, 1.0), (6, 6, 192.0), (12, 2, 1.0), (14, 2, 192.0)):
+        put(T.zs[:, :, 15:15 + n], T.zs[:, :, 15:15 + n], [[-16, 8], [-1, n]], -lane, 1, val, "zs", "zs")
+    sel(T.rst[:], T.onb[:, 0:192], [[0, 32], [1, 6]], A.is_gt, 0, 0, "onb", "rst")
     for e in range(-5, 16):
         act(T.zsel[:, e + 5, :], T.zs[:, :, 15 - e:31 - e], F.Copy, "zs", "zsel" if e == 15 else "zsel%d" % e)
     act(T.ucon[:], T.urow[:], F.Identity, "urow0 urow1 isE isV", "ucon", bias=isV, scale=isE)
@@ -340,7 +339,7 @@ def rank_program(g, core, T, topo):
         return T.sc[:, 16 * t + k:16 * t + k + 1]
 
     def winner(t):
-        scan(T.bc[:], KW[t], T.zer[:], MAX, ADD, "P%d zer" % KB[t], "bc")
+        scan(T.bc[:], KW[t], T.zer[:, 0:64], MAX, ADD, "P%d zer" % KB[t], "bc")
         op("V", lambda: g.vector.transpose(T.row[:], T.bc[:, 32:64]), "bc", "row")
         red(sc(t, 1), T.row[:], MAX, "row", "gm")
         ts(T.cnt[:, t:t + 1], sc(t, 1), 16.5, 1.0 / 32, ADD, MUL, "gm", "cnt")
@@ -377,13 +376,11 @@ def rank_program(g, core, T, topo):
         bn, lo, hi = (T.bn0, 1, B) if t == 0 else (T.bn1, 2, B - 1)
         bk, kb, nb = "bn%d0 bn%d1" % (t, t), "P%d" % KB[t], "P%d" % KB[t + 1]
         for h in range(2):
-            ts(bn[:, 4 * h:4 * h + 4, lo:hi], P[1][:, 4 * h * (hi - lo):(4 * h + 4) * (hi - lo)], b32, ap, ADD, EQ,
-               "P1 ap%d b32%d" % (t, t), "bn%d%d" % (t, h))
-        for h in range(2):
-            gs, bh = slice(4 * h, 4 * h + 4), "bn%d%d" % (t, h)
-            cp(T.OH[:, gs, 0:24, 29], bn[:, gs, own], bh, "OH29%d" % h)
+            gs, bh, won = slice(4 * h, 4 * h + 4), "bn%d%d" % (t, h), "cd ap%d b32%d" % (t, t)
+            ts(bn[:, gs, lo:hi], T.cd[:, gs, lo:hi], b32, ap, ADD, EQ, won, bh)
+            ts(T.OH[:, gs, 0:24, 29], T.cd[:, gs, own], b32, ap, ADD, EQ, won, "OH29%d" % h)
             if t == 1:
-                cp(T.OH[:, gs, 0:24, 30], bn[:, gs, HL - 1:HL + 23], bh, "OH30%d" % h)
+                ts(T.OH[:, gs, 0:24, 30], T.cd[:, gs, HL - 1:HL + 23], b32, ap, ADD, EQ, won, "OH30%d" % h)
             mms(P[4][:, 0, 0:9], [(T.OH[:, q // 6, 4 * (q % 6):4 * (q % 6) + 4, :], bn[:, q // 6, 4 * (q % 6) + 2:4 * (q % 6) + 11])
                                   for q in range(24 * h, 24 * h + 24)], "OH28 OH29%d OH30%d %s" % (h, h, bh), "P4", h == 0, h == 1)
         record(t)
@@ -393,6 +390,7 @@ def rank_program(g, core, T, topo):
         else:
             ts(sc(t, 3), av, 28.0, None, EQ, None, "a1", "sL")
             ts(sc(t, 4), bv, 28.0, None, EQ, None, "b1", "sR")
+            ts(T.enx[:], T.xrow[:], float(S0 + 1), None, EQ, None, "xrow", "enx")
         ts(T.mlt[:], T.xrow[:], bv, None, EQ, None, "xrow b%d" % t, "mlt")
         ts(T.nega[:], T.xrow[:], av, -BIG / 128, EQ, MUL, "xrow a%d" % t, "nega")
         if t == 1:
@@ -423,7 +421,7 @@ def rank_program(g, core, T, topo):
             code_of(P[1][:, 0:248], T.C1[:, :, 1:32], [T.C1[:, :, 2:33]], "C1", "P1")
             ts(T.OH[:, :, 0:24, 28], T.C1[:, :, own], 29.0, None, EQ, None, "C1", "OH28")
             tt(T.mlb[:], T.mlb[:], T.mlu[:], SUB, "mlb mlu", "mlb")
-            tt(T.mr[:], T.mrb[:], T.ent[:], SUB, "mrb ent", "mr")
+            cp(T.cd[:, :, 2:33], P[1][:, 0:248], "P1", "cd")
         else:
             tt(C[:, :, 3:31], P[0][:, 0:224], T.C1[:, :, 3:31], MAX, "P0 C1", "C2")
             tt(T.dd[:, :, 4:30], T.bn0[:, :, 4:30], bn[:, :, 4:30], ADD, "bn00 bn01 " + bk, "dd")
@@ -434,9 +432,10 @@ def rank_program(g, core, T, topo):
                 mm(P[0][:, 48 * s:48 + 48 * s], idb, bun(T.dd, HL, s), True, True, "dd", "P0")
             tt(T.ml[:], T.mlu[:], T.mlb[:], ADD, "mlu mlb", "ml")
             tt(T.g1[:], P[1][:, 0:192], T.dd[:, :, 6:30], MUL, "P1 dd", "g1")
-            tt(T.rvt[:], T.ent[:], T.mrt[:], SUB, "ent mrt", "rvt")
+            tt(T.rvt[:], T.en1[:], T.mrt[:], SUB, "en1 mrt", "rvt")
             mms(P[2][:, 0:192], [(idb, C[:, :, 6:30]), (idn, C[:, :, 5:29]), (idb, T.g1[:])], "C2 g1", "P2")
             scan(T.d12[:], T.rst[:], P[0][:, 0:192], MUL, ADD, "rst P0", "d12")
+            cp(T.cb[:], P[6][:, 0:192], "P6", "cb")
             mm(P[3][:, 0:128], T.idf[:], T.sixu[:], True, False, "sixu", "P3")
         wait("V", "ar%d" % (t + 1), arrive)
         red(sc(t, 6), ld[:, 0::2], ADD, "tL%d" % t, "Ls")
@@ -444,10 +443,9 @@ def rank_program(g, core, T, topo):
         ts(T.r1[:], T.ml[:], sc(t, 6), None, MUL, None, "ml Ls", "r1")
         ts(T.r2[:], T.cv[:], sc(t, 7), None, MUL, None, "cv Rs", "r2")
         mm(K[t + 1], T.rvt[:], T.r1[:], False, False, "rvt r1", nb)
-        mm(K[t + 1], T.mrb[:] if t == 0 else T.mr[:], T.r2[:], False, True, "mrb mr r2", nb)
+        mm(K[t + 1], T.mrb[:] if t == 0 else T.mr[:], T.r2[:], False, True, "mrb r2" if t == 0 else "mr r2", nb)
         if t == 0:
-            ts(T.enx[:], T.xrow[:], float(S0 + 1), None, EQ, None, "xrow", "enx")
-            ts(T.ent[:], T.yrev[:], float(S0 + 1), 32.0, EQ, MUL, "yrev", "ent")
+            tt(T.mr[:], T.mrb[:], T.ent[:], SUB, "mrb ent", "mr")
         else:
             tt(T.h1[:], P[2][:, 0:192], T.dd[:, :, 5:29], MUL, "P2 dd", "h1")
             mm(P[4][:, :, 0:6], idb, T.d12[:], True, False, "d12", "P4")
@@ -460,7 +458,7 @@ def rank_program(g, core, T, topo):
 
     ap, b32 = winner(2)
     wv, dv = sc(2, 8), sc(2, 9)
-    ts(T.b3[:], P[6][:, 0:192], b32, ap, ADD, EQ, "P6 ap2 b322", "b3")
+    ts(T.b3[:], T.cb[:], b32, ap, ADD, EQ, "cb ap2 b322", "b3")
     mm(P[4][:, :, 0:6], i8, T.b3[:], False, False, "b3", "P4")
     tt(wv, ap, b32, SUB, "ap2 b322", "wv")
     ts(dv, ap, 31.0, None, ADD, None, "ap2", "dv")
@@ -479,25 +477,25 @@ def rank_program(g, core, T, topo):
         tt(out, P[5][:, :, d:6], m, MUL, "P5 Xm%d" % d, "Xv%d" % d)
         if d < 4:
             for s in range(4):
-                mm(P[0][:, s::4], T.X[:, d, 8 * s:8 * s + 8, :], idb, d == 0 and s == 0, d == 3 and s == 3,
-                   "Xv%d Xv4" % d, "P0")
+                mm(P[0][:, s::4], T.X[:, d, 8 * s:8 * s + 8, :], idb, d == 3 and s == 0, d == 0 and s == 3,
+                   "Xv0 Xv4 idb" if d == 0 else "Xv%d idb" % d, "P0")
 
+    mask(3)
+    mask(2)
+    value(3)
+    value(2)
+    mask(1)
     mask(4)
+    value(1)
+    cp(T.zf[:, 0:128], P[3][:, 0:128], "P3", "zf")
+    mms(P[6][:, 0:32], [(T.zf[:, 12 - 4 * m4:140 - 4 * m4], T.rmh[:, m4, :]) for m4 in range(4)], "zf rmh", "P6")
     mask(0)
     value(4)
     value(0)
-    mask(1)
-    mask(2)
-    value(1)
-    mask(3)
-    value(2)
-    cp(T.zf[:, 0:128], P[3][:, 0:128], "P3", "zf")
-    mms(P[6][:, 0:32], [(T.zf[:, 12 - 4 * m4:140 - 4 * m4], T.rmh[:, m4, :]) for m4 in range(4)], "zf rmh", "P6")
-    value(3)
     ts(T.o16[:], P[6][:, 0:32], float(L // 2), None, ADD, None, "P6", "o16")
     record(2)
     dma("Y", T.mg[:], T.mgs[0:1, 0:9], "dout", "a0 b0 c0 a1 b1 c1 a2 b2 c2", "")
-    for k in range(3):
+    for k in range(4):
         us = slice(16 * CUT[k + 1], 16 * CUT[k])
         act(T.xr[:, us], P[0][:, us], F.Copy, "P0", "xr%d" % k)
     mms(P[7][0:8, 0:1], [(ends(d, s), T.onb[:, 0:1]) for d in (T.d12, T.d3) for s in range(4)], "d12 d3 onb", "P7")
@@ -509,17 +507,23 @@ def rank_program(g, core, T, topo):
         tt(T.W[:, 16:16 + 96 * CUT[k] - 5].indirect(T.o16[:, CUT[k + 1]:CUT[k]]), T.xr[:, us], T.ucon[:, us], MUL,
            "o16 xr%d ucon W" % k, "Ws W%d" % k)
         c0, n = 6 * CUT[k + 1], 6 * (CUT[k] - CUT[k + 1])
-        mms(P[1 + k][:, 0:n], [(T.zsel[:, e + 5, :], T.W[:, 16 + e + 16 * c0:16 + e + 16 * (c0 + n) - 15:16])
-                               for e in range(-5, 16)], "zsel W%d" % k, "P%d" % (1 + k))
+        mms(P[SB[k]][:, 0:n], [(T.zsel[:, e + 5, :], T.W[:, 16 + e + 16 * c0:16 + e + 16 * (c0 + n) - 15:16])
+                               for e in range(-5, 16)], "zsel W%d" % k, "P%d" % SB[k])
 
     def places(k):
         c0, c1 = 6 * CUT[k + 1], 6 * CUT[k]
-        ts(T.j16[:, c0:c1], P[1 + k][:, 0:c1 - c0], 49152.0 - 15.5, 1.0 / 32, ADD, MUL, "P%d" % (1 + k), "j%d" % k)
+        if k == 0:
+            act(T.j16[:, c0:c1], P[SB[k]][:, 0:c1 - c0], F.Identity, "P%d" % SB[k], "j%d" % k, bias=(49152.0 - 15.5) / 32,
+                scale=1.0 / 32)
+        else:
+            ts(T.j16[:, c0:c1], P[SB[k]][:, 0:c1 - c0], 49152.0 - 15.5, 1.0 / 32, ADD, MUL, "P%d" % SB[k], "j%d" % k)
 
-    def symbols(k):
-        c0, c1 = 6 * CUT[k + 1], 6 * CUT[k]
-        ts(T.jt[:, c0:c1], T.j16[:, c0:c1], -32.0, 49151.0, MUL, ADD, "j%d" % k, "jt%d" % k)
-        tt(T.sy[:, c0:c1], P[1 + k][:, 0:c1 - c0], T.jt[:, c0:c1], ADD, "P%d jt%d" % (1 + k, k), "sy%d" % k)
+    def symbols(*ks):
+        c0, c1 = 6 * CUT[ks[1] + 1], 6 * CUT[ks[0]]
+        ts(T.jt[:, c0:c1], T.j16[:, c0:c1], -32.0, 49151.0, MUL, ADD, "j%d j%d" % ks, "jt%d" % ks[0])
+        for k in ks:
+            c0, c1 = 6 * CUT[k + 1], 6 * CUT[k]
+            tt(T.sy[:, c0:c1], P[SB[k]][:, 0:c1 - c0], T.jt[:, c0:c1], ADD, "P%d jt%d" % (SB[k], ks[0]), "sy%d" % k)
 
     YW = "Y0a Y0b Y0h Y0e"
 
@@ -531,30 +535,29 @@ def rank_program(g, core, T, topo):
             cp(T.Y[:, 16 * c0:16 * c1], src, YW + " j%d" % k, key)
         return lambda: dma(queue, T.y[:, 16 * c0:16 * c1], T.Y[:, 16 * c0:16 * c1], "dout", key, "")
 
-    scatter(0)
-    scatter(1)
+    for k in range(3):
+        scatter(k)
     places(0)
-    vectors("S", 0, 162, 192)()
-    vectors("S", 0, 132, 162)()
-    scatter(2)
+    vectors("S", 0, 156, 192)()
     places(1)
-    store = [vectors("S", 1, 110, 132), vectors("S", 1, 88, 110)]
-    symbols(0)
-    symbols(1)
-    vectors("V", 1, 72, 88)()
+    scatter(3)
+    store = vectors("S", 1, TS[0], 156)
+    vectors("V", 1, 108, TS[0])()
     places(2)
-    store[0]()
-    symbols(2)
-    store[1]()
-    store = [vectors("S", 2, 54, 72), vectors("S", 2, 40, 54, queue="S")]
+    symbols(0, 1)
+    store()
+    store = vectors("S", 2, TS[1], 108)
+    places(3)
+    vectors("V", 2, 48, TS[1])()
+    symbols(2, 3)
+    store()
+    store = vectors("S", 3, TS[2], 48, queue="S")
     for b in range(6):
-        op("V", lambda: g.vector.transpose(T.fsb[:, :, b, :], T.sy[:, b::6]), "sy0 sy1 sy2", "fsb%d" % b)
+        op("V", lambda: g.vector.transpose(T.fsb[:, :, b, :], T.sy[:, b::6]), "sy0 sy1 sy2 sy3", "fsb%d" % b)
     for k in range(2):
         dma("Y", T.fs[k::2, :], T.fsb[:, k, :, :], "dout", " ".join("fsb%d" % b for b in range(6)), "")
-    store[0]()
-    vectors("V", 2, 20, 40)()
-    store[1]()
-    vectors("V", 2, 0, 20)()
+    store()
+    vectors("V", 3, 0, TS[2])()
 
     for e in count:
         wait("G", "c" + e, count[e])

@@ -2,31 +2,34 @@ from concourse.bass import DstId, RemoteDMATransfer
 from concourse.mybir import AluOpType as A, AxisListType, ActivationFunctionType as F
 
 N, L, M, S0 = 6, 3072, 6144, 28
-HL, B = 4, 34
+HL, B, H = 4, 22, 1536
 BIG = 8388608.0
-WV = (860, 1312, 1680)
-GV = 96
-NPV = 21
-CUT = (32, 26, 18, 8, 0)
-TS = (124, 66, 16)
+WV = (880, 1280)
+GC = (0, 50, 98, 122, 128, 134, 192)
+NPV = (22, 21)
+DB = (14, 16, 19)
+CUT = (32, 26, 16, 8, 0)
+TS = (120, 66, 56, 28, 20, 10, 170)
 SB = (1, 2, 3, 6)
 HB = (2, 0)
 KB = (3, 6, 7)
 bf, f16, f32, i32, u16 = "bfloat16", "float16", "float32", "int32", "uint16"
 
 _SBUF = [
-    (i32, [192], "posi rint pce"), (i32, [2048], "win"), (i32, [4], "lei pint pnt2 cnt"), (i32, [8, 25], "wi wj"), (i32, [2, 72], "wm"),
-    (u16, [192], "r16 p16 j16"), (u16, [32], "o16"),
-    (bf, [M], "vew"), (bf, [512], "xr ucon"), (bf, [3088], "G W Y0"), (bf, [L], "Y"), (bf, [2, 400], "fz"),
-    (bf, [192], "i32c rst d12 b3 hsv d3"), (bf, [8, B], "S bn0 bn1 C1 C2 dd"), (bf, [8, 24], "inv g1 h1"),
-    (bf, [8, 25, 32], "OH"), (bf, [8, 25, 28 - NPV], "tab"), (bf, [400], "onb"), (bf, [8, 80], "mst"), (f16, [8, B], "cd"), (f16, [192], "cb"),
+    (i32, [192], "posi rint pce"), (i32, [2052], "win"), (i32, [4], "lei pint pnt2 cnt"), (i32, [16, 13], "wi wj"),
+    (i32, [2, 144], "wm"), (u16, [192], "r16 p16 j16"), (u16, [32], "o16"), (u16, [8 * N], "ld1"), (u16, [16 * N], "ld2"),
+    (bf, [M], "vew"), (bf, [512], "xr ucon"), (bf, [3088], "G W Y0"), (bf, [L], "Y"), (bf, [800], "fz"),
+    (bf, [192], "i32c rst rs12 d12 base b3 b3n hsv d3 c3"), (bf, [16, B], "S bn0 bn1 C1 C2 dd"), (bf, [16, 12], "inv g1 h1"),
+    (bf, [16, 13, 32], "OH"), (bf, [16, 13, 28 - min(NPV)], "tab"), (bf, [400], "onb"), (bf, [8, 80], "mst"),
     (bf, [8], "pk"), (bf, [8, 128], "dg"), (bf, [128], "tris trii ngb zeb"), (bf, [4, 32, 16], "X"), (bf, [8, 36], "zs"),
     (bf, [21, 128], "zsel"),
-    (f16, [144], "zf"), (f16, [4, 32], "rmh"), (f16, [128], "sumh"), (f16, [2, 32], "msg"), (f16, [2, N, 32], "land"),
-    (f32, [4], "lef kcol flb"), (f32, [8, 25], "fT"), (f32, [72], "fm"), (f32, [128], "onf rep idf yrev mrb mr mrt rvt ent en1 eqb zer"),
-    (f32, [192], "jl jt sy"), (f32, [4, 32], "rmm"), (f32, [8, 16], "sixu"), (f32, [512], "urow"),
-    (f32, [32], "xrow col nega k0t mlb ml mlt mlu cv enx r1 r2 row"), (f32, [64], "k0 ksb bc"),
-    (f32, [33], "c32 ne"), (f32, [16], "colk mL mR"), (f32, [12 * N], "ld1 ld2"),
+    (f16, [16, B], "cd"), (f16, [192], "cb cn"), (f16, [2, 144], "zf"), (f16, [4, 16], "rmh"), (f16, [128], "sumh"),
+    (f16, [2, 32], "msg"), (f16, [2, N, 32], "land"),
+    (f32, [4], "lef kcol flb par"), (f32, [16, 13], "fT"), (f32, [144], "fm"),
+    (f32, [128], "onf rep idf yrev mrb mr mrt rvt ent en1 eqb zer"),
+    (f32, [192], "jl jt sy"), (f32, [512], "urow"),
+    (f32, [32], "xrow col nega mlb ml mlt mlu cv enx r1 r2 row sixu"), (f32, [64], "k0 ksb bc rmm"),
+    (f32, [33], "c32 ne"), (f32, [16], "colk mL mR"),
     (f32, [3, 33], "run"), (f32, [64], "sc"), (f32, [12], "mgs"), (f32, [2, 6, 16], "fsb"),
 ]
 SCRATCH = {n: ("sbuf", [128] + s, d) for d, s, names in _SBUF for n in names.split()}
@@ -121,6 +124,12 @@ def rank_program(g, core, T, topo):
     def sel(out, a, pat, cmp, base, cm, r, w):
         op("G", lambda: g.affine_select(out, a, pat, cmp, 0.0, base, cm), r, w)
 
+    def put(out, a, pat, base, cm, val, r, w):
+        op("G", lambda: g.affine_select(out, a, pat, A.not_equal, val, base, cm), r, w)
+
+    def fill(out, n, c, w):
+        act(out, T.onb[:, 0:n], F.Identity, "onb onb2" if n > 128 else "onb", w, bias=c, scale=0.0)
+
     ndma = {}
 
     def dma(e, out, a, sem, r, w):
@@ -139,127 +148,132 @@ def rank_program(g, core, T, topo):
 
     def send(src, dst, sem, r):
         order("G", r.split(), [])
-        trs = []
         for peers, engs in ((far, far_eng), (near, near_eng)):
             ids = [DstId(rid=topo.addr(T.cores[p])[0], pnc=topo.addr(T.cores[p])[1]) for p in peers]
-            trs.append(RemoteDMATransfer(dst_ids=ids, dma_engine_mask=sum(1 << e for e in engs), remote_sem=T.sem[sem],
-                                         srcs=[src], dsts=[dst] * len(peers)))
+            g.remote_dma_fused([RemoteDMATransfer(dst_ids=ids, dma_engine_mask=sum(1 << e for e in engs), remote_sem=T.sem[sem],
+                                                  srcs=[src], dsts=[dst] * len(peers))], local_sem=T.sem.sent)
             nsent[0] += len(engs)
-        g.remote_dma_fused(trs, local_sem=T.sem.sent)
 
     arrive = len(far) * len(far_eng) + len(near) * len(near_eng)
     P = [T["P%d" % k] for k in range(8)]
     EQ, ADD, SUB, MUL, MAX = A.is_equal, A.add, A.subtract, A.mult, A.max
     idb, idn, idm, i29, i30, i8, iL, iR = (T.dg[:, k, :] for k in range(8))
-    own = slice(HL, HL + 24)
+    own = slice(HL, HL + 12)
+    half = (slice(0, 8), slice(8, 16))
 
     dma("Y", T.posi[:], T.pos[:], "dpos", "", "posi")
     dma("S", T.lei[0:8, 0:1], T.le[:], "dle", "", "lei")
-    def fill(out, n, c, w):
-        act(out, T.onb[:, 0:n], F.Identity, "onb", w, bias=c, scale=0.0)
-
-    ms(T.onb[:], 1.0, "onb")
+    ms(T.onb[:, 0:128], 1.0, "onb")
     ms(T.win[:, 0:WV[0]], 0, "win0")
     iota(T.win[:, WV[0]:WV[1]], [[0, WV[1] - WV[0]]], 0, 0, "win1", False)
-    fill(T.win[:, WV[1]:WV[2]], WV[2] - WV[1], 0.0, "win2")
-    fill(T.win[:, WV[2]:2048], 2048 - WV[2], 0.0, "win3")
-    order("Y", [], ["win0", "win1", "win2", "win3"])
-    order("S", [], ["win0", "win1", "win2", "win3"])
+    for c0 in range(WV[1], 2048, 128):
+        fill(T.win[:, c0:c0 + 128], 128, 0.0, "win%d" % c0)
+    ms(T.onb[:, 128:400], 1.0, "onb2")
+    ms(T.onf[:], 1.0, "onf")
+    order("Y", [], ["win0", "win1", "win1920"])
+    order("S", [], ["win0", "win1", "win1920"])
     for k in range(3):
-        dma("YSY"[k], T.win[k::16, :], T.st[:, 2048 * k:2048 * k + 2048], "dst", "", "win" if k == 2 else "")
+        dma("YSY"[k], T.win[k::16, 0:2048], T.st[:, 2048 * k:2048 * k + 2048], "dst", "", "win" if k == 2 else "")
     dma("Y", T.vew[:], T.ve[:], "dve", "posi win", "vew")
 
-    ms(T.onf[:], 1.0, "onf")
     ms(T.mst[:], 0.0, "mst")
-    ms(T.msg[:], 0.0, "msg")
-    ms(T.zf[:], 0.0, "zf")
-    ms(T.pk[:], 0.0, "pk")
-    for k in range(2):
-        fill(T.fz[:, k, :], 400, 0.0, "fz_ fz" if k else "fz_")
+    fill(T.fz[:, 0:400], 400, 0.0, "fz_")
+    fill(T.fz[:, 400:800], 400, 0.0, "fz")
+    fill(T.win[:, 2048:2052], 4, -1.0, "wend")
+    fill(T.pk[:], 8, 0.0, "pk")
     fill(T.G[:, 0:16], 16, 0.0, "Gl")
     fill(T.G[:, 3072:3088], 16, 0.0, "G")
-    fill(T.ngb[:], 128, -1.0, "ngb")
-    fill(T.sixu[:], 128, 0.0, "sixu")
-    iota(T.pint[:, 0:1], [[0, 1]], 0, 1, "pint", False)
     iota(T.kcol[:, 0:1], [[0, 1]], 0, 16, "kcol")
-    sel(T.rep[:], T.onf[:], [[-1, 8], [0, 16]], EQ, 0, 1, "onf", "rep")
     iota(T.jl[:], [[16, 192]], 0, 1, "jl")
+    sel(T.rep[0:8, :], T.onf[0:8, :], [[-1, 8], [0, 16]], EQ, 0, 1, "onf", "rep")
     sel(T.mst[:, :, 32:48], T.onb[:, 0:128], [[-16, 8], [-1, 16]], EQ, 0, 1, "onb", "mst")
     for k in range(3):
-        op("G", lambda: g.affine_select(T.pk[:], T.pk[:], [[-16, 8]], A.not_equal, 64.0 ** k, -k, 1), "pk", "pk")
+        put(T.pk[:], T.pk[:], [[-16, 8]], -k, 1, 64.0 ** k, "pk", "pk")
+    iota(T.pint[:, 0:1], [[0, 1]], 0, 1, "pint", False)
+    iota(T.OH[:, :, :, 28:32], [[0, 832]], 0, 0, "OH28 OH290 OH291 OH300 OH301")
     iota(T.yrev[:], [[0, 4], [-1, 32]], 31, 0, "yrev")
     iota(T.xrow[:], [[1, 32]], 0, 0, "xrow")
-    sel(T.idf[:], T.onf[:], [[-1, 128]], EQ, 0, 1, "onf", "idf")
     sel(idb, T.onb[:, 0:128], [[-1, 128]], EQ, 0, 1, "onb", "idb")
-    sel(T.tris[:], T.ngb[:], [[1, 128]], A.is_gt, 0, -1, "ngb", "tris")
-    sel(T.trii[:], T.ngb[:], [[1, 128]], A.is_ge, 0, -1, "ngb", "trii")
-    sel(T.rmm[:], T.onf[:], [[-1, 4], [-4, 32]], EQ, 0, 1, "onf", "rmm")
-    iota(T.sixu[:, :, 12:16], [[0, 8], [6, 4]], -L // 2, 24, "sixu")
-    iota(T.i32c[:], [[0, 32], [32, 6]], 0, 0, "i32c")
-    iota(T.urow[:, 0:256], [[1, 256]], -256, 0, "urow0")
-    iota(T.urow[:, 256:512], [[1, 256]], 1, 0, "urow1")
-    zc, kc, z28, le28, isE, isV, yc, e1, e2, e3 = (T.col[:, k:k + 1] for k in range(10))
+    iota(T.k0[:, 0:28], [[-1, 28]], 31 + 32 * 4 * 2 * N * (L // 2), 0, "k0a")
+    iota(T.k0[:, 28:32], [[-1, 4]], 3, 0, "k0b")
+    iota(T.k0[:, 32:64], [[0, 32]], 0, 0, "k0c")
+    for k in range(4):
+        put(T.k0[:, 0:32], T.k0[:, 0:32], [[1, 32]], -31 - 32 * k, 1, -BIG, "k0a k0b k0", "k0")
+    zc, kc, z28, le28, isE, isV, e1, e2, e3 = (T.col[:, k:k + 1] for k in range(9))
+
+    def symbol_gather(e, k):
+        c0, c1 = GC[k], GC[k + 1]
+        out, src = T.G[:, HL + 16 * c0:HL + 16 * c1], T.win[:].indirect(T.r16[:, c0:c1])
+        keys = "win wend " + ("r16" if k < 2 else "r16b")
+        if e == "S":
+            act(out, src, F.Identity, keys + " G", "G%d" % k, bias=1.0)
+        else:
+            ts(out, src, 1.0, None, ADD, None, keys + " Gl", "G%d" % k)
 
     tt(T.lef[0:8, 0:1], T.lei[0:8, 0:1], T.kcol[0:8, 0:1], ADD, "lei kcol", "lef")
     mm(P[7][:, 256:257], T.rep[0:8, :], T.lef[0:8, 0:1], True, True, "rep lef", "P7")
-    ts(T.rint[:], T.posi[:], 2047, None, A.bitwise_and, None, "posi", "rint")
     ts(T.pce[:], T.posi[:], -3071.5, 1.0 / 2048, ADD, MUL, "posi", "pce")
-    cp(T.r16[:], T.rint[:], "rint", "r16")
-    act(T.G[:, HL + 16 * GV:HL + L], T.win[:].indirect(T.r16[:, GV:192]), F.Identity, "win r16 G", "GS", bias=1.0)
+    ts(T.rint[:], T.posi[:], 2047, None, A.bitwise_and, None, "posi", "rint")
     for x in range(3):
-        ts(T.fz[:, 0, 6 + x:6 + x + 384:6], T.pce[:, x::3], -63.0 / 64, -63.0 / 4096, MUL, MAX, "pce fz", "fz%d" % x)
-    for x in range(3):
-        ts(T.fz[:, 1, 6 + x:6 + x + 384:6], T.jl[:, x::3], P[7][:, 256:257], -2.0, A.is_ge, MUL, "jl P7 fz", "fv%d" % x)
-    ts(T.G[:, HL:HL + 16 * GV], T.win[:].indirect(T.r16[:, 0:GV]), 1.0, None, ADD, None, "win r16 Gl", "GV")
+        ts(T.fz[:, 12 + x:780:12], T.pce[:, x::3], -63.0 / 64, -63.0 / 4096, MUL, MAX, "pce fz_ fz", "fz%d" % x)
+    ts(T.jt[:, 0:98], T.jl[:, 0:98], P[7][:, 256:257], 2048.0, A.is_ge, MUL, "jl P7", "out")
+    ts(T.jt[:, 98:192], T.jl[:, 98:192], P[7][:, 256:257], 2048.0, A.is_ge, MUL, "jl P7", "outb")
+    tt(T.r16[:, 0:98], T.rint[:, 0:98], T.jt[:, 0:98], MAX, "rint out", "r16")
+    symbol_gather("S", 1)
+    tt(T.r16[:, 98:192], T.rint[:, 98:192], T.jt[:, 98:192], MAX, "rint outb", "r16b")
+    symbol_gather("V", 0)
 
-    def f_terms(pairs, b0, n):
-        return [(T.fz[:, k, 6 + 6 * (x // 3) + x % 3 - 3 * rho:388 + 6 * (x // 3) + x % 3 - 3 * rho:3],
-                 T.mst[:, :, 32 - HL + 24 * rho - 16 * x + b0:32 - HL + 24 * rho - 16 * x + b0 + n])
-                for rho, x in pairs for k in range(2)]
+    def f_turn(out, h, b0, n, bank):
+        terms = []
+        for rho in range(4):
+            for x in range((12 * rho + b0 - HL) // 16, (12 * rho + b0 + n - 1 - HL) // 16 + 1):
+                a0, c0 = 12 + 384 * h + 12 * (x // 3) + x % 3 - 3 * rho, 32 - HL + 12 * rho - 16 * x + b0
+                terms.append((T.fz[:, a0:a0 + 382:3], T.mst[:, :, c0:c0 + n]))
+        mms(out, terms, "fz0 fz1 fz2 mst", bank)
 
-    FZ = "fz0 fz1 fz2 fv0 fv1 fv2 mst"
-    mms(P[7][:, 0:200], f_terms(((0, 0), (0, 1), (1, 1), (1, 2), (1, 3)), 4, 25), FZ, "P7")
-    mms(P[7][:, 200:232], f_terms(((0, -1), (1, 1)), 0, 4), FZ, "P7")
-    mms(P[7][:, 232:272], f_terms(((0, 1), (1, 3)), 29, 5), FZ, "P7")
-    act(T.fT[:], P[7][:, 0:200], F.Relu, "P7", "fT", bias=1.0 / 64)
-    act(T.fm[:], P[7][:, 200:272], F.Relu, "P7", "fm", bias=1.0 / 64)
-    for k in range(2):
-        fill(T.OH[:, 4 * k:4 * k + 4, :, 28:32], 400, 0.0, "OH_ OH28 OH290 OH291 OH300 OH301" if k else "OH_")
-    HALF = (slice(0, 13), slice(13, 25))
-    for b in list(range(4, 29)) + list(range(4)) + list(range(29, B)):
-        bank = 3 if b < 4 or b >= 29 else 4 if b < 17 else 5
-        out = P[bank][:, 0:8, (b - 4) % 13] if bank > 3 else P[3][:, b:32:4] if b < 4 else P[3][:, b + 3:72:5]
-        mm(out, T.G[:, b:b + 3049:24], T.pk[:], True, True, "GV GS pk", "P%d" % bank)
-    ts(T.pnt2[:, 0:1], T.pint[:, 0:1], 31, None, A.bitwise_and, None, "pint", "pa")
-    ts(T.pnt2[:, 1:2], T.pint[:, 0:1], 5, None, A.arith_shift_right, None, "pint", "pb")
-    ts(T.pnt2[:, 2:3], T.pint[:, 0:1], 15, None, A.bitwise_and, None, "pint", "pc")
-    ms(T.k0[:], 0.0, "k0")
-    cp(T.col[:, 0:2], T.pnt2[:, 0:2], "pa pb", "zc")
-    ts(idn, idb, -1.0, None, MUL, None, "idb", "idn")
-    ts(idm, idb, -1.0 / 32, None, MUL, None, "idb", "idm")
-    ts(yc, zc, -1.0, 31.0, MUL, ADD, "zc", "yc")
-    ts(T.sumh[:], T.yrev[:], zc, 32.0, EQ, MUL, "yrev zc", "sumh")
-    ts(T.k0t[:], T.xrow[:], yc, -BIG, EQ, MUL, "xrow yc", "k0t")
-    SH = (T.S[:, :, HL:HL + 13], T.S[:, :, HL + 13:HL + 25])
-    digit = [[lambda h=h: tt(T.wi[:, :, HALF[h]], P[4 + h][:, 0:8, 0:13 - h], T.fT[:, :, HALF[h]], MUL, "P%d fT" % (4 + h), "wi%d" % h),
-              lambda h=h: ts(T.wj[:, :, HALF[h]], T.wi[:, :, HALF[h]], 63, None, A.bitwise_and, None, "wi%d" % h, "wj%d" % h),
-              lambda h=h: cp(SH[h], T.wj[:, :, HALF[h]], "wj%d" % h, "S%d" % h)] for h in range(2)]
-    for step in digit[0] + digit[1][:1]:
-        step()
+    def s_turn(out, h, b, bank):
+        mm(out, T.G[:, H * h + b:H * h + b + 1525:12], T.pk[:], True, True, ("G0 G1 pk", "G1 G2 G3 G4 G5 pk")[h], bank)
 
     for h in range(2):
-        for x in range(NPV, 28):
-            act(T.tab[:, :, HALF[h], x - NPV], T.wj[:, :, HALF[h]], F.Abs, "wj%d" % h, "tab%d_%d" % (h, x), bias=-float(x + 1))
-        act(T.OH[:, :, HALF[h], NPV:28], T.tab[:, :, HALF[h], :], F.Relu,
-            " ".join("tab%d_%d" % (h, x) for x in range(NPV, 28)), "OHs%d" % h, bias=1.0, scale=-1.0)
-        for x in range(NPV):
-            ts(T.OH[:, :, HALF[h], x], SH[h], float(x + 1), None, EQ, None, "S%d" % h, "OHv%d_%d" % (h, x))
-            if h == 0 and x in (1, 4):
-                digit[1][1 + x // 4]()
+        f_turn(P[7][:, 104 * h:104 * h + 104], h, HL, 13, "P7")
+    for b in range(13):
+        s_turn(P[4][:, 0:8, b], 0, HL + b, "P4")
+    act(T.fT[:], P[7][:, 0:208], F.Identity, "P7", "fT0 fT1", bias=1.0 / 64)
+    symbol_gather("S", 5)
+    for h in range(2):
+        f_turn(P[6][:, 32 * h:32 * h + 32], h, 0, 4, "P6")
+        f_turn(P[6][:, 64 + 40 * h:104 + 40 * h], h, 17, 5, "P6")
+    digit = [[lambda h=h: tt(T.wi[:, half[h], :], P[4 + h][:, 0:8, 0:13], T.fT[:, half[h], :], MUL, "P%d fT%d" % (4 + h, h), "wi%d" % h),
+              lambda h=h: ts(T.wj[:, half[h], :], T.wi[:, half[h], :], 63, None, A.bitwise_and, None, "wi%d" % h, "wj%d" % h),
+              lambda h=h: cp(T.S[:, half[h], HL:HL + 13], T.wj[:, half[h], :], "wj%d" % h, "S%d" % h)] for h in range(2)]
+    for k in range(3):
+        symbol_gather("V", 2 + k)
+        digit[0][k]()
+    for b in range(13):
+        s_turn(P[5][:, 0:8, b], 1, HL + b, "P5")
+    for h in range(2):
+        for b in list(range(4)) + list(range(17, B)):
+            out = P[3][:, 32 * h + b:32 * h + 32:4] if b < 4 else P[3][:, 47 + 40 * h + b:104 + 40 * h:5]
+            mm(out, T.G[:, H * h + b:H * h + b + 1525:12], T.pk[:], True, True, "G0 G1 G2 G3 G4 G5 pk", "P3")
+    ts(T.pnt2[:, 0:1], T.pint[:, 0:1], 31, None, A.bitwise_and, None, "pint", "pa")
+    ts(T.pnt2[:, 1:2], T.pint[:, 0:1], 5, None, A.arith_shift_right, None, "pint", "pb")
+
+    for h in range(2):
+        n = NPV[h]
+        for x in range(n):
+            ts(T.OH[:, half[h], :, x], T.S[:, half[h], HL:HL + 13], float(x + 1), None, EQ, None, "S%d" % h, "OHv%d_%d" % (h, x))
+            if h == 0 and x in DB:
+                digit[1][DB.index(x)]()
+        for x in range(n, 28):
+            act(T.tab[:, half[h], :, x - n], T.wj[:, half[h], :], F.Abs, "wj%d" % h, "tab%d_%d" % (h, x), bias=-float(x + 1))
+        for x0, x1 in ((n, 25), (25, 28)):
+            act(T.OH[:, half[h], :, x0:x1], T.tab[:, half[h], :, x0 - n:x1 - n], F.Relu,
+                " ".join("tab%d_%d" % (h, x) for x in range(x0, x1)), "OHs%d" % h if x1 == 28 else "", bias=1.0, scale=-1.0)
         for q in range(24):
-            gg, b0 = q // 3, 12 * h + 4 * (q % 3)
-            mm(P[HB[h]][:, 0:112], T.OH[:, gg, b0 + 1:b0 + 5, :], T.OH[:, gg, b0:b0 + 4, 0:28], q == 0, q == 23,
-               "OHs%d OHv%d_%d OH28" % (h, h, NPV - 1), "P%d" % HB[h])
+            row, b0 = 8 * h + q // 3, 4 * (q % 3)
+            mm(P[HB[h]][:, 0:112], T.OH[:, row, b0 + 1:b0 + 5, :], T.OH[:, row, b0:b0 + 4, 0:28], q == 0, q == 23,
+               "OHs%d OHv%d_%d OH28" % (h, h, n - 1), "P%d" % HB[h])
+    act(T.fm[:], P[6][:, 0:144], F.Identity, "P6", "fm", bias=1.0 / 64)
 
     def code_of(out, prev, cur, r, w):
         mms(out, [(idn, prev)] + [(idm, c) for c in cur], r + " idn idm", w)
@@ -267,73 +281,82 @@ def rank_program(g, core, T, topo):
     def counts(h):
         for k in range(4):
             ts(T.msg[32 * k:32 * k + 32, h, 0:28], P[HB[h]][32 * k:32 * k + 32, 28 * k:28 * k + 28], -float(L // 2), None,
-               ADD, None, "P%d msg" % HB[h], "msg%d%d" % (h, k))
+               ADD, None, "P%d" % HB[h], "msg%d%d" % (h, k))
         keys = " ".join("msg%d%d" % (h, k) for k in range(4))
-        send(T.msg[:, h, :], T.land[:, h, rank, :], "ar0" if h == 0 else "a%d" % rank, keys)
+        send(T.msg[:, h, 0:28], T.land[:, h, rank, 0:28], "ar0" if h == 0 else "a%d" % rank, keys)
         return keys
 
     MSG0 = counts(0)
-    tt(T.wm[:, 0, :], P[3][:, 0:72], T.fm[:], MUL, "P3 fm", "wih")
-    ts(T.colk[:], T.xrow[:, 0:16], kc, None, SUB, None, "xrow zc", "colk")
+    cp(T.col[:, 0:2], T.pnt2[:, 0:2], "pa pb", "zc")
+    tt(T.wm[:, 0, :], P[3][:, 0:144], T.fm[:], MUL, "P3 fm", "wih")
+    ts(idn, idb, -1.0, None, MUL, None, "idb", "idn")
+    ts(idm, idb, -1.0 / 32, None, MUL, None, "idb", "idm")
     ts(T.wm[:, 1, :], T.wm[:, 0, :], 63, None, A.bitwise_and, None, "wih", "wjh")
-    ts(T.mL[:], T.colk[:], 4.0, None, EQ, None, "colk", "mL")
-    cp(T.S[:, :, 0:4], T.wm[:, 1, 0:32], "wjh", "Sl")
-    cp(T.S[:, :, 29:B], T.wm[:, 1, 32:72], "wjh", "Sr")
-    tt(T.k0[:, 0:32], T.k0t[:], T.yrev[:, 0:32], ADD, "k0t yrev", "k0")
-    cp(T.p16[:], T.posi[:], "posi", "p16")
-    ts(T.k0[:, 0:28], T.k0[:, 0:28], 32.0 * 4 * 2 * N * (L // 2), None, ADD, None, "k0", "k0")
-    ts(T.mR[:], T.colk[:], 1.0, None, EQ, None, "colk", "mR")
+    ts(T.sumh[:], T.yrev[:], zc, 32.0, EQ, MUL, "yrev zc", "sumh")
+    cp(T.S[:, :, 0:4], T.wm[:, 1, 0:64], "wjh", "Sl")
+    cp(T.S[:, :, 17:B], T.wm[:, 1, 64:144], "wjh", "Sr")
     ms(T.zeb[:], 0.0, "zeb")
     ms(T.zer[:], 0.0, "zer")
     MSG1 = counts(1)
-    act(T.W[:], T.G[:], F.Identity, "GV GS", "W", bias=0.0, scale=0.0)
+    cp(T.p16[:], T.posi[:], "posi", "p16")
+    fill(T.ngb[:], 128, -1.0, "ngb")
+    act(T.W[:], T.G[:], F.Identity, "G0 G1 G2 G3 G4 G5", "W", bias=0.0, scale=0.0)
     act(T.Y0[:, 0:1536], T.vew[:].indirect(T.p16[:, 0:96]), F.Copy, "vew p16", "Y0a")
     act(T.Y0[:, 1542:3078], T.vew[:].indirect(T.p16[:, 96:192]), F.Copy, "vew p16", "Y0b")
-    act(T.X[:], T.G[:, 0:2048], F.Identity, "GV GS", "X", bias=0.0, scale=0.0)
+    act(T.X[:], T.G[:, 0:2048], F.Identity, "G0 G1 G2 G3 G4 G5", "X", bias=0.0, scale=0.0)
     K = [P[k][:, 0:32] for k in KB]
     KW = [P[k][:, 0:64] for k in KB]
-    mm(KW[0], T.idf[:], T.k0[:], True, False, "idf k0", "P3")
-    code_of(P[1][:, 0:264], T.S[:, :, 0:33], [T.S[:, :, 1:34]], "S0 S1 Sl Sr", "P1")
-    mms(K[0], [(T.sumh[:], T.msg[:, h, :]) for h in range(2)], "sumh %s %s" % (MSG0, MSG1), "P3", False, False)
+    sel(T.idf[:], T.onf[:], [[-1, 128]], EQ, 0, 1, "onf", "idf")
+    code_of(P[1][:, 0:336], T.S[:, :, 0:B - 1], [T.S[:, :, 1:B]], "S0 S1 Sl Sr", "P1")
+    mm(KW[0], T.idf[:], T.k0[:], True, False, "idf k0 k0c", "P3")
+    K28 = P[KB[0]][:, 0:28]
+    mms(K28, [(T.sumh[:], T.msg[:, h, 0:28]) for h in range(2)], "sumh %s %s" % (MSG0, MSG1), "P3", False, False)
     wait("P", "ar0", arrive)
-    mms(K[0], [(T.sumh[:], T.land[:, 0, r, :]) for r in others], "sumh", "P3", False, False)
+    mms(K28, [(T.sumh[:], T.land[:, 0, r, 0:28]) for r in others], "sumh", "P3", False, False)
     for n, r in enumerate(near + far):
         wait("P", "a%d" % r, len(near_eng) if r in near else len(far_eng))
-        mm(K[0], T.sumh[:], T.land[:, 1, r, :], False, n == N - 2, "sumh", "P3")
-
-    def put(out, a, pat, base, cm, val, r, w):
-        op("G", lambda: g.affine_select(out, a, pat, A.not_equal, val, base, cm), r, w)
+        mm(K28, T.sumh[:], T.land[:, 1, r, 0:28], False, n == N - 2, "sumh", "P3")
 
     ms(T.c32[:], 1.0 / 32, "c32")
     ms(T.ne[:], 1.0, "ne")
-    ms(T.zs[:], 0.0, "zs")
-    cp(T.cd[:, :, 1:B], P[1][:, 0:264], "P1", "cd")
+    ms(T.ld2[:], 0, "ld")
+    cp(T.cd[:, :, 1:B], P[1][:, 0:336], "P1", "cd")
+    ts(T.colk[:], T.xrow[:, 0:16], kc, None, SUB, None, "xrow zc", "colk")
     ts(le28, zc, 28.5, None, A.is_lt, None, "zc", "le28")
     ts(z28, zc, 28.0, None, EQ, None, "zc", "z28")
-    ts(e1, T.pnt2[:, 2:3], 5.5, None, A.is_gt, None, "pc", "e1")
-    ts(e2, T.pnt2[:, 2:3], 12.5, None, SUB, None, "pc", "e2")
     ts(T.sc[:, 5:6], zc, 29.0, None, EQ, None, "zc", "selz")
+    ts(T.mL[:], T.colk[:], 4.0, None, EQ, None, "colk", "mL")
+    ts(T.mR[:], T.colk[:], 1.0, None, EQ, None, "colk", "mR")
     ts(T.mlb[:], T.xrow[:], zc, le28, EQ, MUL, "xrow zc le28", "mlb")
     ts(T.mrb[:], T.sumh[:], le28, None, MUL, None, "sumh le28", "mrb")
-    ts(e3, e2, e2, 0.5, MUL, A.is_gt, "e2", "e3")
     ts(T.enx[:], T.xrow[:], float(S0), None, EQ, None, "xrow", "enx")
-    ts(T.inv[:], T.S[:, :, own], 0.0, 8.0, EQ, MUL, "S0 S1", "inv")
-    tt(isE, e1, e3, MUL, "e1 e3", "isE")
-    cp(T.rmh[:], T.rmm[:], "rmm", "rmh")
-    ts(isV, isE, -1.0, 1.0, MUL, ADD, "isE", "isV")
+    ms(T.zs[:], 0.0, "zs")
     put(T.ent[:], T.zer[:], [[0, 4], [-1, 32]], 31 - S0, 0, 32.0, "zer", "ent")
     put(i29, T.zeb[:], [[-1, 128]], 0, 1, 29.0, "zeb", "i29")
+    iota(T.sixu[:], [[H, 2], [6, 2], [0, 8]], -L // 2, 12, "sixu")
+    iota(T.i32c[:], [[0, 32], [32, 6]], 0, 0, "i32c")
     put(T.en1[:], T.zer[:], [[0, 4], [-1, 32]], 30 - S0, 0, 32.0, "zer", "en1")
     put(i30, T.zeb[:], [[-1, 128]], 0, 1, 30.0, "zeb", "i30")
-    put(i8, T.zeb[:], [[-1, 128]], 0, 1, 8.0, "zeb", "i8")
-    iota(T.Y0[:, 1536:1542], [[0, 6]], 0, 0, "Y0h")
-    iota(T.Y0[:, 3078:3088], [[0, 10]], 0, 0, "Y0e")
-    for lane, n, val in ((0, 6, 1.0), (6, 6, 192.0), (12, 2, 1.0), (14, 2, 192.0)):
-        put(T.zs[:, :, 15:15 + n], T.zs[:, :, 15:15 + n], [[-16, 8], [-1, n]], -lane, 1, val, "zs", "zs")
-    sel(T.rst[:], T.onb[:, 0:192], [[0, 32], [1, 6]], A.is_gt, 0, 0, "onb", "rst")
-    for e in range(-5, 16):
-        act(T.zsel[:, e + 5, :], T.zs[:, :, 15 - e:31 - e], F.Copy, "zs", "zsel" if e == 15 else "zsel%d" % e)
-    act(T.ucon[:], T.urow[:], F.Identity, "urow0 urow1 isE isV", "ucon", bias=isV, scale=isE)
+    sel(T.rst[:], T.onb[:, 0:192], [[0, 32], [1, 6]], A.is_gt, 0, 0, "onb onb2", "rst")
+
+    def constants_of_the_compaction():
+        for lane, n, val in ((0, 6, 1.0), (6, 6, 192.0), (12, 2, 1.0), (14, 2, 192.0)):
+            put(T.zs[:, :, 15:15 + n], T.zs[:, :, 15:15 + n], [[-16, 8], [-1, n]], -lane, 1, val, "zs", "zs")
+        put(i8, T.zeb[:], [[-1, 128]], 0, 1, 8.0, "zeb", "i8")
+        sel(T.tris[:], T.ngb[:], [[1, 128]], A.is_gt, 0, -1, "ngb", "tris")
+        sel(T.trii[:], T.ngb[:], [[1, 128]], A.is_ge, 0, -1, "ngb", "trii")
+        sel(T.rs12[:], T.onb[:, 0:192], [[0, 16], [1, 12]], A.is_gt, 0, 0, "onb onb2", "rs12")
+        sel(T.rmm[:], T.onf[:, 0:64], [[-2, 4], [-8, 16]], A.is_ge, 0, 1, "onf", "rmm")
+        sel(T.rmm[:], T.rmm[:], [[2, 4], [8, 16]], A.is_ge, 1, -1, "rmm", "rmm")
+        for e in range(-5, 16):
+            act(T.zsel[:, e + 5, :], T.zs[:, :, 15 - e:31 - e], F.Copy, "zs", "zsel" if e == 15 else "zsel%d" % e)
+        act(T.rmh[:], T.rmm[:], F.Copy, "rmm", "rmh")
+
+    def constants_of_the_scatter():
+        iota(T.urow[:, 0:256], [[1, 256]], -256, 0, "urow0")
+        iota(T.urow[:, 256:512], [[1, 256]], 1, 0, "urow1")
+        iota(T.Y0[:, 1536:1542], [[0, 6]], 0, 0, "Y0h")
+        iota(T.Y0[:, 3078:3088], [[0, 10]], 0, 0, "Y0e")
 
     def sc(t, k):
         return T.sc[:, 16 * t + k:16 * t + k + 1]
@@ -342,9 +365,14 @@ def rank_program(g, core, T, topo):
         scan(T.bc[:], KW[t], T.zer[:, 0:64], MAX, ADD, "P%d zer" % KB[t], "bc")
         op("V", lambda: g.vector.transpose(T.row[:], T.bc[:, 32:64]), "bc", "row")
         red(sc(t, 1), T.row[:], MAX, "row", "gm")
-        ts(T.cnt[:, t:t + 1], sc(t, 1), 16.5, 1.0 / 32, ADD, MUL, "gm", "cnt")
+        if t < 2:
+            ts(T.cnt[:, t:t + 1], sc(t, 1), 16.5, 1.0 / 32, ADD, MUL, "gm", "cnt")
+        else:
+            act(T.cnt[:, t:t + 1], sc(t, 1), F.Identity, "gm", "cnt", bias=16.5 / 32, scale=1.0 / 32)
+            act(sc(t, 2), T.cnt[:, t:t + 1], F.Identity, "cnt gm", "ap%d" % t, bias=sc(t, 1), scale=-32.0)
         ts(T.ne[:, 0:32], T.row[:], sc(t, 1), None, A.not_equal, None, "row gm", "ne")
-        ts(sc(t, 2), T.cnt[:, t:t + 1], -32.0, sc(t, 1), MUL, ADD, "cnt gm", "ap%d" % t)
+        if t < 2:
+            ts(sc(t, 2), T.cnt[:, t:t + 1], -32.0, sc(t, 1), MUL, ADD, "cnt gm", "ap%d" % t)
         scan(T.run[:, t, :], T.c32[:], T.ne[:], ADD, MUL, "c32 ne", "b32%d" % t)
         return sc(t, 2), T.run[:, t, 32:33]
 
@@ -354,15 +382,13 @@ def rank_program(g, core, T, topo):
         ts(T.mgs[:, 3 * t + 2:3 * t + 3], T.cnt[:, t:t + 1], -1.0, None, ADD, None, "cnt", "c%d" % t)
 
     def bun(src, c0, s):
-        return src[:, :, c0 + 6 * s:c0 + 6 * s + 6]
+        return src[:, half[s // 2], c0 + 6 * (s % 2):c0 + 6 * (s % 2) + 6]
 
     def ends(src, s):
         return src[:, 48 * s + 5:48 * s + 48:6]
 
-    def firsts(src, key, stop):
-        for s in range(4):
-            mms(P[3][:, 12 + s:128:16], [(T.trii[:] if s2 < s else T.tris[:], ends(src, s2)) for s2 in range(4)],
-                "trii tris " + key, "P3", False, stop and s == 3)
+    def first_of(s):
+        return P[3][:, 8 * s:8 * s + 8]
 
     def bundles(bank, terms, r):
         for lhsT, src, c0 in terms:
@@ -376,17 +402,17 @@ def rank_program(g, core, T, topo):
         bn, lo, hi = (T.bn0, 1, B) if t == 0 else (T.bn1, 2, B - 1)
         bk, kb, nb = "bn%d0 bn%d1" % (t, t), "P%d" % KB[t], "P%d" % KB[t + 1]
         for h in range(2):
-            gs, bh, won = slice(4 * h, 4 * h + 4), "bn%d%d" % (t, h), "cd ap%d b32%d" % (t, t)
+            gs, bh, won = half[h], "bn%d%d" % (t, h), "cd ap%d b32%d" % (t, t)
             ts(bn[:, gs, lo:hi], T.cd[:, gs, lo:hi], b32, ap, ADD, EQ, won, bh)
-            ts(T.OH[:, gs, 0:24, 29], T.cd[:, gs, own], b32, ap, ADD, EQ, won, "OH29%d" % h)
+            ts(T.OH[:, gs, 0:12, 29], T.cd[:, gs, own], b32, ap, ADD, EQ, won, "OH29%d" % h)
             if t == 1:
-                ts(T.OH[:, gs, 0:24, 30], T.cd[:, gs, HL - 1:HL + 23], b32, ap, ADD, EQ, won, "OH30%d" % h)
-            mms(P[4][:, 0, 0:9], [(T.OH[:, q // 6, 4 * (q % 6):4 * (q % 6) + 4, :], bn[:, q // 6, 4 * (q % 6) + 2:4 * (q % 6) + 11])
+                ts(T.OH[:, gs, 0:12, 30], T.cd[:, gs, HL - 1:HL + 11], b32, ap, ADD, EQ, won, "OH30%d" % h)
+            mms(P[4][:, 0, 0:9], [(T.OH[:, q // 3, 4 * (q % 3):4 * (q % 3) + 4, :], bn[:, q // 3, 4 * (q % 3) + 2:4 * (q % 3) + 11])
                                   for q in range(24 * h, 24 * h + 24)], "OH28 OH29%d OH30%d %s" % (h, h, bh), "P4", h == 0, h == 1)
         record(t)
         cp(T.ksb[:], KW[t], kb, "ksb")
         if t == 0:
-            mms(P[0][:, 0:256], [(i29, bn[:, :, 1:33]), (i29, bn[:, :, 2:34])], "i29 " + bk, "P0")
+            mms(P[0][:, 0:320], [(i29, bn[:, :, 1:B - 1]), (i29, bn[:, :, 2:B])], "i29 " + bk, "P0")
         else:
             ts(sc(t, 3), av, 28.0, None, EQ, None, "a1", "sL")
             ts(sc(t, 4), bv, 28.0, None, EQ, None, "b1", "sR")
@@ -399,7 +425,7 @@ def rank_program(g, core, T, topo):
             ts(iL, i30, sc(t, 3), None, MUL, None, "i30 sL", "iL")
             ts(iR, i30, sc(t, 4), None, MUL, None, "i30 sR", "iR")
             ts(sc(t, 5), zc, sc(t, 4), 29.0, SUB, EQ, "zc sR", "selz")
-            mms(P[0][:, 0:224], [(i30, bn[:, :, 3:31]), (i30, bn[:, :, 4:32]), (iL, bn[:, :, 5:33]), (iR, bn[:, :, 2:30])],
+            mms(P[0][:, 0:256], [(i30, bn[:, :, 3:19]), (i30, bn[:, :, 4:20]), (iL, bn[:, :, 5:21]), (iR, bn[:, :, 2:18])],
                 "i30 iL iR " + bk, "P0")
         tt(T.cv[:], T.enx[:], T.mlt[:], SUB, "enx mlt", "cv")
         ts(T.eqb[:], T.yrev[:], bv, None, EQ, None, "yrev b%d" % t, "eqb")
@@ -410,33 +436,50 @@ def rank_program(g, core, T, topo):
         if t == 0:
             tt(T.rvt[:], T.ent[:], T.mrt[:], SUB, "ent mrt", "rvt")
             tt(T.ml[:], T.mlu[:], T.mlb[:], ADD, "mlu mlb", "ml")
-        ld, c0 = T.ld1 if t == 0 else T.ld2, 12 * rank
-        tt(ld[:, c0:c0 + 12:2], P[4][:, 0, 3:9], T.mL[:, 3:9], MUL, "P4 mL", "tL%d" % t)
-        tt(ld[:, c0 + 1:c0 + 12:2], P[4][:, 0, 0:6], T.mR[:, 0:6], MUL, "P4 mR", "tR%d" % t)
-        send(ld[:, c0:c0 + 12], ld[:, c0:c0 + 12], "ar%d" % (t + 1), "tL%d tR%d" % (t, t))
+        ld, c0, n = T.ld1 if t == 0 else T.ld2, (8 << t) * rank, 4 + t
+        tt(ld[:, c0:c0 + 2 * n:2], P[4][:, 0, 4:4 + n], T.mL[:, 4:4 + n], MUL, "P4 mL ld", "tL%d" % t)
+        tt(ld[:, c0 + 1:c0 + 2 * n:2], P[4][:, 0, 1 - t:5], T.mR[:, 1 - t:5], MUL, "P4 mR ld", "tR%d" % t)
+        send(ld[:, c0:c0 + 2 * n], ld[:, c0:c0 + 2 * n], "ar%d" % (t + 1), "tL%d tR%d" % (t, t))
         if t == 0:
-            tt(T.C1[:, :, 1:33], P[0][:, 0:256], T.S[:, :, 1:33], MAX, "P0 S0 S1 Sl Sr", "C1")
+            constants_of_the_compaction()
+            ts(T.pnt2[:, 2:3], T.pint[:, 0:1], 15, None, A.bitwise_and, None, "pint", "pc")
+            ts(T.inv[:], T.S[:, :, own], 0.0, 8.0, EQ, MUL, "S0 S1", "inv")
+            tt(T.C1[:, :, 1:B - 1], P[0][:, 0:320], T.S[:, :, 1:B - 1], MAX, "P0 S0 S1 Sl Sr", "C1")
             ts(T.mlu[:], T.mlt[:], z28, None, MUL, None, "mlt z28", "mlu")
             ts(T.ent[:], T.mrt[:], z28, None, MUL, None, "mrt z28", "ent")
-            code_of(P[1][:, 0:248], T.C1[:, :, 1:32], [T.C1[:, :, 2:33]], "C1", "P1")
-            ts(T.OH[:, :, 0:24, 28], T.C1[:, :, own], 29.0, None, EQ, None, "C1", "OH28")
+            code_of(P[1][:, 0:304], T.C1[:, :, 1:B - 2], [T.C1[:, :, 2:B - 1]], "C1", "P1")
+            ts(T.OH[:, :, 0:12, 28], T.C1[:, :, own], 29.0, None, EQ, None, "C1", "OH28")
             tt(T.mlb[:], T.mlb[:], T.mlu[:], SUB, "mlb mlu", "mlb")
-            cp(T.cd[:, :, 2:33], P[1][:, 0:248], "P1", "cd")
+            ts(e1, T.pnt2[:, 2:3], 5.5, None, A.is_gt, None, "pc", "e1")
+            ts(e2, T.pnt2[:, 2:3], 12.5, None, SUB, None, "pc", "e2")
+            cp(T.cd[:, :, 2:B - 1], P[1][:, 0:304], "P1", "cd")
+            ts(e3, e2, e2, 0.5, MUL, A.is_gt, "e2", "e3")
+            ms(T.zf[:], 0.0, "zf")
+            ts(T.pnt2[:, 3:4], T.pint[:, 0:1], 1, None, A.bitwise_and, None, "pint", "pd")
+            tt(isE, e1, e3, MUL, "e1 e3", "isE")
         else:
-            tt(C[:, :, 3:31], P[0][:, 0:224], T.C1[:, :, 3:31], MAX, "P0 C1", "C2")
-            tt(T.dd[:, :, 4:30], T.bn0[:, :, 4:30], bn[:, :, 4:30], ADD, "bn00 bn01 " + bk, "dd")
-            mms(P[1][:, 0:192], [(idb, C[:, :, 7:31]), (idn, C[:, :, 6:30])], "C2", "P1")
+            constants_of_the_scatter()
+            tt(C[:, :, 3:19], P[0][:, 0:256], T.C1[:, :, 3:19], MAX, "P0 C1", "C2")
+            tt(T.dd[:, :, 4:18], T.bn0[:, :, 4:18], bn[:, :, 4:18], ADD, "bn00 bn01 " + bk, "dd")
+            mms(P[1][:, 0:192], [(idb, C[:, :, 7:19]), (idn, C[:, :, 6:18])], "C2", "P1")
             for s in range(4):
                 code_of(P[6][:, 48 * s:48 * s + 48], bun(C, 3, s), [bun(C, HL, s)], "C2", "P6")
+            code_of(P[6][:, 192:384], C[:, :, 3:15], [C[:, :, own]], "C2", "P6")
             for s in range(4):
                 mm(P[0][:, 48 * s:48 + 48 * s], idb, bun(T.dd, HL, s), True, True, "dd", "P0")
             tt(T.ml[:], T.mlu[:], T.mlb[:], ADD, "mlu mlb", "ml")
-            tt(T.g1[:], P[1][:, 0:192], T.dd[:, :, 6:30], MUL, "P1 dd", "g1")
+            tt(T.g1[:], P[1][:, 0:192], T.dd[:, :, 6:18], MUL, "P1 dd", "g1")
             tt(T.rvt[:], T.en1[:], T.mrt[:], SUB, "en1 mrt", "rvt")
-            mms(P[2][:, 0:192], [(idb, C[:, :, 6:30]), (idn, C[:, :, 5:29]), (idb, T.g1[:])], "C2 g1", "P2")
+            bundles(5, [(idb, C, HL)], "C2")
+            for s in range(4):
+                mm(P[2][:, 48 * s:48 * s + 48], i8, bun(T.dd, HL, s), False, False, "dd i8", "P2")
+            mms(P[1][:, 192:384], [(idb, C[:, :, 6:18]), (idn, C[:, :, 5:17]), (idb, T.g1[:])], "C2 g1", "P1")
             scan(T.d12[:], T.rst[:], P[0][:, 0:192], MUL, ADD, "rst P0", "d12")
-            cp(T.cb[:], P[6][:, 0:192], "P6", "cb")
-            mm(P[3][:, 0:128], T.idf[:], T.sixu[:], True, False, "sixu", "P3")
+            act(T.cb[:], P[6][:, 0:192], F.Copy, "P6", "cb")
+            act(T.cn[:], P[6][:, 192:384], F.Copy, "P6", "cn")
+            mm(P[2][:, 0:192], idb, T.d12[:], False, True, "d12", "P2")
+            act(T.base[:], P[2][:, 0:192], F.Copy, "P2", "base")
+            act(T.ucon[:], T.urow[:], F.Identity, "urow0 urow1 isE isV", "ucon", bias=isV, scale=isE)
         wait("V", "ar%d" % (t + 1), arrive)
         red(sc(t, 6), ld[:, 0::2], ADD, "tL%d" % t, "Ls")
         red(sc(t, 7), ld[:, 1::2], ADD, "tR%d" % t, "Rs")
@@ -446,118 +489,170 @@ def rank_program(g, core, T, topo):
         mm(K[t + 1], T.mrb[:] if t == 0 else T.mr[:], T.r2[:], False, True, "mrb r2" if t == 0 else "mr r2", nb)
         if t == 0:
             tt(T.mr[:], T.mrb[:], T.ent[:], SUB, "mrb ent", "mr")
-        else:
-            tt(T.h1[:], P[2][:, 0:192], T.dd[:, :, 5:29], MUL, "P2 dd", "h1")
-            mm(P[4][:, :, 0:6], idb, T.d12[:], True, False, "d12", "P4")
-            bundles(4, [(i8, T.dd, HL), (idb, T.inv, 0)], "dd inv i8")
+            act(isV, isE, F.Identity, "isE", "isV", bias=1.0, scale=-1.0)
+            act(T.par[:, 0:1], T.pnt2[:, 3:4], F.Identity, "pd", "pare", bias=1.0, scale=-1.0)
+            act(T.par[:, 1:2], T.pnt2[:, 3:4], F.Copy, "pd pare", "par")
+            mm(P[3][:, 0:32], T.idf[:], T.sixu[:], True, False, "sixu", "P3")
             mm(P[5][:, :, 0:6], idb, T.i32c[:], True, False, "i32c", "P5")
-            bundles(5, [(idb, C, HL)], "C2")
+            for s in range(4):
+                mm(P[2][:, 48 * s:48 * s + 48], idb, bun(T.inv, 0, s), s == 0, False, "inv", "P2")
+        else:
+            tt(T.h1[:], P[1][:, 192:384], T.dd[:, :, 5:17], MUL, "P1 dd", "h1")
+            mm(P[4][:, :, 0:6], idb, T.base[:], True, False, "base", "P4")
+            mm(P[2][:, 0:192], idb, T.base[:], True, False, "base", "P2")
+            for s in range(4):
+                mms(first_of(s), [(T.ngb[:] if s2 // 2 < s // 2 else T.trii[:] if s2 < s else T.tris[:], ends(T.d12, s2))
+                                  for s2 in range(s // 2 * 2 + 2)], "trii tris d12", "P3", False, False)
             for s in range(4):
                 code_of(P[1][:, 48 * s:48 + 48 * s], bun(C, HL, s), [bun(C, 5, s), bun(T.h1, 0, s)], "C2 h1", "P1")
-            firsts(T.d12, "d12", False)
 
     ap, b32 = winner(2)
     wv, dv = sc(2, 8), sc(2, 9)
     ts(T.b3[:], T.cb[:], b32, ap, ADD, EQ, "cb ap2 b322", "b3")
     mm(P[4][:, :, 0:6], i8, T.b3[:], False, False, "b3", "P4")
+    mm(P[2][:, 0:192], i8, T.b3[:], False, False, "b3", "P2")
     tt(wv, ap, b32, SUB, "ap2 b322", "wv")
-    ts(dv, ap, 31.0, None, ADD, None, "ap2", "dv")
+    ts(T.b3n[:], T.cn[:], b32, ap, ADD, EQ, "cn ap2 b322", "b3n")
     scan(T.d3[:], T.rst[:], T.b3[:], MUL, ADD, "rst b3", "d3")
     mm(P[4][:, :, 0:6], idb, T.d3[:], False, True, "d3", "P4")
+    mm(P[2][:, 0:192], idb, T.d3[:], False, True, "d3", "P2")
+    act(dv, ap, F.Identity, "ap2", "dv", bias=31.0)
     ts(T.hsv[:], P[1][:, 0:192], wv, dv, EQ, MUL, "P1 wv dv", "hsv")
     mm(P[5][:, :, 0:6], idb, T.hsv[:], False, True, "hsv", "P5")
-    firsts(T.d3, "d3", True)
+    scan(T.c3[:], T.rs12[:], T.b3n[:], MUL, ADD, "rs12 b3n", "c3")
+    for s in (2, 3, 0, 1):
+        h0 = 96 * (s // 2)
+        mms(first_of(s), [(T.tris[:], T.c3[:, h0 + 11:h0 + 96:12])] + [(T.ngb[:], T.c3[:, 11:96:12])] * (s // 2)
+            + [(idn, T.c3[:, h0 + 5:h0 + 96:12])] * (s % 2), "tris c3", "P3", False, s == 1)
+    def first_places(h):
+        for k in range(4):
+            act(T.zf[:, h, 12 + k:128:16], first_of(2 * h + k % 2), F.Identity, "P3 par zf", "zf%d%d" % (h, k),
+                bias=0.0, scale=T.par[:, k // 2:k // 2 + 1])
 
-    def mask(d):
-        out = T.X[:, d, :, 6:12 - d] if d < 4 else T.X[:, 0, :, 14:16]
-        ts(out, P[4][:, :, d:6], float(d), None, EQ, None, "P4 X", "Xm%d" % d)
+    act(T.X[:, 0, :, 6:12], P[2][:, 0:192], F.Relu, "P2 X", "Xm00 Xm01", bias=1.0, scale=-1.0)
+    first_places(1)
+    first_places(0)
 
-    def value(d):
-        out, m = (T.X[:, d, :, 0:6 - d], T.X[:, d, :, 6:12 - d]) if d < 4 else (T.X[:, 0, :, 12:14], T.X[:, 0, :, 14:16])
-        tt(out, P[5][:, :, d:6], m, MUL, "P5 Xm%d" % d, "Xv%d" % d)
-        if d < 4:
-            for s in range(4):
-                mm(P[0][:, s::4], T.X[:, d, 8 * s:8 * s + 8, :], idb, d == 3 and s == 0, d == 0 and s == 3,
-                   "Xv0 Xv4 idb" if d == 0 else "Xv%d idb" % d, "P0")
+    def mask(d, h):
+        rows = slice(16 * h, 16 * h + 16)
+        out = T.X[:, d, rows, 6:12 - d] if d < 4 else T.X[:, 0, rows, 14:16]
+        ts(out, P[4][:, rows, d:6], float(d), None, EQ, None, "P4 X", "Xm%d%d" % (d, h))
 
-    mask(3)
-    mask(2)
-    value(3)
-    value(2)
-    mask(1)
-    mask(4)
-    value(1)
-    cp(T.zf[:, 0:128], P[3][:, 0:128], "P3", "zf")
-    mms(P[6][:, 0:32], [(T.zf[:, 12 - 4 * m4:140 - 4 * m4], T.rmh[:, m4, :]) for m4 in range(4)], "zf rmh", "P6")
-    mask(0)
-    value(4)
-    value(0)
-    ts(T.o16[:], P[6][:, 0:32], float(L // 2), None, ADD, None, "P6", "o16")
-    record(2)
+    def value(d, h):
+        rows = slice(16 * h, 16 * h + 16)
+        out, m = (T.X[:, d, rows, 0:6 - d], T.X[:, d, rows, 6:12 - d]) if d < 4 else (T.X[:, 0, rows, 12:14], T.X[:, 0, rows, 14:16])
+        tt(out, P[5][:, rows, d:6], m, MUL, "P5 Xm%d%d" % (d, h), "Xv%d%d" % (d, h))
+        for k in range(2 if d < 4 else 0):
+            mm(P[7 * (1 - h)][:, 256 * h + k:256 * h + 256:2], T.X[:, d, 16 * h + 8 * k:16 * h + 8 * k + 8, :], idb,
+               d == 3 and k == 0, d == 0 and k == 1, "Xv%d%d Xv4%d" % (d, h, h) if d == 0 else "Xv%d%d" % (d, h), "P%d" % (7 * (1 - h)))
+
+    def close_up(h, between):
+        mask(3, h)
+        mask(2, h)
+        mask(1, h)
+        value(3, h)
+        mask(4, h)
+        value(2, h)
+        value(1, h)
+        between()
+        value(4, h)
+        value(0, h)
+
+    def first_list(h):
+        mms(P[6][:, 16 * h:16 * h + 16], [(T.zf[:, h, 12 - 4 * k:140 - 4 * k], T.rmh[:, k, :]) for k in range(4)],
+            "zf%d3 rmh" % h, "P6")
+        act(T.o16[:, 16 * h:16 * h + 16], P[6][:, 16 * h:16 * h + 16], F.Identity, "P6", "o16%d" % h, bias=float(L // 2))
+
+    def lanes(k):
+        us, bank = slice(16 * CUT[k + 1], 16 * CUT[k]), 0 if k < 2 else 7
+        act(T.xr[:, us], P[bank][:, us], F.Copy, "P%d" % bank, "xr%d" % k)
+
+    close_up(1, lambda: first_list(1))
+    lanes(0)
+    lanes(1)
+    act(T.mgs[:, 6:7], ap, F.Identity, "ap2", "a2", bias=-1.0, scale=-1.0)
+    act(T.mgs[:, 7:8], b32, F.Identity, "b322", "b2", bias=-1.0, scale=32.0)
+    act(T.mgs[:, 8:9], T.cnt[:, 2:3], F.Identity, "cnt", "c2", bias=-1.0)
     dma("Y", T.mg[:], T.mgs[0:1, 0:9], "dout", "a0 b0 c0 a1 b1 c1 a2 b2 c2", "")
-    for k in range(4):
-        us = slice(16 * CUT[k + 1], 16 * CUT[k])
-        act(T.xr[:, us], P[0][:, us], F.Copy, "P0", "xr%d" % k)
-    mms(P[7][0:8, 0:1], [(ends(d, s), T.onb[:, 0:1]) for d in (T.d12, T.d3) for s in range(4)], "d12 d3 onb", "P7")
-    tt(T.flb[0:8, 0:1], T.lei[0:8, 0:1], P[7][0:8, 0:1], SUB, "lei P7", "flb")
-    dma("Y", T.fl[:], T.flb[0:8, 0:1], "dout", "flb", "")
+    close_up(0, lambda: None)
+    first_list(0)
 
     def scatter(k):
         us = slice(16 * CUT[k + 1], 16 * CUT[k])
         tt(T.W[:, 16:16 + 96 * CUT[k] - 5].indirect(T.o16[:, CUT[k + 1]:CUT[k]]), T.xr[:, us], T.ucon[:, us], MUL,
-           "o16 xr%d ucon W" % k, "Ws W%d" % k)
+           "o16%d xr%d ucon W" % (1 - k // 2, k), "Ws W%d" % k)
         c0, n = 6 * CUT[k + 1], 6 * (CUT[k] - CUT[k + 1])
         mms(P[SB[k]][:, 0:n], [(T.zsel[:, e + 5, :], T.W[:, 16 + e + 16 * c0:16 + e + 16 * (c0 + n) - 15:16])
                                for e in range(-5, 16)], "zsel W%d" % k, "P%d" % SB[k])
 
     def places(k):
         c0, c1 = 6 * CUT[k + 1], 6 * CUT[k]
-        if k == 0:
+        if k < 2:
             act(T.j16[:, c0:c1], P[SB[k]][:, 0:c1 - c0], F.Identity, "P%d" % SB[k], "j%d" % k, bias=(49152.0 - 15.5) / 32,
                 scale=1.0 / 32)
         else:
             ts(T.j16[:, c0:c1], P[SB[k]][:, 0:c1 - c0], 49152.0 - 15.5, 1.0 / 32, ADD, MUL, "P%d" % SB[k], "j%d" % k)
 
-    def symbols(*ks):
+    def shifted(*ks):
         c0, c1 = 6 * CUT[ks[1] + 1], 6 * CUT[ks[0]]
         ts(T.jt[:, c0:c1], T.j16[:, c0:c1], -32.0, 49151.0, MUL, ADD, "j%d j%d" % ks, "jt%d" % ks[0])
+
+    def symbols(*ks):
         for k in ks:
             c0, c1 = 6 * CUT[k + 1], 6 * CUT[k]
             tt(T.sy[:, c0:c1], P[SB[k]][:, 0:c1 - c0], T.jt[:, c0:c1], ADD, "P%d jt%d" % (SB[k], ks[0]), "sy%d" % k)
 
-    YW = "Y0a Y0b Y0h Y0e"
+    YW, made = "Y0a Y0b Y0h Y0e", {}
 
-    def vectors(e, k, c0, c1, queue="Y"):
+    def vectors(e, k, c0, c1):
         src, key = T.Y0[:].indirect(T.j16[:, c0:c1]), "Y_%d" % c0
         if e == "S":
             act(T.Y[:, 16 * c0:16 * c1], src, F.Copy, YW + " j%d" % k, key)
         else:
             cp(T.Y[:, 16 * c0:16 * c1], src, YW + " j%d" % k, key)
-        return lambda: dma(queue, T.y[:, 16 * c0:16 * c1], T.Y[:, 16 * c0:16 * c1], "dout", key, "")
+        made[c0] = key
 
-    for k in range(3):
-        scatter(k)
+    def store(c0, c1, queue="Y"):
+        dma(queue, T.y[:, 16 * c0:16 * c1], T.Y[:, 16 * c0:16 * c1], "dout", " ".join(made[c] for c in made if c0 <= c < c1), "")
+
+    E = [6 * c for c in CUT]
+    lanes(2)
+    lanes(3)
+    mms(P[4][0:8, 0, 0:1], [(ends(d, s), T.onb[:, 0:1]) for d in (T.d12, T.d3) for s in range(4)], "d12 d3 onb", "P4")
+    scatter(0)
+    scatter(1)
+    tt(T.flb[0:8, 0:1], T.lei[0:8, 0:1], P[4][0:8, 0, 0:1], SUB, "lei P4", "flb")
+    dma("Y", T.fl[:], T.flb[0:8, 0:1], "dout", "flb", "")
+    scatter(2)
     places(0)
-    vectors("S", 0, 156, 192)()
+    vectors("S", 0, TS[6], E[0])
     places(1)
+    vectors("S", 0, E[1], TS[6])
+    store(E[1], E[0])
     scatter(3)
-    store = vectors("S", 1, TS[0], 156)
-    vectors("V", 1, 108, TS[0])()
+    shifted(0, 1)
+    vectors("S", 1, TS[0], E[1])
+    vectors("V", 1, E[2], TS[0])
     places(2)
     symbols(0, 1)
-    store()
-    store = vectors("S", 2, TS[1], 108)
+    store(E[2], E[1])
+    vectors("S", 2, TS[1], E[2])
     places(3)
-    vectors("V", 2, 48, TS[1])()
+    vectors("V", 2, TS[2], TS[1])
+    shifted(2, 3)
+    vectors("V", 2, E[3], TS[2])
     symbols(2, 3)
-    store()
-    store = vectors("S", 3, TS[2], 48, queue="S")
+    store(E[3], E[2])
+    vectors("S", 3, TS[3], E[3])
+    vectors("S", 3, TS[4], TS[3])
+    vectors("V", 3, TS[5], TS[4])
     for b in range(6):
         op("V", lambda: g.vector.transpose(T.fsb[:, :, b, :], T.sy[:, b::6]), "sy0 sy1 sy2 sy3", "fsb%d" % b)
+    store(TS[3], E[3])
     for k in range(2):
         dma("Y", T.fs[k::2, :], T.fsb[:, k, :, :], "dout", " ".join("fsb%d" % b for b in range(6)), "")
-    store()
-    vectors("V", 3, 0, TS[2])()
+    vectors("V", 3, 0, TS[5])
+    store(0, TS[3], "S")
 
     for e in count:
         wait("G", "c" + e, count[e])

from concourse.bass import DstId, RemoteDMATransfer
from concourse.mybir import AluOpType as A, AxisListType, ActivationFunctionType as F

N, L, M, S0 = 6, 3072, 6144, 28
HL, B, H = 4, 22, 1536
BIG = 8388608.0
WV = (880, 1280)
GC = (0, 50, 98, 122, 128, 134, 192)
NPV = (22, 21)
DB = (14, 16, 19)
CUT = (32, 26, 16, 8, 0)
TS = (120, 66, 56, 28, 20, 10, 170)
SB = (1, 2, 3, 6)
HB = (2, 0)
KB = (3, 6, 7)
bf, f16, f32, i32, u16 = "bfloat16", "float16", "float32", "int32", "uint16"

_SBUF = [
    (i32, [192], "posi rint pce"), (i32, [2052], "win"), (i32, [4], "lei pint pnt2 cnt"), (i32, [16, 13], "wi wj"),
    (i32, [2, 144], "wm"), (u16, [192], "r16 p16 j16"), (u16, [32], "o16"), (u16, [8 * N], "ld1"), (u16, [16 * N], "ld2"),
    (bf, [M], "vew"), (bf, [512], "xr ucon"), (bf, [3088], "G W Y0"), (bf, [L], "Y"), (bf, [800], "fz"),
    (bf, [192], "i32c rst rs12 d12 base b3 b3n hsv d3 c3"), (bf, [16, B], "S bn0 bn1 C1 C2 dd"), (bf, [16, 12], "inv g1 h1"),
    (bf, [16, 13, 32], "OH"), (bf, [16, 13, 28 - min(NPV)], "tab"), (bf, [400], "onb"), (bf, [8, 80], "mst"),
    (bf, [8], "pk"), (bf, [8, 128], "dg"), (bf, [128], "tris trii ngb zeb"), (bf, [4, 32, 16], "X"), (bf, [8, 36], "zs"),
    (bf, [21, 128], "zsel"),
    (f16, [16, B], "cd"), (f16, [192], "cb cn"), (f16, [2, 144], "zf"), (f16, [4, 16], "rmh"), (f16, [128], "sumh"),
    (f16, [2, 32], "msg"), (f16, [2, N, 32], "land"),
    (f32, [4], "lef kcol flb par"), (f32, [16, 13], "fT"), (f32, [144], "fm"),
    (f32, [128], "onf rep idf yrev mrb mr mrt rvt ent en1 eqb zer"),
    (f32, [192], "jl jt sy"), (f32, [512], "urow"),
    (f32, [32], "xrow col nega mlb ml mlt mlu cv enx r1 r2 row sixu"), (f32, [64], "k0 ksb bc rmm"),
    (f32, [33], "c32 ne"), (f32, [16], "colk mL mR"),
    (f32, [3, 33], "run"), (f32, [64], "sc"), (f32, [12], "mgs"), (f32, [2, 6, 16], "fsb"),
]
SCRATCH = {n: ("sbuf", [128] + s, d) for d, s, names in _SBUF for n in names.split()}
for _k in range(8):
    SCRATCH["P%d" % _k] = ("psum", [128, 32, 16] if _k in (4, 5) else [128, 512], f32)

SEMAPHORES = (["cV", "cS", "cP", "cG", "dpos", "dst", "dle", "dve", "dout", "sent", "ar0", "ar1", "ar2"]
              + ["a%d" % r for r in range(N)])


def rank_program(g, core, T, topo):
    rank = T.rank_of(core)
    if rank is None:
        return
    eng = {"V": g.vector, "S": g.scalar, "P": g.tensor, "G": g, "Y": g.sync}
    count = {"V": 0, "S": 0, "P": 0, "G": 0}
    waited = {e: {} for e in eng}
    lastw, readers = {}, {}

    def wait(e, sem, val):
        if waited[e].get(sem, 0) < val:
            eng[e].wait_ge(T.sem[sem], val)
            waited[e][sem] = val

    def order(e, r, w):
        for k in r:
            if k in lastw and not (e == "P" and lastw[k][2] == "P"):
                wait(e, lastw[k][0], lastw[k][1])
            if k[0] == "P":
                for x in readers.get(k, []):
                    if x[2] != e:
                        wait(e, x[0], x[1])
        for k in w:
            for x in readers.get(k, []) + ([lastw[k]] if k in lastw else []):
                if not (e == "P" and x[2] == "P"):
                    wait(e, x[0], x[1])

    def note(tok, r, w):
        for k in r:
            readers.setdefault(k, []).append(tok)
        for k in w:
            lastw[k] = tok
            readers[k] = []

    def op(e, fn, r, w):
        r, w = r.split(), w.split()
        order(e, r, w)
        count[e] += 1
        fn().then_inc(T.sem["c" + e], 1)
        note(("c" + e, count[e], e), r, w)

    def ts(out, in0, s1, s2, o0, o1, r, w):
        if o1 is None:
            op("V", lambda: g.vector.tensor_scalar(out, in0, s1, None, o0), r, w)
        else:
            op("V", lambda: g.vector.tensor_scalar(out, in0, s1, s2, o0, o1), r, w)

    def tt(out, a, b, o, r, w):
        op("V", lambda: g.vector.tensor_tensor(out, a, b, o), r, w)

    def cp(out, a, r, w):
        op("V", lambda: g.vector.tensor_copy(out, a), r, w)

    def ms(out, c, w):
        op("V", lambda: g.vector.memset(out, c), "", w)

    def red(out, a, o, r, w):
        op("V", lambda: g.vector.tensor_reduce(out, a, AxisListType.X, o), r, w)

    def scan(out, d0, d1, o0, o1, r, w):
        op("V", lambda: g.vector.tensor_tensor_scan(out, d0, d1, 0.0, o0, o1), r, w)

    def act(out, a, fn, r, w, bias=None, scale=1.0):
        if bias is None:
            op("S", lambda: g.scalar.activation(out, a, fn), r, w)
        else:
            op("S", lambda: g.scalar.activation(out, a, fn, bias=bias, scale=scale), r, w)

    def mm(out, lhsT, rhs, start, stop, r, w):
        op("P", lambda: g.tensor.matmul(out, lhsT, rhs, start, stop), r, w)

    def mms(out, terms, r, w, start=True, stop=True):
        for n, (lhsT, rhs) in enumerate(terms):
            mm(out, lhsT, rhs, start and n == 0, stop and n == len(terms) - 1, r, w)

    def iota(out, pat, base, cm, w, fl=True):
        if fl:
            op("G", lambda: g.iota(out, pat, base, cm, allow_small_or_imprecise_dtypes=True), "", w)
        else:
            op("G", lambda: g.iota(out, pat, base, cm), "", w)

    def sel(out, a, pat, cmp, base, cm, r, w):
        op("G", lambda: g.affine_select(out, a, pat, cmp, 0.0, base, cm), r, w)

    def put(out, a, pat, base, cm, val, r, w):
        op("G", lambda: g.affine_select(out, a, pat, A.not_equal, val, base, cm), r, w)

    def fill(out, n, c, w):
        act(out, T.onb[:, 0:n], F.Identity, "onb onb2" if n > 128 else "onb", w, bias=c, scale=0.0)

    ndma = {}

    def dma(e, out, a, sem, r, w):
        r, w = r.split(), w.split()
        order(e, r, w)
        ndma[sem] = ndma.get(sem, 0) + 16
        eng[e].dma_start(out, a).then_inc(T.sem[sem], 16)
        note((sem, ndma[sem], "D"), r, w)

    others = [r for r in range(N) if r != rank]
    near = [r for r in others if topo.chip(T.cores[r]) == topo.chip(core)]
    far = [r for r in others if r not in near]
    far_eng = topo.engines(core, T.cores[far[0]])
    near_eng = [e for e in topo.engines(core, T.cores[near[0]]) if e not in far_eng]
    nsent = [0]

    def send(src, dst, sem, r):
        order("G", r.split(), [])
        for peers, engs in ((far, far_eng), (near, near_eng)):
            ids = [DstId(rid=topo.addr(T.cores[p])[0], pnc=topo.addr(T.cores[p])[1]) for p in peers]
            g.remote_dma_fused([RemoteDMATransfer(dst_ids=ids, dma_engine_mask=sum(1 << e for e in engs), remote_sem=T.sem[sem],
                                                  srcs=[src], dsts=[dst] * len(peers))], local_sem=T.sem.sent)
            nsent[0] += len(engs)

    arrive = len(far) * len(far_eng) + len(near) * len(near_eng)
    P = [T["P%d" % k] for k in range(8)]
    EQ, ADD, SUB, MUL, MAX = A.is_equal, A.add, A.subtract, A.mult, A.max
    idb, idn, idm, i29, i30, i8, iL, iR = (T.dg[:, k, :] for k in range(8))
    own = slice(HL, HL + 12)
    half = (slice(0, 8), slice(8, 16))

    dma("Y", T.posi[:], T.pos[:], "dpos", "", "posi")
    dma("S", T.lei[0:8, 0:1], T.le[:], "dle", "", "lei")
    ms(T.onb[:, 0:128], 1.0, "onb")
    ms(T.win[:, 0:WV[0]], 0, "win0")
    iota(T.win[:, WV[0]:WV[1]], [[0, WV[1] - WV[0]]], 0, 0, "win1", False)
    for c0 in range(WV[1], 2048, 128):
        fill(T.win[:, c0:c0 + 128], 128, 0.0, "win%d" % c0)
    ms(T.onb[:, 128:400], 1.0, "onb2")
    ms(T.onf[:], 1.0, "onf")
    order("Y", [], ["win0", "win1", "win1920"])
    order("S", [], ["win0", "win1", "win1920"])
    for k in range(3):
        dma("YSY"[k], T.win[k::16, 0:2048], T.st[:, 2048 * k:2048 * k + 2048], "dst", "", "win" if k == 2 else "")
    dma("Y", T.vew[:], T.ve[:], "dve", "posi win", "vew")

    ms(T.mst[:], 0.0, "mst")
    fill(T.fz[:, 0:400], 400, 0.0, "fz_")
    fill(T.fz[:, 400:800], 400, 0.0, "fz")
    fill(T.win[:, 2048:2052], 4, -1.0, "wend")
    fill(T.pk[:], 8, 0.0, "pk")
    fill(T.G[:, 0:16], 16, 0.0, "Gl")
    fill(T.G[:, 3072:3088], 16, 0.0, "G")
    iota(T.kcol[:, 0:1], [[0, 1]], 0, 16, "kcol")
    iota(T.jl[:], [[16, 192]], 0, 1, "jl")
    sel(T.rep[0:8, :], T.onf[0:8, :], [[-1, 8], [0, 16]], EQ, 0, 1, "onf", "rep")
    sel(T.mst[:, :, 32:48], T.onb[:, 0:128], [[-16, 8], [-1, 16]], EQ, 0, 1, "onb", "mst")
    for k in range(3):
        put(T.pk[:], T.pk[:], [[-16, 8]], -k, 1, 64.0 ** k, "pk", "pk")
    iota(T.pint[:, 0:1], [[0, 1]], 0, 1, "pint", False)
    iota(T.OH[:, :, :, 28:32], [[0, 832]], 0, 0, "OH28 OH290 OH291 OH300 OH301")
    iota(T.yrev[:], [[0, 4], [-1, 32]], 31, 0, "yrev")
    iota(T.xrow[:], [[1, 32]], 0, 0, "xrow")
    sel(idb, T.onb[:, 0:128], [[-1, 128]], EQ, 0, 1, "onb", "idb")
    iota(T.k0[:, 0:28], [[-1, 28]], 31 + 32 * 4 * 2 * N * (L // 2), 0, "k0a")
    iota(T.k0[:, 28:32], [[-1, 4]], 3, 0, "k0b")
    iota(T.k0[:, 32:64], [[0, 32]], 0, 0, "k0c")
    for k in range(4):
        put(T.k0[:, 0:32], T.k0[:, 0:32], [[1, 32]], -31 - 32 * k, 1, -BIG, "k0a k0b k0", "k0")
    zc, kc, z28, le28, isE, isV, e1, e2, e3 = (T.col[:, k:k + 1] for k in range(9))

    def symbol_gather(e, k):
        c0, c1 = GC[k], GC[k + 1]
        out, src = T.G[:, HL + 16 * c0:HL + 16 * c1], T.win[:].indirect(T.r16[:, c0:c1])
        keys = "win wend " + ("r16" if k < 2 else "r16b")
        if e == "S":
            act(out, src, F.Identity, keys + " G", "G%d" % k, bias=1.0)
        else:
            ts(out, src, 1.0, None, ADD, None, keys + " Gl", "G%d" % k)

    tt(T.lef[0:8, 0:1], T.lei[0:8, 0:1], T.kcol[0:8, 0:1], ADD, "lei kcol", "lef")
    mm(P[7][:, 256:257], T.rep[0:8, :], T.lef[0:8, 0:1], True, True, "rep lef", "P7")
    ts(T.pce[:], T.posi[:], -3071.5, 1.0 / 2048, ADD, MUL, "posi", "pce")
    ts(T.rint[:], T.posi[:], 2047, None, A.bitwise_and, None, "posi", "rint")
    for x in range(3):
        ts(T.fz[:, 12 + x:780:12], T.pce[:, x::3], -63.0 / 64, -63.0 / 4096, MUL, MAX, "pce fz_ fz", "fz%d" % x)
    ts(T.jt[:, 0:98], T.jl[:, 0:98], P[7][:, 256:257], 2048.0, A.is_ge, MUL, "jl P7", "out")
    ts(T.jt[:, 98:192], T.jl[:, 98:192], P[7][:, 256:257], 2048.0, A.is_ge, MUL, "jl P7", "outb")
    tt(T.r16[:, 0:98], T.rint[:, 0:98], T.jt[:, 0:98], MAX, "rint out", "r16")
    symbol_gather("S", 1)
    tt(T.r16[:, 98:192], T.rint[:, 98:192], T.jt[:, 98:192], MAX, "rint outb", "r16b")
    symbol_gather("V", 0)

    def f_turn(out, h, b0, n, bank):
        terms = []
        for rho in range(4):
            for x in range((12 * rho + b0 - HL) // 16, (12 * rho + b0 + n - 1 - HL) // 16 + 1):
                a0, c0 = 12 + 384 * h + 12 * (x // 3) + x % 3 - 3 * rho, 32 - HL + 12 * rho - 16 * x + b0
                terms.append((T.fz[:, a0:a0 + 382:3], T.mst[:, :, c0:c0 + n]))
        mms(out, terms, "fz0 fz1 fz2 mst", bank)

    def s_turn(out, h, b, bank):
        mm(out, T.G[:, H * h + b:H * h + b + 1525:12], T.pk[:], True, True, ("G0 G1 pk", "G1 G2 G3 G4 G5 pk")[h], bank)

    for h in range(2):
        f_turn(P[7][:, 104 * h:104 * h + 104], h, HL, 13, "P7")
    for b in range(13):
        s_turn(P[4][:, 0:8, b], 0, HL + b, "P4")
    act(T.fT[:], P[7][:, 0:208], F.Identity, "P7", "fT0 fT1", bias=1.0 / 64)
    symbol_gather("S", 5)
    for h in range(2):
        f_turn(P[6][:, 32 * h:32 * h + 32], h, 0, 4, "P6")
        f_turn(P[6][:, 64 + 40 * h:104 + 40 * h], h, 17, 5, "P6")
    digit = [[lambda h=h: tt(T.wi[:, half[h], :], P[4 + h][:, 0:8, 0:13], T.fT[:, half[h], :], MUL, "P%d fT%d" % (4 + h, h), "wi%d" % h),
              lambda h=h: ts(T.wj[:, half[h], :], T.wi[:, half[h], :], 63, None, A.bitwise_and, None, "wi%d" % h, "wj%d" % h),
              lambda h=h: cp(T.S[:, half[h], HL:HL + 13], T.wj[:, half[h], :], "wj%d" % h, "S%d" % h)] for h in range(2)]
    for k in range(3):
        symbol_gather("V", 2 + k)
        digit[0][k]()
    for b in range(13):
        s_turn(P[5][:, 0:8, b], 1, HL + b, "P5")
    for h in range(2):
        for b in list(range(4)) + list(range(17, B)):
            out = P[3][:, 32 * h + b:32 * h + 32:4] if b < 4 else P[3][:, 47 + 40 * h + b:104 + 40 * h:5]
            mm(out, T.G[:, H * h + b:H * h + b + 1525:12], T.pk[:], True, True, "G0 G1 G2 G3 G4 G5 pk", "P3")
    ts(T.pnt2[:, 0:1], T.pint[:, 0:1], 31, None, A.bitwise_and, None, "pint", "pa")
    ts(T.pnt2[:, 1:2], T.pint[:, 0:1], 5, None, A.arith_shift_right, None, "pint", "pb")

    for h in range(2):
        n = NPV[h]
        for x in range(n):
            ts(T.OH[:, half[h], :, x], T.S[:, half[h], HL:HL + 13], float(x + 1), None, EQ, None, "S%d" % h, "OHv%d_%d" % (h, x))
            if h == 0 and x in DB:
                digit[1][DB.index(x)]()
        for x in range(n, 28):
            act(T.tab[:, half[h], :, x - n], T.wj[:, half[h], :], F.Abs, "wj%d" % h, "tab%d_%d" % (h, x), bias=-float(x + 1))
        for x0, x1 in ((n, 25), (25, 28)):
            act(T.OH[:, half[h], :, x0:x1], T.tab[:, half[h], :, x0 - n:x1 - n], F.Relu,
                " ".join("tab%d_%d" % (h, x) for x in range(x0, x1)), "OHs%d" % h if x1 == 28 else "", bias=1.0, scale=-1.0)
        for q in range(24):
            row, b0 = 8 * h + q // 3, 4 * (q % 3)
            mm(P[HB[h]][:, 0:112], T.OH[:, row, b0 + 1:b0 + 5, :], T.OH[:, row, b0:b0 + 4, 0:28], q == 0, q == 23,
               "OHs%d OHv%d_%d OH28" % (h, h, n - 1), "P%d" % HB[h])
    act(T.fm[:], P[6][:, 0:144], F.Identity, "P6", "fm", bias=1.0 / 64)

    def code_of(out, prev, cur, r, w):
        mms(out, [(idn, prev)] + [(idm, c) for c in cur], r + " idn idm", w)

    def counts(h):
        for k in range(4):
            ts(T.msg[32 * k:32 * k + 32, h, 0:28], P[HB[h]][32 * k:32 * k + 32, 28 * k:28 * k + 28], -float(L // 2), None,
               ADD, None, "P%d" % HB[h], "msg%d%d" % (h, k))
        keys = " ".join("msg%d%d" % (h, k) for k in range(4))
        send(T.msg[:, h, 0:28], T.land[:, h, rank, 0:28], "ar0" if h == 0 else "a%d" % rank, keys)
        return keys

    MSG0 = counts(0)
    cp(T.col[:, 0:2], T.pnt2[:, 0:2], "pa pb", "zc")
    tt(T.wm[:, 0, :], P[3][:, 0:144], T.fm[:], MUL, "P3 fm", "wih")
    ts(idn, idb, -1.0, None, MUL, None, "idb", "idn")
    ts(idm, idb, -1.0 / 32, None, MUL, None, "idb", "idm")
    ts(T.wm[:, 1, :], T.wm[:, 0, :], 63, None, A.bitwise_and, None, "wih", "wjh")
    ts(T.sumh[:], T.yrev[:], zc, 32.0, EQ, MUL, "yrev zc", "sumh")
    cp(T.S[:, :, 0:4], T.wm[:, 1, 0:64], "wjh", "Sl")
    cp(T.S[:, :, 17:B], T.wm[:, 1, 64:144], "wjh", "Sr")
    ms(T.zeb[:], 0.0, "zeb")
    ms(T.zer[:], 0.0, "zer")
    MSG1 = counts(1)
    cp(T.p16[:], T.posi[:], "posi", "p16")
    fill(T.ngb[:], 128, -1.0, "ngb")
    act(T.W[:], T.G[:], F.Identity, "G0 G1 G2 G3 G4 G5", "W", bias=0.0, scale=0.0)
    act(T.Y0[:, 0:1536], T.vew[:].indirect(T.p16[:, 0:96]), F.Copy, "vew p16", "Y0a")
    act(T.Y0[:, 1542:3078], T.vew[:].indirect(T.p16[:, 96:192]), F.Copy, "vew p16", "Y0b")
    act(T.X[:], T.G[:, 0:2048], F.Identity, "G0 G1 G2 G3 G4 G5", "X", bias=0.0, scale=0.0)
    K = [P[k][:, 0:32] for k in KB]
    KW = [P[k][:, 0:64] for k in KB]
    sel(T.idf[:], T.onf[:], [[-1, 128]], EQ, 0, 1, "onf", "idf")
    code_of(P[1][:, 0:336], T.S[:, :, 0:B - 1], [T.S[:, :, 1:B]], "S0 S1 Sl Sr", "P1")
    mm(KW[0], T.idf[:], T.k0[:], True, False, "idf k0 k0c", "P3")
    K28 = P[KB[0]][:, 0:28]
    mms(K28, [(T.sumh[:], T.msg[:, h, 0:28]) for h in range(2)], "sumh %s %s" % (MSG0, MSG1), "P3", False, False)
    wait("P", "ar0", arrive)
    mms(K28, [(T.sumh[:], T.land[:, 0, r, 0:28]) for r in others], "sumh", "P3", False, False)
    for n, r in enumerate(near + far):
        wait("P", "a%d" % r, len(near_eng) if r in near else len(far_eng))
        mm(K28, T.sumh[:], T.land[:, 1, r, 0:28], False, n == N - 2, "sumh", "P3")

    ms(T.c32[:], 1.0 / 32, "c32")
    ms(T.ne[:], 1.0, "ne")
    ms(T.ld2[:], 0, "ld")
    cp(T.cd[:, :, 1:B], P[1][:, 0:336], "P1", "cd")
    ts(T.colk[:], T.xrow[:, 0:16], kc, None, SUB, None, "xrow zc", "colk")
    ts(le28, zc, 28.5, None, A.is_lt, None, "zc", "le28")
    ts(z28, zc, 28.0, None, EQ, None, "zc", "z28")
    ts(T.sc[:, 5:6], zc, 29.0, None, EQ, None, "zc", "selz")
    ts(T.mL[:], T.colk[:], 4.0, None, EQ, None, "colk", "mL")
    ts(T.mR[:], T.colk[:], 1.0, None, EQ, None, "colk", "mR")
    ts(T.mlb[:], T.xrow[:], zc, le28, EQ, MUL, "xrow zc le28", "mlb")
    ts(T.mrb[:], T.sumh[:], le28, None, MUL, None, "sumh le28", "mrb")
    ts(T.enx[:], T.xrow[:], float(S0), None, EQ, None, "xrow", "enx")
    ms(T.zs[:], 0.0, "zs")
    put(T.ent[:], T.zer[:], [[0, 4], [-1, 32]], 31 - S0, 0, 32.0, "zer", "ent")
    put(i29, T.zeb[:], [[-1, 128]], 0, 1, 29.0, "zeb", "i29")
    iota(T.sixu[:], [[H, 2], [6, 2], [0, 8]], -L // 2, 12, "sixu")
    iota(T.i32c[:], [[0, 32], [32, 6]], 0, 0, "i32c")
    put(T.en1[:], T.zer[:], [[0, 4], [-1, 32]], 30 - S0, 0, 32.0, "zer", "en1")
    put(i30, T.zeb[:], [[-1, 128]], 0, 1, 30.0, "zeb", "i30")
    sel(T.rst[:], T.onb[:, 0:192], [[0, 32], [1, 6]], A.is_gt, 0, 0, "onb onb2", "rst")

    def constants_of_the_compaction():
        for lane, n, val in ((0, 6, 1.0), (6, 6, 192.0), (12, 2, 1.0), (14, 2, 192.0)):
            put(T.zs[:, :, 15:15 + n], T.zs[:, :, 15:15 + n], [[-16, 8], [-1, n]], -lane, 1, val, "zs", "zs")
        put(i8, T.zeb[:], [[-1, 128]], 0, 1, 8.0, "zeb", "i8")
        sel(T.tris[:], T.ngb[:], [[1, 128]], A.is_gt, 0, -1, "ngb", "tris")
        sel(T.trii[:], T.ngb[:], [[1, 128]], A.is_ge, 0, -1, "ngb", "trii")
        sel(T.rs12[:], T.onb[:, 0:192], [[0, 16], [1, 12]], A.is_gt, 0, 0, "onb onb2", "rs12")
        sel(T.rmm[:], T.onf[:, 0:64], [[-2, 4], [-8, 16]], A.is_ge, 0, 1, "onf", "rmm")
        sel(T.rmm[:], T.rmm[:], [[2, 4], [8, 16]], A.is_ge, 1, -1, "rmm", "rmm")
        for e in range(-5, 16):
            act(T.zsel[:, e + 5, :], T.zs[:, :, 15 - e:31 - e], F.Copy, "zs", "zsel" if e == 15 else "zsel%d" % e)
        act(T.rmh[:], T.rmm[:], F.Copy, "rmm", "rmh")

    def constants_of_the_scatter():
        iota(T.urow[:, 0:256], [[1, 256]], -256, 0, "urow0")
        iota(T.urow[:, 256:512], [[1, 256]], 1, 0, "urow1")
        iota(T.Y0[:, 1536:1542], [[0, 6]], 0, 0, "Y0h")
        iota(T.Y0[:, 3078:3088], [[0, 10]], 0, 0, "Y0e")

    def sc(t, k):
        return T.sc[:, 16 * t + k:16 * t + k + 1]

    def winner(t):
        scan(T.bc[:], KW[t], T.zer[:, 0:64], MAX, ADD, "P%d zer" % KB[t], "bc")
        op("V", lambda: g.vector.transpose(T.row[:], T.bc[:, 32:64]), "bc", "row")
        red(sc(t, 1), T.row[:], MAX, "row", "gm")
        if t < 2:
            ts(T.cnt[:, t:t + 1], sc(t, 1), 16.5, 1.0 / 32, ADD, MUL, "gm", "cnt")
        else:
            act(T.cnt[:, t:t + 1], sc(t, 1), F.Identity, "gm", "cnt", bias=16.5 / 32, scale=1.0 / 32)
            act(sc(t, 2), T.cnt[:, t:t + 1], F.Identity, "cnt gm", "ap%d" % t, bias=sc(t, 1), scale=-32.0)
        ts(T.ne[:, 0:32], T.row[:], sc(t, 1), None, A.not_equal, None, "row gm", "ne")
        if t < 2:
            ts(sc(t, 2), T.cnt[:, t:t + 1], -32.0, sc(t, 1), MUL, ADD, "cnt gm", "ap%d" % t)
        scan(T.run[:, t, :], T.c32[:], T.ne[:], ADD, MUL, "c32 ne", "b32%d" % t)
        return sc(t, 2), T.run[:, t, 32:33]

    def record(t):
        ts(T.mgs[:, 3 * t:3 * t + 1], sc(t, 2), -1.0, -1.0, MUL, ADD, "ap%d" % t, "a%d" % t)
        ts(T.mgs[:, 3 * t + 1:3 * t + 2], T.run[:, t, 32:33], 32.0, -1.0, MUL, ADD, "b32%d" % t, "b%d" % t)
        ts(T.mgs[:, 3 * t + 2:3 * t + 3], T.cnt[:, t:t + 1], -1.0, None, ADD, None, "cnt", "c%d" % t)

    def bun(src, c0, s):
        return src[:, half[s // 2], c0 + 6 * (s % 2):c0 + 6 * (s % 2) + 6]

    def ends(src, s):
        return src[:, 48 * s + 5:48 * s + 48:6]

    def first_of(s):
        return P[3][:, 8 * s:8 * s + 8]

    def bundles(bank, terms, r):
        for lhsT, src, c0 in terms:
            for s in range(4):
                mm(P[bank][:, 8 * s:8 * s + 8, 0:6], lhsT, bun(src, c0, s), False, False, r, "P%d" % bank)

    C = T.C2
    for t in range(2):
        ap, b32 = winner(t)
        av, bv = T.mgs[:, 3 * t:3 * t + 1], T.mgs[:, 3 * t + 1:3 * t + 2]
        bn, lo, hi = (T.bn0, 1, B) if t == 0 else (T.bn1, 2, B - 1)
        bk, kb, nb = "bn%d0 bn%d1" % (t, t), "P%d" % KB[t], "P%d" % KB[t + 1]
        for h in range(2):
            gs, bh, won = half[h], "bn%d%d" % (t, h), "cd ap%d b32%d" % (t, t)
            ts(bn[:, gs, lo:hi], T.cd[:, gs, lo:hi], b32, ap, ADD, EQ, won, bh)
            ts(T.OH[:, gs, 0:12, 29], T.cd[:, gs, own], b32, ap, ADD, EQ, won, "OH29%d" % h)
            if t == 1:
                ts(T.OH[:, gs, 0:12, 30], T.cd[:, gs, HL - 1:HL + 11], b32, ap, ADD, EQ, won, "OH30%d" % h)
            mms(P[4][:, 0, 0:9], [(T.OH[:, q // 3, 4 * (q % 3):4 * (q % 3) + 4, :], bn[:, q // 3, 4 * (q % 3) + 2:4 * (q % 3) + 11])
                                  for q in range(24 * h, 24 * h + 24)], "OH28 OH29%d OH30%d %s" % (h, h, bh), "P4", h == 0, h == 1)
        record(t)
        cp(T.ksb[:], KW[t], kb, "ksb")
        if t == 0:
            mms(P[0][:, 0:320], [(i29, bn[:, :, 1:B - 1]), (i29, bn[:, :, 2:B])], "i29 " + bk, "P0")
        else:
            ts(sc(t, 3), av, 28.0, None, EQ, None, "a1", "sL")
            ts(sc(t, 4), bv, 28.0, None, EQ, None, "b1", "sR")
            ts(T.enx[:], T.xrow[:], float(S0 + 1), None, EQ, None, "xrow", "enx")
        ts(T.mlt[:], T.xrow[:], bv, None, EQ, None, "xrow b%d" % t, "mlt")
        ts(T.nega[:], T.xrow[:], av, -BIG / 128, EQ, MUL, "xrow a%d" % t, "nega")
        if t == 1:
            ts(T.mL[:], T.colk[:], sc(t, 3), 4.0, SUB, EQ, "colk sL", "mL")
            ts(T.mR[:], T.colk[:], sc(t, 4), 1.0, ADD, EQ, "colk sR", "mR")
            ts(iL, i30, sc(t, 3), None, MUL, None, "i30 sL", "iL")
            ts(iR, i30, sc(t, 4), None, MUL, None, "i30 sR", "iR")
            ts(sc(t, 5), zc, sc(t, 4), 29.0, SUB, EQ, "zc sR", "selz")
            mms(P[0][:, 0:256], [(i30, bn[:, :, 3:19]), (i30, bn[:, :, 4:20]), (iL, bn[:, :, 5:21]), (iR, bn[:, :, 2:18])],
                "i30 iL iR " + bk, "P0")
        tt(T.cv[:], T.enx[:], T.mlt[:], SUB, "enx mlt", "cv")
        ts(T.eqb[:], T.yrev[:], bv, None, EQ, None, "yrev b%d" % t, "eqb")
        ts(T.mrt[:], T.yrev[:], av, 32.0, EQ, MUL, "yrev a%d" % t, "mrt")
        ts(T.mlu[:], T.cv[:], sc(t, 5), None, MUL, None, "cv selz", "mlu")
        mm(KW[t + 1], T.idf[:], T.ksb[:], True, False, "idf ksb", nb)
        mm(K[t + 1], T.eqb[:], T.nega[:], False, False, "eqb nega", nb)
        if t == 0:
            tt(T.rvt[:], T.ent[:], T.mrt[:], SUB, "ent mrt", "rvt")
            tt(T.ml[:], T.mlu[:], T.mlb[:], ADD, "mlu mlb", "ml")
        ld, c0, n = T.ld1 if t == 0 else T.ld2, (8 << t) * rank, 4 + t
        tt(ld[:, c0:c0 + 2 * n:2], P[4][:, 0, 4:4 + n], T.mL[:, 4:4 + n], MUL, "P4 mL ld", "tL%d" % t)
        tt(ld[:, c0 + 1:c0 + 2 * n:2], P[4][:, 0, 1 - t:5], T.mR[:, 1 - t:5], MUL, "P4 mR ld", "tR%d" % t)
        send(ld[:, c0:c0 + 2 * n], ld[:, c0:c0 + 2 * n], "ar%d" % (t + 1), "tL%d tR%d" % (t, t))
        if t == 0:
            constants_of_the_compaction()
            ts(T.pnt2[:, 2:3], T.pint[:, 0:1], 15, None, A.bitwise_and, None, "pint", "pc")
            ts(T.inv[:], T.S[:, :, own], 0.0, 8.0, EQ, MUL, "S0 S1", "inv")
            tt(T.C1[:, :, 1:B - 1], P[0][:, 0:320], T.S[:, :, 1:B - 1], MAX, "P0 S0 S1 Sl Sr", "C1")
            ts(T.mlu[:], T.mlt[:], z28, None, MUL, None, "mlt z28", "mlu")
            ts(T.ent[:], T.mrt[:], z28, None, MUL, None, "mrt z28", "ent")
            code_of(P[1][:, 0:304], T.C1[:, :, 1:B - 2], [T.C1[:, :, 2:B - 1]], "C1", "P1")
            ts(T.OH[:, :, 0:12, 28], T.C1[:, :, own], 29.0, None, EQ, None, "C1", "OH28")
            tt(T.mlb[:], T.mlb[:], T.mlu[:], SUB, "mlb mlu", "mlb")
            ts(e1, T.pnt2[:, 2:3], 5.5, None, A.is_gt, None, "pc", "e1")
            ts(e2, T.pnt2[:, 2:3], 12.5, None, SUB, None, "pc", "e2")
            cp(T.cd[:, :, 2:B - 1], P[1][:, 0:304], "P1", "cd")
            ts(e3, e2, e2, 0.5, MUL, A.is_gt, "e2", "e3")
            ms(T.zf[:], 0.0, "zf")
            ts(T.pnt2[:, 3:4], T.pint[:, 0:1], 1, None, A.bitwise_and, None, "pint", "pd")
            tt(isE, e1, e3, MUL, "e1 e3", "isE")
        else:
            constants_of_the_scatter()
            tt(C[:, :, 3:19], P[0][:, 0:256], T.C1[:, :, 3:19], MAX, "P0 C1", "C2")
            tt(T.dd[:, :, 4:18], T.bn0[:, :, 4:18], bn[:, :, 4:18], ADD, "bn00 bn01 " + bk, "dd")
            mms(P[1][:, 0:192], [(idb, C[:, :, 7:19]), (idn, C[:, :, 6:18])], "C2", "P1")
            for s in range(4):
                code_of(P[6][:, 48 * s:48 * s + 48], bun(C, 3, s), [bun(C, HL, s)], "C2", "P6")
            code_of(P[6][:, 192:384], C[:, :, 3:15], [C[:, :, own]], "C2", "P6")
            for s in range(4):
                mm(P[0][:, 48 * s:48 + 48 * s], idb, bun(T.dd, HL, s), True, True, "dd", "P0")
            tt(T.ml[:], T.mlu[:], T.mlb[:], ADD, "mlu mlb", "ml")
            tt(T.g1[:], P[1][:, 0:192], T.dd[:, :, 6:18], MUL, "P1 dd", "g1")
            tt(T.rvt[:], T.en1[:], T.mrt[:], SUB, "en1 mrt", "rvt")
            bundles(5, [(idb, C, HL)], "C2")
            for s in range(4):
                mm(P[2][:, 48 * s:48 * s + 48], i8, bun(T.dd, HL, s), False, False, "dd i8", "P2")
            mms(P[1][:, 192:384], [(idb, C[:, :, 6:18]), (idn, C[:, :, 5:17]), (idb, T.g1[:])], "C2 g1", "P1")
            scan(T.d12[:], T.rst[:], P[0][:, 0:192], MUL, ADD, "rst P0", "d12")
            act(T.cb[:], P[6][:, 0:192], F.Copy, "P6", "cb")
            act(T.cn[:], P[6][:, 192:384], F.Copy, "P6", "cn")
            mm(P[2][:, 0:192], idb, T.d12[:], False, True, "d12", "P2")
            act(T.base[:], P[2][:, 0:192], F.Copy, "P2", "base")
            act(T.ucon[:], T.urow[:], F.Identity, "urow0 urow1 isE isV", "ucon", bias=isV, scale=isE)
        wait("V", "ar%d" % (t + 1), arrive)
        red(sc(t, 6), ld[:, 0::2], ADD, "tL%d" % t, "Ls")
        red(sc(t, 7), ld[:, 1::2], ADD, "tR%d" % t, "Rs")
        ts(T.r1[:], T.ml[:], sc(t, 6), None, MUL, None, "ml Ls", "r1")
        ts(T.r2[:], T.cv[:], sc(t, 7), None, MUL, None, "cv Rs", "r2")
        mm(K[t + 1], T.rvt[:], T.r1[:], False, False, "rvt r1", nb)
        mm(K[t + 1], T.mrb[:] if t == 0 else T.mr[:], T.r2[:], False, True, "mrb r2" if t == 0 else "mr r2", nb)
        if t == 0:
            tt(T.mr[:], T.mrb[:], T.ent[:], SUB, "mrb ent", "mr")
            act(isV, isE, F.Identity, "isE", "isV", bias=1.0, scale=-1.0)
            act(T.par[:, 0:1], T.pnt2[:, 3:4], F.Identity, "pd", "pare", bias=1.0, scale=-1.0)
            act(T.par[:, 1:2], T.pnt2[:, 3:4], F.Copy, "pd pare", "par")
            mm(P[3][:, 0:32], T.idf[:], T.sixu[:], True, False, "sixu", "P3")
            mm(P[5][:, :, 0:6], idb, T.i32c[:], True, False, "i32c", "P5")
            for s in range(4):
                mm(P[2][:, 48 * s:48 * s + 48], idb, bun(T.inv, 0, s), s == 0, False, "inv", "P2")
        else:
            tt(T.h1[:], P[1][:, 192:384], T.dd[:, :, 5:17], MUL, "P1 dd", "h1")
            mm(P[4][:, :, 0:6], idb, T.base[:], True, False, "base", "P4")
            mm(P[2][:, 0:192], idb, T.base[:], True, False, "base", "P2")
            for s in range(4):
                mms(first_of(s), [(T.ngb[:] if s2 // 2 < s // 2 else T.trii[:] if s2 < s else T.tris[:], ends(T.d12, s2))
                                  for s2 in range(s // 2 * 2 + 2)], "trii tris d12", "P3", False, False)
            for s in range(4):
                code_of(P[1][:, 48 * s:48 + 48 * s], bun(C, HL, s), [bun(C, 5, s), bun(T.h1, 0, s)], "C2 h1", "P1")

    ap, b32 = winner(2)
    wv, dv = sc(2, 8), sc(2, 9)
    ts(T.b3[:], T.cb[:], b32, ap, ADD, EQ, "cb ap2 b322", "b3")
    mm(P[4][:, :, 0:6], i8, T.b3[:], False, False, "b3", "P4")
    mm(P[2][:, 0:192], i8, T.b3[:], False, False, "b3", "P2")
    tt(wv, ap, b32, SUB, "ap2 b322", "wv")
    ts(T.b3n[:], T.cn[:], b32, ap, ADD, EQ, "cn ap2 b322", "b3n")
    scan(T.d3[:], T.rst[:], T.b3[:], MUL, ADD, "rst b3", "d3")
    mm(P[4][:, :, 0:6], idb, T.d3[:], False, True, "d3", "P4")
    mm(P[2][:, 0:192], idb, T.d3[:], False, True, "d3", "P2")
    act(dv, ap, F.Identity, "ap2", "dv", bias=31.0)
    ts(T.hsv[:], P[1][:, 0:192], wv, dv, EQ, MUL, "P1 wv dv", "hsv")
    mm(P[5][:, :, 0:6], idb, T.hsv[:], False, True, "hsv", "P5")
    scan(T.c3[:], T.rs12[:], T.b3n[:], MUL, ADD, "rs12 b3n", "c3")
    for s in (2, 3, 0, 1):
        h0 = 96 * (s // 2)
        mms(first_of(s), [(T.tris[:], T.c3[:, h0 + 11:h0 + 96:12])] + [(T.ngb[:], T.c3[:, 11:96:12])] * (s // 2)
            + [(idn, T.c3[:, h0 + 5:h0 + 96:12])] * (s % 2), "tris c3", "P3", False, s == 1)
    def first_places(h):
        for k in range(4):
            act(T.zf[:, h, 12 + k:128:16], first_of(2 * h + k % 2), F.Identity, "P3 par zf", "zf%d%d" % (h, k),
                bias=0.0, scale=T.par[:, k // 2:k // 2 + 1])

    act(T.X[:, 0, :, 6:12], P[2][:, 0:192], F.Relu, "P2 X", "Xm00 Xm01", bias=1.0, scale=-1.0)
    first_places(1)
    first_places(0)

    def mask(d, h):
        rows = slice(16 * h, 16 * h + 16)
        out = T.X[:, d, rows, 6:12 - d] if d < 4 else T.X[:, 0, rows, 14:16]
        ts(out, P[4][:, rows, d:6], float(d), None, EQ, None, "P4 X", "Xm%d%d" % (d, h))

    def value(d, h):
        rows = slice(16 * h, 16 * h + 16)
        out, m = (T.X[:, d, rows, 0:6 - d], T.X[:, d, rows, 6:12 - d]) if d < 4 else (T.X[:, 0, rows, 12:14], T.X[:, 0, rows, 14:16])
        tt(out, P[5][:, rows, d:6], m, MUL, "P5 Xm%d%d" % (d, h), "Xv%d%d" % (d, h))
        for k in range(2 if d < 4 else 0):
            mm(P[7 * (1 - h)][:, 256 * h + k:256 * h + 256:2], T.X[:, d, 16 * h + 8 * k:16 * h + 8 * k + 8, :], idb,
               d == 3 and k == 0, d == 0 and k == 1, "Xv%d%d Xv4%d" % (d, h, h) if d == 0 else "Xv%d%d" % (d, h), "P%d" % (7 * (1 - h)))

    def close_up(h, between):
        mask(3, h)
        mask(2, h)
        mask(1, h)
        value(3, h)
        mask(4, h)
        value(2, h)
        value(1, h)
        between()
        value(4, h)
        value(0, h)

    def first_list(h):
        mms(P[6][:, 16 * h:16 * h + 16], [(T.zf[:, h, 12 - 4 * k:140 - 4 * k], T.rmh[:, k, :]) for k in range(4)],
            "zf%d3 rmh" % h, "P6")
        act(T.o16[:, 16 * h:16 * h + 16], P[6][:, 16 * h:16 * h + 16], F.Identity, "P6", "o16%d" % h, bias=float(L // 2))

    def lanes(k):
        us, bank = slice(16 * CUT[k + 1], 16 * CUT[k]), 0 if k < 2 else 7
        act(T.xr[:, us], P[bank][:, us], F.Copy, "P%d" % bank, "xr%d" % k)

    close_up(1, lambda: first_list(1))
    lanes(0)
    lanes(1)
    act(T.mgs[:, 6:7], ap, F.Identity, "ap2", "a2", bias=-1.0, scale=-1.0)
    act(T.mgs[:, 7:8], b32, F.Identity, "b322", "b2", bias=-1.0, scale=32.0)
    act(T.mgs[:, 8:9], T.cnt[:, 2:3], F.Identity, "cnt", "c2", bias=-1.0)
    dma("Y", T.mg[:], T.mgs[0:1, 0:9], "dout", "a0 b0 c0 a1 b1 c1 a2 b2 c2", "")
    close_up(0, lambda: None)
    first_list(0)

    def scatter(k):
        us = slice(16 * CUT[k + 1], 16 * CUT[k])
        tt(T.W[:, 16:16 + 96 * CUT[k] - 5].indirect(T.o16[:, CUT[k + 1]:CUT[k]]), T.xr[:, us], T.ucon[:, us], MUL,
           "o16%d xr%d ucon W" % (1 - k // 2, k), "Ws W%d" % k)
        c0, n = 6 * CUT[k + 1], 6 * (CUT[k] - CUT[k + 1])
        mms(P[SB[k]][:, 0:n], [(T.zsel[:, e + 5, :], T.W[:, 16 + e + 16 * c0:16 + e + 16 * (c0 + n) - 15:16])
                               for e in range(-5, 16)], "zsel W%d" % k, "P%d" % SB[k])

    def places(k):
        c0, c1 = 6 * CUT[k + 1], 6 * CUT[k]
        if k < 2:
            act(T.j16[:, c0:c1], P[SB[k]][:, 0:c1 - c0], F.Identity, "P%d" % SB[k], "j%d" % k, bias=(49152.0 - 15.5) / 32,
                scale=1.0 / 32)
        else:
            ts(T.j16[:, c0:c1], P[SB[k]][:, 0:c1 - c0], 49152.0 - 15.5, 1.0 / 32, ADD, MUL, "P%d" % SB[k], "j%d" % k)

    def shifted(*ks):
        c0, c1 = 6 * CUT[ks[1] + 1], 6 * CUT[ks[0]]
        ts(T.jt[:, c0:c1], T.j16[:, c0:c1], -32.0, 49151.0, MUL, ADD, "j%d j%d" % ks, "jt%d" % ks[0])

    def symbols(*ks):
        for k in ks:
            c0, c1 = 6 * CUT[k + 1], 6 * CUT[k]
            tt(T.sy[:, c0:c1], P[SB[k]][:, 0:c1 - c0], T.jt[:, c0:c1], ADD, "P%d jt%d" % (SB[k], ks[0]), "sy%d" % k)

    YW, made = "Y0a Y0b Y0h Y0e", {}

    def vectors(e, k, c0, c1):
        src, key = T.Y0[:].indirect(T.j16[:, c0:c1]), "Y_%d" % c0
        if e == "S":
            act(T.Y[:, 16 * c0:16 * c1], src, F.Copy, YW + " j%d" % k, key)
        else:
            cp(T.Y[:, 16 * c0:16 * c1], src, YW + " j%d" % k, key)
        made[c0] = key

    def store(c0, c1, queue="Y"):
        dma(queue, T.y[:, 16 * c0:16 * c1], T.Y[:, 16 * c0:16 * c1], "dout", " ".join(made[c] for c in made if c0 <= c < c1), "")

    E = [6 * c for c in CUT]
    lanes(2)
    lanes(3)
    mms(P[4][0:8, 0, 0:1], [(ends(d, s), T.onb[:, 0:1]) for d in (T.d12, T.d3) for s in range(4)], "d12 d3 onb", "P4")
    scatter(0)
    scatter(1)
    tt(T.flb[0:8, 0:1], T.lei[0:8, 0:1], P[4][0:8, 0, 0:1], SUB, "lei P4", "flb")
    dma("Y", T.fl[:], T.flb[0:8, 0:1], "dout", "flb", "")
    scatter(2)
    places(0)
    vectors("S", 0, TS[6], E[0])
    places(1)
    vectors("S", 0, E[1], TS[6])
    store(E[1], E[0])
    scatter(3)
    shifted(0, 1)
    vectors("S", 1, TS[0], E[1])
    vectors("V", 1, E[2], TS[0])
    places(2)
    symbols(0, 1)
    store(E[2], E[1])
    vectors("S", 2, TS[1], E[2])
    places(3)
    vectors("V", 2, TS[2], TS[1])
    shifted(2, 3)
    vectors("V", 2, E[3], TS[2])
    symbols(2, 3)
    store(E[3], E[2])
    vectors("S", 3, TS[3], E[3])
    vectors("S", 3, TS[4], TS[3])
    vectors("V", 3, TS[5], TS[4])
    for b in range(6):
        op("V", lambda: g.vector.transpose(T.fsb[:, :, b, :], T.sy[:, b::6]), "sy0 sy1 sy2 sy3", "fsb%d" % b)
    store(TS[3], E[3])
    for k in range(2):
        dma("Y", T.fs[k::2, :], T.fsb[:, k, :, :], "dout", " ".join("fsb%d" % b for b in range(6)), "")
    vectors("V", 3, 0, TS[5])
    store(0, TS[3], "S")

    for e in count:
        wait("G", "c" + e, count[e])
    for s in ndma:
        wait("G", s, ndma[s])
    wait("G", "sent", nsent[0])
